import numpy as np, ml_dtypes
CORES = [30,158,46,174,86,214]
N = 6
BF = ml_dtypes.bfloat16
W, L, M, P, Q, F, RO = 2048, 16, 6, 32, 16, 6, 2
CAP = (N - 1) * Q
def look(u, m):
    return (u * (u >> 5) + (2 * m + 1) * u) & (W - 1)
def pick(x, ix):
    return np.take_along_axis(x, ix[..., None, :], -1)
def pack(x, w, th):
    return {"x0": np.ascontiguousarray(x.reshape(N, 128, W)).astype(np.float32).astype(BF), "wt": np.ascontiguousarray(w).reshape(N, 128, 1).astype(np.float32).astype(BF),
            "th": np.repeat(th, 16, axis=1).astype(np.int32)}
def texture(rng):
    x = np.empty((N, 8, 16, W), np.int64); stock = rng.permutation(np.array([8, 24, 60, 120, 200, 300, 400, 600]))
    for g in range(8):
        n = int(stock[g]); base = rng.integers(0, 256, (n, 16))
        for q in range(N):
            e = 1.5 + rng.random()
            x[q, g] = (base[np.minimum((n * rng.random(W) ** e).astype(np.int64), n - 1)] + rng.integers(-2, 3, (W, 16))).T
    return np.clip(x, 0, 255)
def far(rng):
    return rng.integers(0, 256, (N, 8, 16, W))
def weights(rng):
    w = rng.integers(0, 256, (8, 16)); w[:, 0] = 1; w[:, 1] = 16; w[:, 13:] = 0
    return w
def with_hash(rng, w, u):
    k = rng.integers(0, 256, (len(u), 16)); v = (u - k[:, 2:] @ w[2:]) & (W - 1)
    k[:, 0] = v & 15; k[:, 1] = v >> 4
    return k
def odd(rng, m, n):
    u = np.arange(1, W, 2); u = rng.permutation(u[((u >> 5) & 1) == 0])
    i = np.unique(look(u, m), return_index=True)[1]
    assert len(i) >= n
    return rng.permutation(u[i])[:n]
def runs(rng):
    r = W // (L + F); n = min(r, CAP + 12)
    return L * np.sort(rng.permutation(r)[:n]) + L - 2
def setup_inputs(rng):
    return pack(texture(rng), rng.integers(0, 256, (N, 8, 16)), rng.integers(20, 41, (N, 8, 2)))
def setup_inputs_room(rng):
    x = far(rng); w = weights(rng); th = np.stack([rng.integers(1, 60, (N, 8)), rng.choice(np.array([1, 2, 40]), (N, 8))], axis=-1)
    th[rng.integers(0, N), rng.integers(4, 6), 1] = 0
    for g in range(8):
        m = g % M; p = runs(rng); n = len(p); u = odd(rng, m, n); c = look(u, m); k = with_hash(rng, w[g], u)
        for q in range(N):
            a = int(rng.choice(np.array([0, 1, CAP - 1, CAP, CAP + 1, n])))
            if q == 0: a = (CAP, CAP + 1, n, CAP - 1, 1, 0, CAP, CAP + 1)[g]
            i = rng.permutation(n)[:a]
            x[q, g][:, c] = k.T; x[q, g][:, p[i]] = k[i].T
    return pack(x, np.broadcast_to(w, (N, 8, 16)), th)
def setup_inputs_ties(rng):
    x = far(rng); w = weights(rng); t = rng.integers(2, 250, 8); t2 = t + rng.integers(-1, 2, (N, 8))
    for g in range(1, 8, 2):
        a = 4 * int(rng.integers(65, 124)) + g % 4; t2[:, g] = a; t[g] = a + int(rng.integers(0, 2))
    th = np.stack([np.broadcast_to(t, (N, 8)), t2], axis=-1)
    for g in range(8):
        m = g % M; p = runs(rng); n = len(p); u = odd(rng, m, n); k = with_hash(rng, w[g], u); k[:, 13:] = 0; more = 255 * (g % 2)
        for q in range(N):
            for c in (look(u, m + 1), look(u, m)):
                z = k + 0; z[:, 14] = rng.integers(0, 3, n); x[q, g][:, c] = z.T
            z = k + 0; z[:, 13] = more; z[:, 15] = t[g] - more + rng.integers(-2, 1, n); x[q, g][:, p] = z.T
    return pack(x, np.broadcast_to(w, (N, 8, 16)), th)
def over_the_end(rng, x, w, g):
    p = W - L - 2; every = np.arange(W); first = look(every, 0); later = look(every, np.arange(1, P)[:, None])
    good = (first >= L) & (first < p - L)
    j, uk = np.nonzero((later > W - F) & good & ~np.any(later == p, axis=0))
    i = int(rng.integers(0, len(uk))); u = int(uk[i]); c1 = int(first[u]); c2 = int(later[j[i], u])
    a = int(rng.choice(every[good & (first != c1)])); ca = int(first[a])
    k = with_hash(rng, w[g], np.array([u]))[0]; k[15] = 0; near = k + 0; near[15] = 3
    ka = with_hash(rng, w[g], np.full(N, a))
    for q in range(N):
        x[q, g][:, [0, ca]] = ka[q][:, None]; x[q, g][:, c1] = near; x[q, g][:, [p, c2 - F]] = k[:, None]
def setup_inputs_ends(rng):
    x = far(rng); w = weights(rng); th = rng.integers(1, 60, (N, 8, 2))
    mm, uu = np.nonzero(look(np.arange(W), np.arange(M)[:, None]) >= W - L // 2)
    for g in range(8):
        if g % 4 == 3:
            over_the_end(rng, x, w, g); th[:, g] = rng.integers(4, 60, (N, 2))
            continue
        if g % 2 == 0:
            o = rng.permutation(len(uu)); c, i = np.unique(look(uu[o], mm[o]), return_index=True); u = uu[o][i]; p = L * rng.permutation(len(u))
        else:
            u = odd(rng, g % M, 1); c = look(u, g % M); p = np.array([W - 2])
        k = with_hash(rng, w[g], u)
        for q in range(N):
            x[q, g][:, c] = k.T; x[q, g][:, p] = k.T
    return pack(x, np.broadcast_to(w, (N, 8, 16)), th)
def setup_inputs_alike(rng):
    x = texture(rng); w = rng.integers(0, 256, (N, 8, 16)); th = rng.integers(20, 41, (N, 8, 2))
    for g in range(0, 8, 2):
        base = rng.integers(0, 256, (4, 16)); x[:, g] = base[rng.integers(0, 4, (N, W))].transpose(0, 2, 1)
    th[:, 0] = 1; th[:, 2] = 4096; th[:, 4, 0] = 0; th[:, 1, 0] = 4096; th[:, 1, 1] = 0; th[:, 3, 1] = 4096
    w[:, 6] = 0; w[:, 5] = 255
    x[:, 1, :, 0] = 255
    w[:, 7] = rng.integers(230, 256, (N, 16))
    up = rng.random((N, 1, W)) < 0.5; up[::2] = False
    x[:, 7] = np.where(up, 255 - rng.integers(0, 40, (N, 16, W)), rng.integers(0, 40, (N, 16, W)))
    for q in range(N):
        x[q, 1][:, L * (1 + rng.permutation(W // L - 1)[:W // L // 2])] = 0
        if q % 2 == 0:
            th[q, 7, 0] = rng.integers(150, 260); th[q, 7, 1] = rng.integers(3100, 3600)
        else:
            th[q, 7, 0] = rng.integers(2048, 3000); th[q, 7, 1] = rng.integers(100, 4097)
            c = look((255 * int(np.sum(w[q, 7]))) & (W - 1), 0); x[q, 7][:, [0, L, c]] = 255
    th[0, 7, 1] = 4096
    return pack(x, w, th)
def setup_inputs_spread(rng):
    x = np.minimum((np.exp2(8 * rng.random((N, 8, 1, W))) * rng.random((N, 8, 16, W))).astype(np.int64), 255)
    w = np.minimum(np.exp2(8 * rng.random((N, 8, 16))).astype(np.int64), 255) * (rng.random((N, 8, 16)) > 0.0625)
    return pack(x, w, np.minimum(np.exp2(12 * rng.random((N, 8, 2))).astype(np.int64), 4096))
def check_inputs(d):
    bad = []
    for k in ("x0", "wt"):
        v = np.asarray(d[k]).astype(np.float32)
        if not np.all((v >= 0) & (v <= 255) & (v == np.floor(v))): bad.append("whole numbers of " + k)
    v = np.asarray(d["th"])
    if np.min(v) < 0 or np.max(v) > 4096: bad.append("range of th")
    v = v.reshape(N, 8, 16, 2)
    if np.any(v != v[:, :, :1]): bad.append("rows of th alike in a group")
    return bad
def reference(x0, wt, th):
    x = x0.astype(np.float32).astype(np.int64).reshape(N, 8, 16, W); w = wt.astype(np.float32).astype(np.int64).reshape(N, 8, 16, 1)
    t = th.astype(np.int64).reshape(N, 8, 16, 2)[:, :, 0]; here = np.arange(W)
    for rnd in range(RO):
        u = np.add.reduce(w * x, axis=2) & (W - 1)
        nx = np.zeros_like(u) + ((here + 1) & (W - 1))
        for m in range(M - 1, -1, -1):
            c = look(u, m); near = np.add.reduce(np.abs(pick(x, c) - x), axis=2) < t[..., :1]
            nx = np.where(near, (c + 1) & (W - 1), nx)
        s = np.zeros((N, 8, W // L, L), np.int64); s[..., 0] = L * np.arange(W // L)
        for k in range(1, L): s[..., k] = np.take_along_axis(nx, s[..., k - 1], -1)
        jump = np.zeros(s.shape, bool); jump[..., :-1] = s[..., 1:] != ((s[..., :-1] + 1) & (W - 1))
        s = s.reshape(N, 8, W); jump = jump.reshape(N, 8, W)
        site = np.argsort(~jump, axis=-1, kind="stable")[..., :CAP]
        live = np.take_along_axis(jump, site, -1); ask = pick(x, np.take_along_axis(s, site, -1))
        found = np.zeros((N, 8, CAP), bool); fill = np.zeros((N, 8, 16, CAP, F), np.int64)
        for q in range(N):
            for d in range(1, N):
                b = (q + d) % N; cut = slice((d - 1) * Q, d * Q); a = ask[q][:, :, cut]
                v = np.add.reduce(w[b] * a, axis=1) & (W - 1); c = look(v[..., None], np.arange(P))
                off = np.add.reduce(np.abs(pick(x[b], c.reshape(8, -1)).reshape(8, 16, Q, P) - a[..., None]), axis=1)
                best = np.take_along_axis(c, np.argmin(off, axis=-1)[..., None], -1)
                found[q][:, cut] = np.min(off, axis=-1) < t[b][:, 1:]
                fill[q][:, :, cut] = pick(x[b], ((best + 1 + np.arange(F)) & (W - 1)).reshape(8, -1)).reshape(8, 16, Q, F)
        found = found & live
        more = np.zeros((N, 8, W), np.int64); np.put_along_axis(more, site, found.astype(np.int64) * F, -1)
        place = here + np.add.accumulate(more, axis=-1) - more
        z = np.zeros((N, 8, 16, W + F * CAP + 1), np.int64)
        np.put_along_axis(z, place[:, :, None], pick(x, s), -1)
        at = np.take_along_axis(place, site, -1)[..., None] + 1 + np.arange(F)
        at = np.where(found[..., None], at, W + F * CAP).reshape(N, 8, 1, CAP * F)
        np.put_along_axis(z, at, fill.reshape(N, 8, 16, CAP * F), -1)
        x = np.ascontiguousarray(z[..., :W])
    return {"y": x.reshape(N, 128, W).astype(np.float32).astype(BF)}

@@ -1,0 +1,589 @@
+import numpy as np
+from concourse.bass import DstId, RemoteDMATransfer
+from concourse.mybir import dt, AluOpType as Op, AxisListType, ActivationFunctionType as Fn
+
+N, W, L, M, P, Q, F, RO = 6, 2048, 16, 6, 32, 16, 6, 2
+H = W // 2
+HJ = H // 16
+ND = N - 1
+SLOT = Q * F + 8
+RING = 6
+NG = 4
+XW = 3072
+
+SB = {}
+PART = {}
+ARENA = {"int32": ["ar_i", 0], "float32": ["ar_f", 0], "bfloat16": ["ar_b", 0], "uint16": ["ar_u", 0]}
+OWN = ("WT", "TH")
+
+
+def sb(name, cols, dtype):
+    if cols <= 160 and dtype in ARENA and name not in OWN and not name.startswith(("QIN", "ASK")):
+        a = ARENA[dtype]
+        PART[name] = (a[0], a[1], cols)
+        a[1] += -(-cols // 16) * 16
+    else:
+        SB[name] = ("sbuf", [128, cols], dtype)
+
+
+def many(names, cols, dtype):
+    for n in names.split():
+        sb(n, cols, dtype)
+
+
+many("XA XB XC", XW, "bfloat16")
+many("XP Xk Xst Xnat WEI EI", W, "bfloat16")
+sb("BIh", W, "float16")
+many("D AB", RING * H, "bfloat16")
+sb("G", NG * H, "bfloat16")
+many("i_ui i_ua i_us i_u2 i_r1 i_r2 i_nxw", 2 * HJ, "int32")
+many("raw msk", 2 * M * HJ, "int32")
+sb("lst", 2 * M * HJ, "uint16")
+sb("RUN", 2 * M * HJ, "float32")
+sb("RG", 2 * M * HJ, "bfloat16")
+many("f_r f_d f_e", 2 * HJ, "float32")
+sb("NXH", 2 * HJ, "float16")
+sb("NXW", W, "float32")
+many("CM CS", 256, "float16")
+many("k_RSh k_IDh k_NIh", 128, "float16")
+many("k_L0h k_ONh", 8, "float16")
+many("LC LF PL", 128, "uint16")
+many("SW J", 128, "float32")
+many("INC ING DEL", 128, "bfloat16")
+many("GO CC EQ LT LO", 640, "bfloat16")
+sb("AL", 8, "uint16")
+many("plc live pl8", 8, "float32")
+for _r in range(RO):
+    many("ASK%d QIN%d" % (_r, _r), ND * Q, "bfloat16")
+    many("FIL%d ZIN%d" % (_r, _r), ND * SLOT, "bfloat16")
+sb("QREP", 12 * ND * Q, "bfloat16")
+many("VM VS", 80, "float32")
+many("q_vi q_va q_vs q_vb q_ki q_km q_kc q_kd", 8, "int32")
+many("q_c0 q_v2 q_KM q_kt", 8, "float32")
+many("qraw qmsk", P * ND, "int32")
+sb("qlst", P * ND, "uint16")
+many("FL SLu", 32, "uint16")
+sb("an", 8, "bfloat16")
+sb("a8", 8, "int32")
+sb("ahl", 16, "int32")
+sb("ahf", 16, "float32")
+many("SL SL2", 32, "float32")
+many("ONB WBLK", 128, "bfloat16")
+many("k_TMP k_BLK k_IDN k_LST1 k_LST6 k_BLK6 k_NB6 k_SHF k_DSH k_ID16 k_NEGI k_N8I k_JJ k_IP1 k_IARRt k_IARR k_ICOL", 128, "bfloat16")
+many("k_NP1 k_NARRt k_NARR", 640, "bfloat16")
+sb("k_MROWf", P * ND, "float32")
+sb("k_MROW", P * ND, "bfloat16")
+sb("k_ZR", 16, "bfloat16")
+sb("k_MC", P, "float32")
+many("k_MKi k_MKa", 128, "int32")
+many("k_MK k_RS k_ONF k_PWb k_PW1", 128, "float32")
+sb("k_RB5", (M - 1) * HJ, "float32")
+many("k_p k_p2 TH", 8, "int32")
+many("k_I16 k_I64 k_I128 k_LB k_T", 8, "float32")
+sb("k_L0", 8, "uint16")
+many("k_CW k_GW WT", 8, "bfloat16")
+many("k_JKb k_JK", 32, "float32")
+for _k in range(8):
+    SB["ps%d" % _k] = ("psum", [128, 512], "float32")
+for _d in ARENA:
+    SB[ARENA[_d][0]] = ("sbuf", [128, ARENA[_d][1]], _d)
+SCRATCH = SB
+SEMAPHORES = ["sV", "sS", "sT", "sG", "lsem", "dx0", "dx1", "dwt", "dth", "dy0", "dy1", "q0", "q1", "z0", "z1"] + ["ga%d" % _k for _k in range(4 * RO)]
+
+WB = ((4, 5), (2, 3))
+PLAN = [tuple(int(c) if c.isdigit() else c for c in x.split(".")) for x in (
+    "sg.0.4 v.0.1 sg.0.3 lists v.0.0 a.0.1 sg.1.4 v.0.2 a.0.0 sl.0.4 v.1.0 a.0.2 sl.0.3 v.1.1 a.1.0 v.1.2 a.1.1 consts sl.1.4 v.1.3 "
+    "a.1.2 v.0.5 a.1.3 v.1.5 a.0.5 first.0 first.1 a.1.5 bl.0 succ.0 bl.1 succ.1 win.0 win.1").split()]
+
+
+def rank_program(g, core, T, topo):
+    rank = T.rank_of(core)
+    if rank is None:
+        return
+    cores = T.cores
+    queue = {"V": g.vector, "S": g.scalar, "T": g.tensor, "G": g, "Y": g.sync}
+    semof = {"V": "sV", "S": "sS", "T": "sT", "G": "sG"}
+    cnt = {"V": 0, "S": 0, "T": 0, "G": 0}
+    known = {"V": {}, "S": {}, "T": {}, "G": {}, "Y": {}}
+    snap = {}
+    log = {}
+
+    def A(name, c0=0, c1=None, step=1):
+        if name in PART:
+            a, o, n = PART[name]
+            return (a, o + c0, o + (n if c1 is None else c1), step)
+        n = SB[name][1][1]
+        return (name, c0, n if c1 is None else c1, step)
+
+    def ap(a):
+        return T[a[0]][:, a[1]:a[2]:a[3]] if a[3] != 1 else T[a[0]][:, a[1]:a[2]]
+
+    def overlap(a, b):
+        if a[1] >= b[2] or b[1] >= a[2]:
+            return False
+        if a[3] == b[3] and a[3] > 1 and (a[1] - b[1]) % a[3]:
+            return False
+        return True
+
+    def wait(e, sem, val):
+        k = known[e]
+        if k.get(sem, 0) >= val:
+            return
+        queue[e].wait_ge(T.sem[sem], val)
+        s = snap.get((sem, val))
+        if s:
+            for q in s:
+                if s[q] > k.get(q, 0):
+                    k[q] = s[q]
+        k[sem] = val
+
+    def need(e, reads, writes):
+        own = semof.get(e)
+        req = {}
+        for lst, isw in ((reads, False), (writes, True)):
+            for a in lst:
+                ps = SB[a[0]][0] == "psum"
+                for (w, b, sem, val) in log.get(a[0], ()):
+                    if sem == own:
+                        if not w or (ps and e == "T" and isw) or not overlap(a, b):
+                            continue
+                    elif not ps:
+                        if not (w or isw) or not overlap(a, b):
+                            continue
+                    if val > req.get(sem, 0):
+                        req[sem] = val
+        for s in sorted(req, key=lambda s: -req[s]):
+            wait(e, s, req[s])
+
+    def covers(a, b):
+        return a[1] <= b[1] and a[2] >= b[2] and (a[3] == 1 or (a[3] == b[3] and (a[1] - b[1]) % a[3] == 0))
+
+    def note(reads, writes, sem, val):
+        for a in writes:
+            l = log.get(a[0], [])
+            if SB[a[0]][0] != "psum":
+                l = [x for x in l if not covers(a, x[1])]
+            else:
+                l = [x for x in l if not (x[0] and x[2] == sem and covers(a, x[1]))]
+            l.append((True, a, sem, val))
+            log[a[0]] = l
+        for a in reads:
+            l = log.setdefault(a[0], [])
+            l[:] = [x for x in l if x[0] or x[2] != sem or not covers(a, x[1])]
+            l.append((False, a, sem, val))
+
+    def do(e, fn, reads, writes):
+        need(e, reads, writes)
+        cnt[e] += 1
+        fn().then_inc(T.sem[semof[e]], 1)
+        snap[(semof[e], cnt[e])] = dict(known[e])
+        note(reads, writes, semof[e], cnt[e])
+
+    def dma(e, out, in_, sem, reads, writes, **kw):
+        need(e, reads, writes)
+        queue[e].dma_start(out=out, in_=in_, **kw).then_inc(T.sem[sem], 16)
+        snap[(sem, 16)] = dict(known[e])
+        note(reads, writes, sem, 16)
+
+    def is_ap(x):
+        return isinstance(x, tuple)
+
+    def val(x):
+        return ap(x) if is_ap(x) else x
+
+    def cp(out, in_):
+        do("V", lambda: g.vector.tensor_copy(ap(out), ap(in_)), [in_], [out])
+
+    def tt(out, a, b, op):
+        do("V", lambda: g.vector.tensor_tensor(ap(out), ap(a), ap(b), op), [a, b], [out])
+
+    def ts(out, a, s1, op0, s2=None, op1=None):
+        rd = [a] + [s for s in (s1, s2) if is_ap(s)]
+        if op1 is None:
+            do("V", lambda: g.vector.tensor_scalar(ap(out), ap(a), val(s1), None, op0), rd, [out])
+        else:
+            do("V", lambda: g.vector.tensor_scalar(ap(out), ap(a), val(s1), val(s2), op0, op1), rd, [out])
+
+    def ms(out, c):
+        do("V", lambda: g.vector.memset(ap(out), c), [], [out])
+
+    def scan(out, d0, d1, op0, op1):
+        do("V", lambda: g.vector.tensor_tensor_scan(ap(out), ap(d0), ap(d1), 0.0, op0, op1), [d0, d1], [out])
+
+    def act(out, in_, func=Fn.Copy, scale=1.0, bias=0.0):
+        do("S", lambda: g.scalar.activation(ap(out), ap(in_), func, bias=bias, scale=val(scale)), [in_] + ([scale] if is_ap(scale) else []), [out])
+
+    def mm(out, l, r, start, stop):
+        do("T", lambda: g.tensor.matmul(ap(out), ap(l), ap(r), start, stop), [l, r], [out])
+
+    def vgather(out, win, off, b=None, op=None):
+        if b is None:
+            do("V", lambda: g.vector.tensor_copy(ap(out), ap(win).indirect(ap(off))), [win, off], [out])
+        else:
+            do("V", lambda: g.vector.tensor_tensor(ap(out), ap(win).indirect(ap(off)), ap(b), op), [win, off, b], [out])
+
+    def sgather(out, win, off, scale=1.0):
+        do("S", lambda: g.scalar.activation(ap(out), ap(win).indirect(ap(off)), Fn.Copy, scale=scale), [win, off], [out])
+
+    def scatter(win, off, in_):
+        do("V", lambda: g.vector.tensor_copy(ap(win).indirect(ap(off)), ap(in_)), [off, in_], [win])
+
+    def iota(out, pattern, base, chan, flag=False):
+        if flag:
+            do("G", lambda: g.iota(ap(out), pattern, base, chan, allow_small_or_imprecise_dtypes=True), [], [out])
+        else:
+            do("G", lambda: g.iota(ap(out), pattern, base, chan), [], [out])
+
+    def asel(out, in_, pattern, op, base, chan):
+        do("G", lambda: g.affine_select(ap(out), ap(in_), pattern, op, 0.0, base, chan), [in_], [out])
+
+    dma("Y", T.WT[:, 0:1], T.wt[:, :], "dwt", [], [A("WT", 0, 1)])
+    dma("Y", T.XA[:, 0:H], T.x0[:, 0:H], "dx0", [], [A("XA", 0, H)])
+    dma("Y", T.XA[:, H:W], T.x0[:, H:W], "dx1", [], [A("XA", H, W)])
+    dma("S", T.TH[:, 0:2], T.th[:, :], "dth", [], [A("TH", 0, 2)])
+
+    K = lambda n, c0=0, c1=None, step=1: A("k_" + n, c0, c1, step)
+    ms(A("ONB"), 1.0)
+    asel(K("TMP"), A("ONB"), [[-16, 8], [0, 16]], Op.is_ge, 0, 1)
+    asel(K("BLK"), K("TMP"), [[16, 8], [0, 16]], Op.is_ge, 15, -1)
+    iota(K("p", 0, 1), [[0, 1]], 0, 1)
+    iota(K("MKi"), [[-1, 128]], 128, 1)
+    iota(K("PWb"), [[H, 2], [1, HJ]], 1, 0, True)
+    iota(K("LB"), [[16, 8]], 0, 0, True)
+    ms(A("WEI"), 0.0)
+    ms(A("EI"), 0.0)
+    for i in range(16):
+        ts(A("WEI", 128 * i + i, 128 * i + 128, 16), K("BLK", i, 128, 16), A("WT", 0, 1), Op.mult)
+    for i in range(16):
+        act(A("EI", 128 * i + i, 128 * i + 128, 16), K("BLK", i, 128, 16))
+    ts(K("p2", 0, 1), K("p", 0, 1), 15, Op.bitwise_and)
+    cp(K("I16", 0, 1), K("p2", 0, 1))
+    ts(K("I64", 0, 1), K("I16", 0, 1), float(HJ), Op.mult)
+    ts(K("I128", 0, 1), K("I16", 0, 1), 128.0, Op.mult)
+    ts(K("PW1"), K("PWb"), K("I64", 0, 1), Op.add)
+    ts(K("L0"), K("LB"), K("I128", 0, 1), Op.add)
+    ts(K("MKa"), K("MKi"), 15, Op.bitwise_and)
+    ts(K("MK"), K("MKa"), 0, Op.is_equal)
+    asel(K("IDN"), A("ONB"), [[-1, 128]], Op.is_equal, 0, 1)
+    ts(K("NEGI"), K("IDN"), -1.0, Op.mult)
+    for i in range(16):
+        ts(A("BIh", 128 * i, 128 * i + 128), K("BLK"), K("MK", i, i + 1), Op.mult)
+    ms(K("RB5"), 0.0)
+    ms(K("RB5", 0, None, M - 1), 100000.0)
+    cp(K("T", 0, 2), A("TH", 0, 2))
+    ms(K("RS"), 1.0)
+    ms(K("RS", 0, None, 16), 0.0)
+    cp(K("RSh"), K("RS"))
+    cp(K("IDh"), K("IDN"))
+    ts(K("NIh"), K("IDN"), -1.0, Op.mult)
+    ts(K("L0h"), K("LB"), K("I128", 0, 1), Op.add)
+    cp(K("ONh"), A("ONB", 0, 8))
+    ms(K("ZR"), 0.0)
+    iota(K("NP1"), [[16, ND], [0, 8], [1, 16]], 1, 0, True)
+    iota(K("JJ"), [[1, 128]], 0, 0, True)
+    iota(K("IP1"), [[0, 8], [1, 16]], 1, 0, True)
+    iota(K("MC"), [[1, P]], 0, 0, True)
+    iota(K("MROWf"), [[1, P], [0, ND]], 0, 0, True)
+    iota(K("JKb", 0, 30), [[16, 30]], 2560, 0, True)
+    asel(K("LST1"), K("BLK"), [[1, 128]], Op.is_ge, -1, -1)
+    asel(K("SHF"), K("BLK"), [[1, 128]], Op.is_equal, -1, -1)
+    asel(K("NARRt"), K("NP1"), [[0, ND], [-16, 8], [0, 16]], Op.is_ge, 0, 1)
+    asel(K("NARR"), K("NARRt"), [[0, ND], [16, 8], [0, 16]], Op.is_ge, 15, -1)
+    asel(K("IARRt"), K("IP1"), [[-16, 8], [0, 16]], Op.is_ge, 0, 1)
+    asel(K("IARR"), K("IARRt"), [[16, 8], [0, 16]], Op.is_ge, 15, -1)
+
+    def consts_b():
+        act(K("MROW"), K("MROWf"), scale=1.0 / P)
+        act(K("LST6"), K("LST1"), scale=6.0)
+        act(K("BLK6"), K("BLK"), scale=6.0)
+        act(K("NB6"), K("BLK"), scale=-6.0)
+        act(K("ID16"), K("IDN"), scale=16.0)
+        act(K("N8I"), K("IDN"), scale=-8192.0)
+        act(K("ICOL"), A("ONB"), scale=K("I16", 0, 1))
+        for r in range(RO):
+            act(A("FIL%d" % r), K("NARR", 0, ND * SLOT), scale=0.0)
+
+    def consts_c():
+        ms(K("ONF"), 1.0)
+        tt(K("DSH"), K("IDN"), K("SHF"), Op.subtract)
+        ts(K("CW", 0, 1), K("MK", 15, 16), -2032.0, Op.mult, 128.0, Op.add)
+        ms(K("CW", 1, 2), 1.0)
+        ms(K("GW", 0, 1), 1.0)
+        ms(K("GW", 1, 2), 128.0)
+        ts(A("WBLK"), K("BLK"), A("WT", 0, 1), Op.mult)
+        ts(K("JK", 0, 30), K("JKb", 0, 30), K("I16", 0, 1), Op.add)
+
+    def send(src, dst, dest, sem, alone):
+        trs, order = [], [d for d in range(ND) if d != alone] + [alone]
+        for k, d in enumerate(order):
+            need("G", [src[d]], [])
+            rid, pid = topo.addr(dest[d], core)
+            es = topo.engines(core, dest[d])
+            if k < 4:
+                n = len(es) // 4
+                mask = sum(1 << e for e in es[n * k:n * k + n])
+                trs.append(RemoteDMATransfer(dst_ids=[DstId(rid=rid, pnc=pid)], dma_engine_mask=mask, remote_sem=T.sem[sem],
+                                             src=ap(src[d]), dst=ap(dst[d])))
+                if k == 3:
+                    g.remote_dma_fused(trs, local_sem=T.sem.lsem)
+        g.remote_dma(ap(dst[alone]), ap(src[alone]), T.sem[sem], T.sem.lsem, pid, rid, topo.mask(core, dest[alone]))
+        tot[0] += 4 * n + len(es)
+        return 4 * n + len(es)
+
+    tot, ring, gs, landed, place, na = [0], [0], [0], {}, {}, [0]
+    xs = ("XA", "XB", "XC")
+    ps = lambda k, c0, c1, step=1: A("ps%d" % k, c0, c1, step)
+    for r in range(RO):
+        X, XN = xs[r], xs[r + 1]
+
+        for h in range(2):
+            for i in range(16):
+                mm(ps(h, 0, HJ), A("WEI", 128 * i, 128 * i + 128), A(X, H * h + HJ * i, H * h + HJ * i + HJ), i == 0, i == 15)
+            for i in range(16):
+                act(A("XP", H * h + i, H * h + H, 16), A(X, H * h + HJ * i, H * h + HJ * i + HJ))
+        if r == 0:
+            act(A(X, W, W + 8), A(X, 0, 8))
+
+        def lists(h):
+            o, e = HJ * h, HJ * h + HJ
+            ui, ua, us = [A("i_" + n, o, e) for n in ("ui", "ua", "us")]
+            u2, bb = ps(6 + h, 128, 128 + HJ), ps(6 + h, 256, 256 + HJ)
+            R = lambda m: A("raw", M * HJ * h + HJ * m, M * HJ * h + HJ * m + HJ)
+            al = lambda n: A(n, M * HJ * h, M * HJ * h + M * HJ)
+            cp(ui, ps(h, 0, HJ))
+            ts(ua, ui, W - 1, Op.bitwise_and)
+            ts(us, ui, W - 1, Op.bitwise_and, 5, Op.arith_shift_right)
+            ts(u2, ua, 2, Op.mult)
+            tt(bb, ua, us, Op.mult)
+            tt(R(0), bb, ua, Op.add)
+            for m in range(1, M):
+                tt(R(m), u2, R(m - 1), Op.add)
+            ts(al("msk"), al("raw"), W - 1, Op.bitwise_and)
+            cp(al("lst"), al("msk"))
+            ts(A("i_r1", o, e), R(0), 1, Op.add)
+            ts(A("i_u2", o, e), ua, 2, Op.mult)
+
+        def lk(h, m):
+            return A("lst", M * HJ * h + HJ * m, M * HJ * h + HJ * m + HJ)
+
+        def slot():
+            ring[0] += 1
+            o = H * (ring[0] % RING)
+            return A("D", o, o + H), A("AB", o, o + H), o
+
+        def gslot(n):
+            gs[0] += 1
+            o = H * (gs[0] % NG)
+            return A("G", o, o + n)
+
+        def dist(h, m, o):
+            out = ps(2 + h, m, (M - 1) * HJ, M - 1) if m < M - 1 else ps(h, 0, HJ)
+            for i in range(16):
+                mm(out, A("EI", 128 * i, 128 * i + 128), A("AB", o + i, o + H, 16), i == 0, i == 15)
+
+        def sgath(h, m):
+            a, b = gslot(H), A("XP", H * h, H * h + H)
+            place["g", h, m] = a
+            sgather(a, A(X, 0, W), lk(h, m), scale=-1.0)
+            dma("G", ap(a), ap(b), "ga%d" % na[0], [b], [a], accum_op=Op.add)
+            na[0] += 1
+
+        def slook(h, m):
+            d, a, o = slot()
+            act(a, place["g", h, m], Fn.Abs)
+            dist(h, m, o)
+
+        def vlook(h, m):
+            d, a, o = slot()
+            place[h, m] = d, a, o
+            vgather(d, A(X, 0, W), lk(h, m), A("XP", H * h, H * h + H), Op.subtract)
+
+        def size(h, m):
+            d, a, o = place[h, m]
+            act(a, d, Fn.Abs)
+            dist(h, m, o)
+
+        def first(h):
+            o, n = M * HJ * h, (M - 1) * HJ
+            scan(A("RUN", o, o + n), K("RB5"), ps(2 + h, 0, n), Op.add, Op.min)
+            ts(A("RG", o, o + n), A("RUN", o, o + n), K("T", 0, 1), Op.is_ge)
+            for m in range(M - 1):
+                mm(ps(6 + h, 0, HJ), K("IDN"), A("RG", o + m, o + n, M - 1), m == 0, m == M - 2)
+
+        def before_last(h):
+            o, n, s, e = M * HJ * h, (M - 1) * HJ, HJ * h, HJ * h + HJ
+            ft, fd = ps(6 + h, 128, 128 + HJ), ps(6 + h, 256, 256 + HJ)
+            tt(ft, ps(6 + h, 0, HJ), A("i_u2", s, e), Op.mult)
+            tt(A("f_r", s, e), ft, A("i_r1", s, e), Op.add)
+            tt(fd, K("PW1", s, e), A("f_r", s, e), Op.subtract)
+            tt(A("f_e", s, e), fd, A("RG", o + M - 2, o + n, M - 1), Op.mult)
+
+        def succ(h):
+            s, e = HJ * h, HJ * h + HJ
+            ft = ps(6 + h, 128, 128 + HJ)
+            ts(ft, ps(h, 0, HJ), K("T", 0, 1), Op.is_ge)
+            tt(A("f_d", s, e), ft, A("f_e", s, e), Op.mult)
+            tt(A("i_r2", s, e), A("f_r", s, e), A("f_d", s, e), Op.add)
+            ts(A("i_nxw", s, e), A("i_r2", s, e), W - 1, Op.bitwise_and)
+            cp(A("NXH", s, e), A("i_nxw", s, e))
+            for i in range(16):
+                mm(ps(WB[h][i // 8], HJ * (i % 8), HJ * (i % 8) + HJ), A("BIh", 128 * i, 128 * i + 128), A("NXH", s, e), True, True)
+
+        def window(h):
+            act(A("NXW", H * h, H * h + 512), ps(WB[h][0], 0, 512))
+            cp(A("NXW", H * h + 512, H * h + H), ps(WB[h][1], 0, 512))
+
+        calls = {"sg": sgath, "sl": slook, "v": vlook, "a": size, "first": first, "bl": before_last, "succ": succ,
+                 "win": window, "lists": lambda: lists(1), "consts": consts_c if r == 0 else (lambda: None)}
+        lists(0)
+        for step in PLAN:
+            calls[step[0]](*step[1:])
+        if r == 0:
+            consts_b()
+
+        mm(ps(7, 15, 128, 16), K("IDh"), K("ONh"), True, True)
+        mm(ps(3, 0, 128, 16), K("IDh"), K("L0h"), True, True)
+        prev, last = K("L0"), K("L0h")
+        sgather(A("Xk", 0, 128), A(X, 0, W), prev)
+        for k in range(1, L):
+            o = 128 * (k % 2)
+            vgather(A("CM", o, o + 128), A("NXW"), prev, K("MK"), Op.mult)
+            scan(A("CS", o, o + 128), K("RSh"), A("CM", o, o + 128), Op.mult, Op.add)
+            prev = A("LC", 8 * k, 8 * k + 8)
+            now = A("CS", o + 15, o + 128, 16)
+            cp(prev, now)
+            mm(ps(3, k, 128, 16), K("IDh"), now, True, True)
+            mm(ps(7, k - 1, 128, 16), K("NIh"), last, True, False)
+            mm(ps(7, k - 1, 128, 16), K("IDh"), now, False, True)
+            last = now
+            if k == L - 1:
+                cp(A("LF"), ps(3, 0, 128))
+                act(A("SW"), ps(7, 0, 128), Fn.Abs, bias=1023.0)
+            sgather(A("Xk", 128 * k, 128 * k + 128), A(X, 0, W), prev)
+        sgather(A("Xst"), A(X, 0, W), A("LF"))
+
+        ts(A("J"), A("SW"), 1024.0, Op.not_equal)
+        mm(ps(2, 0, 2 * ND), K("IDN"), K("ZR", 0, 2 * ND), True, False)
+        scan(A("INC"), K("ONF"), A("J"), Op.mult, Op.add)
+        mm(ps(6, 0, 1), K("LST1"), A("INC", 127, 128), True, True)
+        ts(A("ING"), A("INC"), ps(6, 0, 1), Op.add, 200.0, Op.min)
+        mm(ps(7, 0, 128), K("DSH"), A("ING"), True, True)
+        ts(A("GO"), K("NARR"), ps(6, 0, 1), Op.is_gt)
+        cp(A("DEL"), ps(7, 0, 128))
+        for c in range(2):
+            mm(ps(c, 0, 320), A("DEL"), A("GO", 320 * c, 320 * c + 320), True, True)
+        for c in range(2):
+            tt(A("CC", 320 * c, 320 * c + 320), ps(c, 0, 320), K("NP1", 320 * c, 320 * c + 320), Op.is_lt)
+        for s, w in (("GO", "GW"), ("CC", "CW")):
+            for d in range(ND):
+                mm(ps(2, 2 * d, 2 * d + 2), A(s, 128 * d, 128 * d + 128), K(w, 0, 2), False, s == "CC" and d == ND - 1)
+        ts(A("AL", 0, ND), ps(2, 0, 2 * ND, 2), -1.0, Op.add)
+        ak, qn = "ASK%d" % r, "QIN%d" % r
+        vgather(A(ak), A("Xk"), A("AL", 0, ND))
+        qs = [(Q * d, Q * d + Q) for d in range(ND)]
+        landed["q%d" % r] = send([A(ak, *x) for x in qs], [A(qn, *x) for x in qs], [cores[(rank + 1 + d) % N] for d in range(ND)], "q%d" % r, ND - 1)
+        ts(A("plc", 0, ND), ps(2, 1, 2 * ND, 2), -128.0, Op.add)
+        ts(A("live", 0, ND), A("plc", 0, ND), float(W), Op.is_lt)
+        ts(A("pl8", 0, ND), A("plc", 0, ND), 8193.0, Op.add)
+        mm(ps(6, 0, 128), K("ID16"), K("JJ"), True, False)
+        mm(ps(6, 0, 128), K("IDN"), K("ICOL"), False, False)
+
+        note([], [A(qn)], "q%d" % r, landed["q%d" % r])
+        mm(ps(3, 0, 80), A("WBLK"), A(qn), True, True)
+        act(A("QREP", 0, 80), A(qn))
+        act(A("QREP", 80, 160), A(qn))
+        act(A("QREP", 160, 320), A("QREP", 0, 160))
+        act(A("QREP", 320, 640), A("QREP", 0, 320))
+        act(A("QREP", 640, 960), A("QREP", 0, 320))
+        tt(A("VM"), ps(3, 0, 80), K("MK", 0, 80), Op.mult)
+        scan(A("VS"), K("RS", 0, 80), A("VM"), Op.mult, Op.add)
+        q = lambda n: A("q_" + n, 0, ND)
+        cp(q("vi"), A("VS", 15, 80, 16))
+        ts(q("va"), q("vi"), W - 1, Op.bitwise_and)
+        ts(q("vs"), q("vi"), W - 1, Op.bitwise_and, 5, Op.arith_shift_right)
+        ts(q("v2"), q("va"), 2, Op.mult)
+        tt(q("vb"), q("va"), q("vs"), Op.mult)
+        tt(q("c0"), q("vb"), q("va"), Op.add)
+        for d in range(ND):
+            ts(A("qraw", d, P * ND, ND), K("MC"), A("q_v2", d, d + 1), Op.mult, A("q_c0", d, d + 1), Op.add)
+        ts(A("qmsk"), A("qraw"), W - 1, Op.bitwise_and)
+        cp(A("qlst"), A("qmsk"))
+        parts = [(0, 60), (60, 120), (120, 160)]
+        gb = gslot(640)
+        sgather(gb, A(X, 0, W), A("qlst", 120, 160))
+        for c in range(2):
+            mm(ps(1 - c, 0, 320), K("IDN"), A("G", gb[1] + 320 * c, gb[1] + 320 * c + 320), True, False)
+            mm(ps(1 - c, 0, 320), K("NEGI"), A("QREP", 0, 320), False, True)
+        for t in (0, 2, 1):
+            l0, l1 = parts[t]
+            n = 16 * (l1 - l0)
+            d, a, o = slot()
+            if t < 2:
+                vgather(A("D", o, o + n), A(X, 0, W), A("qlst", l0, l1), A("QREP", 0, n), Op.subtract)
+                act(A("AB", o, o + n), A("D", o, o + n), Fn.Abs)
+            else:
+                for c in range(2):
+                    act(A("AB", o + 320 * c, o + 320 * c + 320), ps(1 - c, 0, 320), Fn.Abs)
+            mm(ps(4, l0, l1), K("IDN"), K("MROW", l0, l1), True, False)
+            for i in range(16):
+                mm(ps(4, l0, l1), A("EI", 128 * i, 128 * i + 128), A("AB", o + i, o + n, 16), False, i == 15)
+        for d in range(ND):
+            a, b = A("q_KM", d, d + 1), ps(4, d, P * ND, ND)
+            do("V", lambda: g.vector.tensor_reduce(ap(a), ap(b), AxisListType.X, Op.min), [b], [a])
+        ts(q("ki"), q("KM"), float(P), Op.mult)
+        fl = "FIL%d" % r
+        ts(q("km"), q("ki"), P - 1, Op.bitwise_and)
+        tt(q("kt"), q("km"), q("v2"), Op.mult)
+        tt(q("kc"), q("kt"), q("c0"), Op.add)
+        ts(q("kd"), q("kc"), W - 1, Op.bitwise_and)
+        for f in range(F):
+            ts(A("FL", f, F * ND, F), q("kd"), f + 1, Op.add)
+        ts(A(fl, Q * F, ND * SLOT, SLOT), q("KM"), K("T", 1, 2), Op.is_lt)
+        for d in (0, 3, 1, 4, 2):
+            (sgather if d > 2 else vgather)(A(fl, SLOT * d, SLOT * d + Q * F), A(X, 0, W + 8), A("FL", F * d, F * d + F))
+        z = "ZIN%d" % r
+        zs = [(SLOT * d, SLOT * d + SLOT) for d in range(ND)]
+        landed["z%d" % r] = send([A(fl, *x) for x in zs], [A(z, *x) for x in zs], [cores[(rank - 1 - d) % N] for d in range(ND)], "z%d" % r, 2)
+        for i in range(16):
+            act(A("Xnat", 128 * i, 128 * i + 128), A("Xst", i, W, 16))
+
+        note([], [A(z)], "z%d" % r, landed["z%d" % r])
+        tt(A("an", 0, ND), A(z, Q * F, ND * SLOT, SLOT), A("live", 0, ND), Op.mult)
+        mm(ps(5, 0, ND), K("LST6"), A("an", 0, ND), True, False)
+        for k in range(1, ND):
+            mm(ps(5, k, ND), K("BLK6"), A("an", 0, ND - k), False, False)
+        mm(ps(5, 0, ND), K("N8I"), A("an", 0, ND), False, True)
+        tt(A("a8", 0, ND), ps(5, 0, ND), A("pl8", 0, ND), Op.add)
+        ts(A("ahl", 0, ND), A("a8", 0, ND), 4, Op.arith_shift_right)
+        ts(A("ahl", ND, 2 * ND), A("a8", 0, ND), 15, Op.bitwise_and)
+        cp(A("ahf", 0, 2 * ND), A("ahl", 0, 2 * ND))
+        for d in range(ND):
+            o = 128 * d
+            hi, lo = A("ahf", d, d + 1), A("ahf", ND + d, ND + d + 1)
+            ts(A("LT", o, o + 128), K("JJ"), hi, Op.is_gt)
+            ts(A("EQ", o, o + 128), K("JJ"), hi, Op.is_equal)
+            ts(A("LO", o, o + 128), K("IARR"), lo, Op.is_gt, -6.0, Op.mult)
+            mm(ps(6, 0, 128), K("NB6"), A("LT", o, o + 128), False, False)
+            mm(ps(6, 0, 128), A("LO", o, o + 128), A("EQ", o, o + 128), False, d == ND - 1)
+        for f in range(F):
+            ts(A("SL", f, F * ND, F), A("a8", 0, ND), f, Op.add)
+        tt(A("SL2", 0, 30), A("SL", 0, 30), K("JK", 0, 30), Op.min)
+        cp(A("SLu", 0, 30), A("SL2", 0, 30))
+        ts(A("PL", HJ, 2 * HJ), ps(6, HJ, 2 * HJ), 0.0, Op.max)
+        ts(A("PL", 0, HJ), ps(6, 0, HJ), 0.0, Op.max)
+        sgather(A(XN, H, W), A("Xnat"), A("PL", HJ, 2 * HJ))
+        vgather(A(XN, 0, H), A("Xnat"), A("PL", 0, HJ))
+        for d in range(ND):
+            scatter(A(XN), A("SLu", F * d, F * d + F), A(z, SLOT * d, SLOT * d + Q * F))
+        if r + 1 < RO:
+            act(A(XN, W, W + 8), A(XN, 0, 8))
+
+    dma("Y", T.y[:, 0:H], T.XC[:, 0:H], "dy0", [A("XC", 0, H)], [])
+    dma("S", T.y[:, H:W], T.XC[:, H:W], "dy1", [A("XC", H, W)], [])
+    for e in ("V", "S", "T", "G"):
+        wait("G", semof[e], cnt[e])
+    g.wait_ge(T.sem.lsem, tot[0])
+    for s in ("dwt", "dx0", "dx1", "dth", "dy0", "dy1"):
+        g.wait_ge(T.sem[s], 16)
+    for s in ("q0", "q1", "z0", "z1"):
+        g.wait_ge(T.sem[s], landed[s])

@@ -6,19 +6,21 @@ N, W, L, M, P, Q, F, RO = 6, 2048, 16, 6, 32, 16, 6, 2
 H = W // 2
 HJ = H // 16
 ND = N - 1
-SLOT = Q * F + 8
-RING = 6
-NG = 4
 XW = 3072
+WRAP = 14
+SL = W + 16 + 128
+SENT = (SL, W + 16)
+NP = 4
+BIG = 2048.0
 
 SB = {}
 PART = {}
-ARENA = {"int32": ["ar_i", 0], "float32": ["ar_f", 0], "bfloat16": ["ar_b", 0], "uint16": ["ar_u", 0]}
+ARENA = {"int32": ["ar_i", 0], "float32": ["ar_f", 0], "bfloat16": ["ar_b", 0], "uint16": ["ar_u", 0], "float16": ["ar_h", 0]}
 OWN = ("WT", "TH")
 
 
 def sb(name, cols, dtype):
-    if cols <= 160 and dtype in ARENA and name not in OWN and not name.startswith(("QIN", "ASK")):
+    if cols <= 160 and name not in OWN:
         a = ARENA[dtype]
         PART[name] = (a[0], a[1], cols)
         a[1] += -(-cols // 16) * 16
@@ -31,74 +33,117 @@ def many(names, cols, dtype):
         sb(n, cols, dtype)
 
 
-many("XA XB XC", XW, "bfloat16")
-many("XP Xk Xst Xnat WEI EI", W, "bfloat16")
-sb("BIh", W, "float16")
-many("D AB", RING * H, "bfloat16")
-sb("G", NG * H, "bfloat16")
-many("i_ui i_ua i_us i_u2 i_r1 i_r2 i_nxw", 2 * HJ, "int32")
+sb("XA", SL, "bfloat16")
+many("XB XC", XW, "bfloat16")
+many("OTH0 OTH1", ND * SL, "bfloat16")
+many("Xst Xnat XI", W, "bfloat16")
+many("BIh CS", W, "float16")
+many("D RL", M * W, "bfloat16")
+many("i_ui i_ua i_us i_u2 i_r1 i_r2 i_fr", 2 * HJ, "int32")
 many("raw msk", 2 * M * HJ, "int32")
 sb("lst", 2 * M * HJ, "uint16")
-sb("RUN", 2 * M * HJ, "float32")
-sb("RG", 2 * M * HJ, "bfloat16")
-many("f_r f_d f_e", 2 * HJ, "float32")
+many("FAR CNT", M * 128, "bfloat16")
+many("f_a f_d f_e", 2 * HJ, "float32")
 sb("NXH", 2 * HJ, "float16")
-sb("NXW", W, "float32")
-many("CM CS", 256, "float16")
-many("k_RSh k_IDh k_NIh", 128, "float16")
+many("NXW NX2", W, "float32")
+sb("CM", 512, "float16")
+many("k_MS k_IDh k_NIh", 128, "float16")
 many("k_L0h k_ONh", 8, "float16")
-many("LC LF PL", 128, "uint16")
-many("SW J", 128, "float32")
-many("INC ING DEL", 128, "bfloat16")
-many("GO CC EQ LT LO", 640, "bfloat16")
+many("LC LF PL NXU", 128, "uint16")
+many("JA JB INC TI", 128, "bfloat16")
+many("GO GP CC", 640, "bfloat16")
+sb("LT", ND * 136, "bfloat16")
+many("LO HI", 640, "bfloat16")
 sb("AL", 8, "uint16")
-many("plc live pl8", 8, "float32")
-for _r in range(RO):
-    many("ASK%d QIN%d" % (_r, _r), ND * Q, "bfloat16")
-    many("FIL%d ZIN%d" % (_r, _r), ND * SLOT, "bfloat16")
+many("plc live pl8 T2 T2a T2L", 8, "float32")
+sb("ASK", ND * Q, "bfloat16")
+sb("FIL", ND * Q * F, "bfloat16")
 sb("QREP", 12 * ND * Q, "bfloat16")
-many("VM VS", 80, "float32")
+sb("G", 640, "bfloat16")
+sb("VS", 80, "float32")
 many("q_vi q_va q_vs q_vb q_ki q_km q_kc q_kd", 8, "int32")
-many("q_c0 q_v2 q_KM q_kt", 8, "float32")
+many("q_c0 q_v2 q_KM q_kt q_kf", 8, "float32")
 many("qraw qmsk", P * ND, "int32")
 sb("qlst", P * ND, "uint16")
 many("FL SLu", 32, "uint16")
 sb("an", 8, "bfloat16")
-sb("a8", 8, "int32")
-sb("ahl", 16, "int32")
-sb("ahf", 16, "float32")
-many("SL SL2", 32, "float32")
-many("ONB WBLK", 128, "bfloat16")
-many("k_TMP k_BLK k_IDN k_LST1 k_LST6 k_BLK6 k_NB6 k_SHF k_DSH k_ID16 k_NEGI k_N8I k_JJ k_IP1 k_IARRt k_IARR k_ICOL", 128, "bfloat16")
+many("a8 alo", 8, "int32")
+many("am alf", 8, "float32")
+sb("ONB", M * 128, "bfloat16")
+many("k_TMP k_BLK k_IDN k_LST1 k_LSTI k_LST6 k_BLK6 k_NEGI k_N8I k_IP1 k_IARRt k_IARR k_IB k_MQ", 128, "bfloat16")
+many("k_Z k_WZ k_J16", 144, "bfloat16")
+many("k_B1 k_B2 k_BN", 8, "bfloat16")
 many("k_NP1 k_NARRt k_NARR", 640, "bfloat16")
 sb("k_MROWf", P * ND, "float32")
 sb("k_MROW", P * ND, "bfloat16")
 sb("k_ZR", 16, "bfloat16")
-sb("k_MC", P, "float32")
-many("k_MKi k_MKa", 128, "int32")
-many("k_MK k_RS k_ONF k_PWb k_PW1", 128, "float32")
-sb("k_RB5", (M - 1) * HJ, "float32")
-many("k_p k_p2 TH", 8, "int32")
-many("k_I16 k_I64 k_I128 k_LB k_T", 8, "float32")
+many("k_MC k_FB", P, "float32")
+many("k_MKi k_MKa k_PWi k_PW", 128, "int32")
+many("k_MK k_MK1 k_MKb k_ONF k_DG k_T1F", 128, "float32")
+many("k_p k_p2 TH k_th k_tl", 8, "int32")
+many("k_I16 k_I128 k_LB k_T k_B k_BQ k_JKb k_JK k_FC WTf", 8, "float32")
 sb("k_L0", 8, "uint16")
-many("k_CW k_GW WT", 8, "bfloat16")
-many("k_JKb k_JK", 32, "float32")
+many("k_CW k_CWa k_CWb k_GW WT", 8, "bfloat16")
 for _k in range(8):
     SB["ps%d" % _k] = ("psum", [128, 512], "float32")
 for _d in ARENA:
     SB[ARENA[_d][0]] = ("sbuf", [128, ARENA[_d][1]], _d)
 SCRATCH = SB
-SEMAPHORES = ["sV", "sS", "sT", "sG", "lsem", "dx0", "dx1", "dwt", "dth", "dy0", "dy1", "q0", "q1", "z0", "z1"] + ["ga%d" % _k for _k in range(4 * RO)]
+NA = 10
+SEMAPHORES = ["sV", "sS", "sT", "sG", "lsem", "dx0", "dx1", "dwt", "dth", "dy0", "dy1", "o0", "o1", "h0", "h1"] + ["ga%d" % _k for _k in range(NA * RO)]
 
-WB = ((4, 5), (2, 3))
 PLAN = [tuple(int(c) if c.isdigit() else c for c in x.split(".")) for x in (
-    "sg.0.4 v.0.1 sg.0.3 lists v.0.0 a.0.1 sg.1.4 v.0.2 a.0.0 sl.0.4 v.1.0 a.0.2 sl.0.3 v.1.1 a.1.0 v.1.2 a.1.1 consts sl.1.4 v.1.3 "
-    "a.1.2 v.0.5 a.1.3 v.1.5 a.0.5 first.0 first.1 a.1.5 bl.0 succ.0 bl.1 succ.1 win.0 win.1").split()]
+    "la.0.0.3 sg.0.0 la.1.0.3 sg.0.1 vg.1.0 sg.2.0 vg.1.1 sg.2.1 c.1 lb.0.3.6 lb.1.3.6 sg.3.0 sg.3.1 sg.4.0 rl.1.0 rl.1.1 tp.1 c.2 "
+    "rl.0.0 rl.0.1 tp.0 vg.4.1 far.1 rl.2.0 rl.2.1 tp.2 vg.5.0 far.0 ab.4.1 ab.3.0 ab.3.1 t1.3 vg.5.1 far.2 ab.4.0 t1.4 far.3 far.4 "
+    "ab.5.0 ab.5.1 count d5.0 before d5.1 succ.0 win.0 succ.1 win.1 wc.0 wc.1").split()]
+
+
+def helpers(topo, cores, core):
+    able = [c for c in topo.cores_of(core) if c != core and all(topo.may_write(c, o) for o in cores if o != core)]
+    dies = sorted(set(topo.die(c) for c in able))
+    out = []
+    for k in range(NP):
+        on = [c for c in able if topo.die(c) == dies[k % len(dies)]]
+        out.append(on[(k // len(dies)) % len(on)])
+    return out
+
+
+def helper_program(g, core, T, topo):
+    cores = T.cores
+    owner = [c for c in cores if core in topo.cores_of(c)]
+    if not owner:
+        return
+    rank = T.rank_of(owner[0])
+    mine = [k for k, c in enumerate(helpers(topo, cores, owner[0])) if c == core]
+    if not mine:
+        return
+    left = 0
+    for r in range(RO):
+        n = SENT[r] // NP
+        g.wait_ge(T.sem["h%d" % r], len(mine) * len(topo.engines(owner[0], core)) // NP)
+        for k in mine:
+            trs = []
+            for d in range(ND):
+                dest = cores[(rank - 1 - d) % N]
+                rid, pid = topo.addr(dest, core)
+                es = topo.engines(core, dest)
+                src, dst = T["OTH%d" % r][:, n * k:n * k + n], T["OTH%d" % r][:, SL * d + n * k:SL * d + n * k + n]
+                if d < ND - 1:
+                    e = len(es) // (ND - 1)
+                    trs.append(RemoteDMATransfer(dst_ids=[DstId(rid=rid, pnc=pid)], dma_engine_mask=sum(1 << x for x in es[e * d:e * d + e]),
+                                                 remote_sem=T.sem["o%d" % r], src=src, dst=dst))
+                    left += e
+                else:
+                    g.remote_dma_fused(trs, local_sem=T.sem.lsem)
+                    g.remote_dma(dst, src, T.sem["o%d" % r], T.sem.lsem, pid, rid, topo.mask(core, dest))
+                    left += len(es)
+    g.wait_ge(T.sem.lsem, left)
 
 
 def rank_program(g, core, T, topo):
     rank = T.rank_of(core)
     if rank is None:
+        helper_program(g, core, T, topo)
         return
     cores = T.cores
     queue = {"V": g.vector, "S": g.scalar, "T": g.tensor, "G": g, "Y": g.sync}
@@ -145,7 +190,7 @@ def rank_program(g, core, T, topo):
                 ps = SB[a[0]][0] == "psum"
                 for (w, b, sem, val) in log.get(a[0], ()):
                     if sem == own:
-                        if not w or (ps and e == "T" and isw) or not overlap(a, b):
+                        if not (w or isw) or (ps and e == "T" and isw) or not overlap(a, b):
                             continue
                     elif not ps:
                         if not (w or isw) or not overlap(a, b):
@@ -234,349 +279,386 @@ def rank_program(g, core, T, topo):
         else:
             do("G", lambda: g.iota(ap(out), pattern, base, chan), [], [out])
 
-    def asel(out, in_, pattern, op, base, chan):
-        do("G", lambda: g.affine_select(ap(out), ap(in_), pattern, op, 0.0, base, chan), [in_], [out])
+    def asel(out, in_, pattern, op, base, chan, fill=0.0):
+        do("G", lambda: g.affine_select(ap(out), ap(in_), pattern, op, fill, base, chan), [in_], [out])
 
     dma("Y", T.WT[:, 0:1], T.wt[:, :], "dwt", [], [A("WT", 0, 1)])
-    dma("Y", T.XA[:, 0:H], T.x0[:, 0:H], "dx0", [], [A("XA", 0, H)])
+    dma("S", T.XA[:, 0:H], T.x0[:, 0:H], "dx0", [], [A("XA", 0, H)])
+    dma("Y", T.TH[:, 0:2], T.th[:, :], "dth", [], [A("TH", 0, 2)])
     dma("Y", T.XA[:, H:W], T.x0[:, H:W], "dx1", [], [A("XA", H, W)])
-    dma("S", T.TH[:, 0:2], T.th[:, :], "dth", [], [A("TH", 0, 2)])
 
     K = lambda n, c0=0, c1=None, step=1: A("k_" + n, c0, c1, step)
-    ms(A("ONB"), 1.0)
-    asel(K("TMP"), A("ONB"), [[-16, 8], [0, 16]], Op.is_ge, 0, 1)
+    ON = A("ONB", 0, 128)
+    ps = lambda k, c0, c1, step=1: A("ps%d" % k, c0, c1, step)
+    ms(ON, 1.0)
+    asel(K("TMP"), ON, [[-16, 8], [0, 16]], Op.is_ge, 0, 1)
     asel(K("BLK"), K("TMP"), [[16, 8], [0, 16]], Op.is_ge, 15, -1)
-    iota(K("p", 0, 1), [[0, 1]], 0, 1)
     iota(K("MKi"), [[-1, 128]], 128, 1)
-    iota(K("PWb"), [[H, 2], [1, HJ]], 1, 0, True)
+    iota(K("p", 0, 1), [[0, 1]], 0, 1)
+    asel(K("IDN"), ON, [[-1, 128]], Op.is_equal, 0, 1)
+    iota(K("PWi"), [[16, 128]], 1, 0)
     iota(K("LB"), [[16, 8]], 0, 0, True)
-    ms(A("WEI"), 0.0)
-    ms(A("EI"), 0.0)
-    for i in range(16):
-        ts(A("WEI", 128 * i + i, 128 * i + 128, 16), K("BLK", i, 128, 16), A("WT", 0, 1), Op.mult)
-    for i in range(16):
-        act(A("EI", 128 * i + i, 128 * i + 128, 16), K("BLK", i, 128, 16))
-    ts(K("p2", 0, 1), K("p", 0, 1), 15, Op.bitwise_and)
-    cp(K("I16", 0, 1), K("p2", 0, 1))
-    ts(K("I64", 0, 1), K("I16", 0, 1), float(HJ), Op.mult)
-    ts(K("I128", 0, 1), K("I16", 0, 1), 128.0, Op.mult)
-    ts(K("PW1"), K("PWb"), K("I64", 0, 1), Op.add)
-    ts(K("L0"), K("LB"), K("I128", 0, 1), Op.add)
+    ms(K("Z"), 0.0)
+    ms(K("WZ"), 0.0)
+    ms(A("ONB", 128), 1.0)
+    ms(A("FAR", 0, None, M), 0.0)
+    ms(K("ONF"), 1.0)
+    B8 = K("BLK", 0, 128, 16)
+    act(K("Z", 15, 143, 16), B8)
+    act(K("B1"), B8)
+    act(K("B2"), B8, scale=2.0)
+    act(K("BN"), B8, scale=-1.0)
     ts(K("MKa"), K("MKi"), 15, Op.bitwise_and)
     ts(K("MK"), K("MKa"), 0, Op.is_equal)
-    asel(K("IDN"), A("ONB"), [[-1, 128]], Op.is_equal, 0, 1)
-    ts(K("NEGI"), K("IDN"), -1.0, Op.mult)
     for i in range(16):
-        ts(A("BIh", 128 * i, 128 * i + 128), K("BLK"), K("MK", i, i + 1), Op.mult)
-    ms(K("RB5"), 0.0)
-    ms(K("RB5", 0, None, M - 1), 100000.0)
+        act(A("BIh", 128 * i, 128 * i + 128), K("BLK"), scale=K("MK", i, i + 1))
+    ts(K("WZ", 15, 143, 16), B8, A("WT", 0, 1), Op.mult)
+    ts(A("XA", W + 16, SL), K("BLK"), A("WT", 0, 1), Op.mult)
     cp(K("T", 0, 2), A("TH", 0, 2))
-    ms(K("RS"), 1.0)
-    ms(K("RS", 0, None, 16), 0.0)
-    cp(K("RSh"), K("RS"))
-    cp(K("IDh"), K("IDN"))
-    ts(K("NIh"), K("IDN"), -1.0, Op.mult)
-    ts(K("L0h"), K("LB"), K("I128", 0, 1), Op.add)
-    cp(K("ONh"), A("ONB", 0, 8))
-    ms(K("ZR"), 0.0)
-    iota(K("NP1"), [[16, ND], [0, 8], [1, 16]], 1, 0, True)
-    iota(K("JJ"), [[1, 128]], 0, 0, True)
-    iota(K("IP1"), [[0, 8], [1, 16]], 1, 0, True)
-    iota(K("MC"), [[1, P]], 0, 0, True)
-    iota(K("MROWf"), [[1, P], [0, ND]], 0, 0, True)
-    iota(K("JKb", 0, 30), [[16, 30]], 2560, 0, True)
-    asel(K("LST1"), K("BLK"), [[1, 128]], Op.is_ge, -1, -1)
-    asel(K("SHF"), K("BLK"), [[1, 128]], Op.is_equal, -1, -1)
-    asel(K("NARRt"), K("NP1"), [[0, ND], [-16, 8], [0, 16]], Op.is_ge, 0, 1)
-    asel(K("NARR"), K("NARRt"), [[0, ND], [16, 8], [0, 16]], Op.is_ge, 15, -1)
-    asel(K("IARRt"), K("IP1"), [[-16, 8], [0, 16]], Op.is_ge, 0, 1)
-    asel(K("IARR"), K("IARRt"), [[16, 8], [0, 16]], Op.is_ge, 15, -1)
+    ts(K("th", 0, 1), A("TH", 1, 2), 6, Op.arith_shift_right)
+    ts(K("tl", 0, 1), A("TH", 1, 2), 63, Op.bitwise_and)
+    ts(K("p2", 0, 1), K("p", 0, 1), 15, Op.bitwise_and)
+    cp(A("XA", W + WRAP, W + WRAP + 1), K("th", 0, 1))
+    cp(A("XA", W + WRAP + 1, W + WRAP + 2), K("tl", 0, 1))
+    cp(K("I16", 0, 1), K("p2", 0, 1))
+    ts(K("DG"), K("IDN"), K("T", 0, 1), Op.mult)
 
-    def consts_b():
+    def consts_1():
+        mm(ps(3, 0, 128), K("ONF"), K("DG"), True, True)
+        cp(K("T1F"), ps(3, 0, 128))
+
+    def consts_g(k):
+        if k == 0:
+            iota(K("NP1"), [[16, ND], [0, 8], [1, 16]], 1, 0, True)
+        if k == 1:
+            asel(K("NARRt"), K("NP1"), [[0, ND], [-16, 8], [0, 16]], Op.is_ge, 0, 1)
+        if k == 2:
+            asel(K("NARR"), K("NARRt"), [[0, ND], [16, 8], [0, 16]], Op.is_ge, 15, -1)
+        if k == 3:
+            asel(K("LST1"), K("BLK"), [[1, 128]], Op.is_ge, -1, -1)
+            asel(K("LSTI"), K("BLK"), [[1, 128]], Op.is_ge, 0, -1)
+            iota(K("J16"), [[16, 144]], 0, 0, True)
+        if k == 4:
+            iota(K("IP1"), [[0, 8], [1, 16]], 1, 0, True)
+            asel(K("IARRt"), K("IP1"), [[-16, 8], [0, 16]], Op.is_ge, 0, 1)
+            asel(K("IARR"), K("IARRt"), [[16, 8], [0, 16]], Op.is_ge, 15, -1)
+        if k == 5:
+            asel(K("IARRt"), K("IP1"), [[-16, 8], [0, 16]], Op.is_ge, 0, 1, 99.0)
+            asel(K("IB"), K("IARRt"), [[16, 8], [0, 16]], Op.is_ge, 15, -1, 99.0)
+            iota(K("MC"), [[1, P]], 0, 0, True)
+        if k == 6:
+            iota(K("MROWf"), [[1, P], [0, ND]], 0, 0, True)
+            iota(K("JKb", 0, ND), [[16 * F, ND]], 2560, 0, True)
+            iota(K("FB", 0, ND * F), [[SL, ND], [1, F]], 1, 0, True)
+            iota(K("FC", 0, F), [[1, F]], 0, 0, True)
+
+    def consts_2():
+        ts(K("PW"), K("PWi"), K("I16", 0, 1), Op.add)
+        ts(K("PW"), K("PW"), W - 1, Op.bitwise_and)
+        ts(K("MK1"), K("MKa"), 15, Op.is_equal, -BIG, Op.mult)
+        ts(K("MKb"), K("MK"), 2 * BIG, Op.mult)
+        tt(K("MS"), K("MK1"), K("MKb"), Op.add)
+        ts(K("MQ"), K("MS"), 1024.0, Op.mult)
+        ts(K("B", 0, 1), K("I16", 0, 1), 15.0, Op.is_lt, BIG, Op.mult)
+        ts(K("BQ", 0, 1), K("B", 0, 1), 1024.0, Op.mult)
+        ts(K("I128", 0, 1), K("I16", 0, 1), 128.0, Op.mult)
+        ts(K("L0"), K("LB"), K("I128", 0, 1), Op.add)
+        ts(K("L0h"), K("LB"), K("I128", 0, 1), Op.add, K("B", 0, 1), Op.subtract)
+        cp(K("IDh"), K("IDN"))
+        ts(K("NIh"), K("IDN"), -1.0, Op.mult)
+        cp(K("ONh"), A("ONB", 0, 8))
+
+    def consts_3():
         act(K("MROW"), K("MROWf"), scale=1.0 / P)
         act(K("LST6"), K("LST1"), scale=6.0)
         act(K("BLK6"), K("BLK"), scale=6.0)
-        act(K("NB6"), K("BLK"), scale=-6.0)
-        act(K("ID16"), K("IDN"), scale=16.0)
         act(K("N8I"), K("IDN"), scale=-8192.0)
-        act(K("ICOL"), A("ONB"), scale=K("I16", 0, 1))
-        for r in range(RO):
-            act(A("FIL%d" % r), K("NARR", 0, ND * SLOT), scale=0.0)
+        act(K("NEGI"), K("IDN"), scale=-1.0)
+        act(K("ZR"), A("ONB", 0, 16), scale=0.0)
+        act(K("CW", 0, 1), A("ONB", 0, 1), scale=16.0)
+        act(K("CW", 1, 2), A("ONB", 0, 1))
+        act(K("GW", 0, 1), A("ONB", 0, 1))
+        act(K("GW", 1, 2), A("ONB", 0, 1), scale=128.0)
 
-    def consts_c():
-        ms(K("ONF"), 1.0)
-        tt(K("DSH"), K("IDN"), K("SHF"), Op.subtract)
-        ts(K("CW", 0, 1), K("MK", 15, 16), -2032.0, Op.mult, 128.0, Op.add)
-        ms(K("CW", 1, 2), 1.0)
-        ms(K("GW", 0, 1), 1.0)
-        ms(K("GW", 1, 2), 128.0)
-        ts(A("WBLK"), K("BLK"), A("WT", 0, 1), Op.mult)
-        ts(K("JK", 0, 30), K("JKb", 0, 30), K("I16", 0, 1), Op.add)
+    def consts_4():
+        ts(K("JKb", ND, ND + 1), K("I16", 0, 1), float(F), Op.mult)
+        ts(K("JK", 0, ND), K("JKb", 0, ND), K("JKb", ND, ND + 1), Op.add)
 
-    def send(src, dst, dest, sem, alone):
-        trs, order = [], [d for d in range(ND) if d != alone] + [alone]
-        for k, d in enumerate(order):
-            need("G", [src[d]], [])
-            rid, pid = topo.addr(dest[d], core)
-            es = topo.engines(core, dest[d])
-            if k < 4:
-                n = len(es) // 4
-                mask = sum(1 << e for e in es[n * k:n * k + n])
-                trs.append(RemoteDMATransfer(dst_ids=[DstId(rid=rid, pnc=pid)], dma_engine_mask=mask, remote_sem=T.sem[sem],
-                                             src=ap(src[d]), dst=ap(dst[d])))
-                if k == 3:
-                    g.remote_dma_fused(trs, local_sem=T.sem.lsem)
-        g.remote_dma(ap(dst[alone]), ap(src[alone]), T.sem[sem], T.sem.lsem, pid, rid, topo.mask(core, dest[alone]))
-        tot[0] += 4 * n + len(es)
-        return 4 * n + len(es)
-
-    tot, ring, gs, landed, place, na = [0], [0], [0], {}, {}, [0]
+    hs = helpers(topo, cores, core)
+    tot, na = [0], [0]
     xs = ("XA", "XB", "XC")
-    ps = lambda k, c0, c1, step=1: A("ps%d" % k, c0, c1, step)
     for r in range(RO):
-        X, XN = xs[r], xs[r + 1]
+        X, XN, OTH = xs[r], xs[r + 1], "OTH%d" % r
 
         for h in range(2):
             for i in range(16):
-                mm(ps(h, 0, HJ), A("WEI", 128 * i, 128 * i + 128), A(X, H * h + HJ * i, H * h + HJ * i + HJ), i == 0, i == 15)
-            for i in range(16):
-                act(A("XP", H * h + i, H * h + H, 16), A(X, H * h + HJ * i, H * h + HJ * i + HJ))
-        if r == 0:
-            act(A(X, W, W + 8), A(X, 0, 8))
+                mm(ps(h, 0, HJ), K("WZ", 15 - i, 143 - i), A(X, H * h + i, H * h + H, 16), i == 0, i == 15)
+        n = WRAP if r == 0 else 16
+        act(A(X, W, W + n), A(X, 0, n))
+        for h in range(2):
+            act(A("XI", H * h, H * h + H), A(X, H * h, H * h + H))
+        n = SENT[r] // NP
+        need("G", [A(X, 0, SENT[r])], [])
+        trs = []
+        for k in range(NP):
+            rid, pid = topo.addr(hs[k], core)
+            es = topo.engines(core, hs[k])
+            e = len(es) // NP
+            trs.append(RemoteDMATransfer(dst_ids=[DstId(rid=rid, pnc=pid)], dma_engine_mask=sum(1 << x for x in es[e * k:e * k + e]),
+                                         remote_sem=T.sem["h%d" % r], src=T[X][:, n * k:n * k + n], dst=T[OTH][:, n * k:n * k + n]))
+            tot[0] += e
+        g.remote_dma_fused(trs, local_sem=T.sem.lsem)
 
-        def lists(h):
+        def lists(h, m0, m1):
             o, e = HJ * h, HJ * h + HJ
             ui, ua, us = [A("i_" + n, o, e) for n in ("ui", "ua", "us")]
             u2, bb = ps(6 + h, 128, 128 + HJ), ps(6 + h, 256, 256 + HJ)
             R = lambda m: A("raw", M * HJ * h + HJ * m, M * HJ * h + HJ * m + HJ)
-            al = lambda n: A(n, M * HJ * h, M * HJ * h + M * HJ)
-            cp(ui, ps(h, 0, HJ))
-            ts(ua, ui, W - 1, Op.bitwise_and)
-            ts(us, ui, W - 1, Op.bitwise_and, 5, Op.arith_shift_right)
-            ts(u2, ua, 2, Op.mult)
-            tt(bb, ua, us, Op.mult)
-            tt(R(0), bb, ua, Op.add)
-            for m in range(1, M):
+            al = lambda n: A(n, M * HJ * h + HJ * m0, M * HJ * h + HJ * m1)
+            if m0 == 0:
+                cp(ui, ps(h, 0, HJ))
+                ts(ua, ui, W - 1, Op.bitwise_and)
+                ts(us, ui, W - 1, Op.bitwise_and, 5, Op.arith_shift_right)
+                tt(bb, ua, us, Op.mult)
+                ts(u2, ua, 2, Op.mult)
+                tt(R(0), bb, ua, Op.add)
+            for m in range(max(m0, 1), m1):
                 tt(R(m), u2, R(m - 1), Op.add)
             ts(al("msk"), al("raw"), W - 1, Op.bitwise_and)
             cp(al("lst"), al("msk"))
-            ts(A("i_r1", o, e), R(0), 1, Op.add)
-            ts(A("i_u2", o, e), ua, 2, Op.mult)
+            if m1 == M:
+                ts(A("i_r1", o, e), R(0), 1, Op.add)
+                ts(A("i_u2", o, e), ua, 2, Op.mult)
 
-        def lk(h, m):
+        def lk(m, h):
             return A("lst", M * HJ * h + HJ * m, M * HJ * h + HJ * m + HJ)
 
-        def slot():
-            ring[0] += 1
-            o = H * (ring[0] % RING)
-            return A("D", o, o + H), A("AB", o, o + H), o
+        U = lambda n, m, h: A(n, W * m + H * h, W * m + H * h + H)
 
-        def gslot(n):
-            gs[0] += 1
-            o = H * (gs[0] % NG)
-            return A("G", o, o + n)
-
-        def dist(h, m, o):
-            out = ps(2 + h, m, (M - 1) * HJ, M - 1) if m < M - 1 else ps(h, 0, HJ)
-            for i in range(16):
-                mm(out, A("EI", 128 * i, 128 * i + 128), A("AB", o + i, o + H, 16), i == 0, i == 15)
-
-        def sgath(h, m):
-            a, b = gslot(H), A("XP", H * h, H * h + H)
-            place["g", h, m] = a
-            sgather(a, A(X, 0, W), lk(h, m), scale=-1.0)
+        def sgath(m, h):
+            a, b = U("D", m, h), A(X, H * h, H * h + H)
+            sgather(a, A(X, 0, W), lk(m, h), scale=-1.0)
             dma("G", ap(a), ap(b), "ga%d" % na[0], [b], [a], accum_op=Op.add)
+            if r == 0:
+                consts_g(na[0])
             na[0] += 1
 
-        def slook(h, m):
-            d, a, o = slot()
-            act(a, place["g", h, m], Fn.Abs)
-            dist(h, m, o)
+        def vgath(m, h):
+            vgather(U("D", m, h), A(X, 0, W), lk(m, h), A("XI", H * h, H * h + H), Op.subtract)
 
-        def vlook(h, m):
-            d, a, o = slot()
-            place[h, m] = d, a, o
-            vgather(d, A(X, 0, W), lk(h, m), A("XP", H * h, H * h + H), Op.subtract)
+        def relu(m, h):
+            ts(U("RL", m, h), U("D", m, h), 0.0, Op.max)
 
-        def size(h, m):
-            d, a, o = place[h, m]
-            act(a, d, Fn.Abs)
-            dist(h, m, o)
+        def size(m, h):
+            act(U("RL", m, h), U("D", m, h), Fn.Abs)
 
-        def first(h):
-            o, n = M * HJ * h, (M - 1) * HJ
-            scan(A("RUN", o, o + n), K("RB5"), ps(2 + h, 0, n), Op.add, Op.min)
-            ts(A("RG", o, o + n), A("RUN", o, o + n), K("T", 0, 1), Op.is_ge)
-            for m in range(M - 1):
-                mm(ps(6 + h, 0, HJ), K("IDN"), A("RG", o + m, o + n, M - 1), m == 0, m == M - 2)
+        def tpass(m, both=True):
+            for i in range(16):
+                out = ps(2 + m % 2, 128 * (m // 2) + i, 128 * (m // 2) + 128, 16)
+                if both:
+                    mm(out, A("D", W * m + i, W * m + W, 16), K("BN"), True, False)
+                mm(out, A("RL", W * m + i, W * m + W, 16), K("B2") if both else K("B1"), not both, True)
 
-        def before_last(h):
-            o, n, s, e = M * HJ * h, (M - 1) * HJ, HJ * h, HJ * h + HJ
-            ft, fd = ps(6 + h, 128, 128 + HJ), ps(6 + h, 256, 256 + HJ)
-            tt(ft, ps(6 + h, 0, HJ), A("i_u2", s, e), Op.mult)
-            tt(A("f_r", s, e), ft, A("i_r1", s, e), Op.add)
-            tt(fd, K("PW1", s, e), A("f_r", s, e), Op.subtract)
-            tt(A("f_e", s, e), fd, A("RG", o + M - 2, o + n, M - 1), Op.mult)
+        def far(m):
+            tt(A("FAR", M - 1 - m, None, M), ps(2 + m % 2, 128 * (m // 2), 128 * (m // 2) + 128), K("T1F"), Op.is_ge)
+
+        def count():
+            scan(A("CNT"), A("ONB"), A("FAR"), Op.add, Op.mult)
+            mm(ps(3, 256, 384), A("CNT", M - 1, None, M), K("IDN"), True, True)
+
+        def before_last():
+            c, ft, fd = ps(3, 256, 384), ps(2, 128, 256), ps(2, 256, 384)
+            tt(ft, c, A("i_u2"), Op.mult)
+            ts(A("f_a"), c, float(M - 1), Op.is_ge)
+            tt(A("i_r2"), ft, A("i_r1"), Op.add)
+            ts(A("i_fr"), A("i_r2"), W - 1, Op.bitwise_and)
+            tt(fd, K("PW"), A("i_fr"), Op.subtract)
+            tt(A("f_e"), fd, A("f_a"), Op.mult)
+
+        def dist5(h):
+            o = W * (M - 1) + H * h
+            for i in range(16):
+                mm(ps(h, 0, HJ), K("Z", 15 - i, 143 - i), A("RL", o + i, o + H, 16), i == 0, i == 15)
 
         def succ(h):
             s, e = HJ * h, HJ * h + HJ
-            ft = ps(6 + h, 128, 128 + HJ)
+            ft, fd = ps(2, 128, 128 + HJ), ps(2, 256, 256 + HJ)
             ts(ft, ps(h, 0, HJ), K("T", 0, 1), Op.is_ge)
-            tt(A("f_d", s, e), ft, A("f_e", s, e), Op.mult)
-            tt(A("i_r2", s, e), A("f_r", s, e), A("f_d", s, e), Op.add)
-            ts(A("i_nxw", s, e), A("i_r2", s, e), W - 1, Op.bitwise_and)
-            cp(A("NXH", s, e), A("i_nxw", s, e))
-            for i in range(16):
-                mm(ps(WB[h][i // 8], HJ * (i % 8), HJ * (i % 8) + HJ), A("BIh", 128 * i, 128 * i + 128), A("NXH", s, e), True, True)
+            tt(fd, ft, A("f_e", s, e), Op.mult)
+            tt(A("NXH", s, e), fd, A("i_fr", s, e), Op.add)
+            cp(A("NXU", s, e), A("NXH", s, e))
 
         def window(h):
-            act(A("NXW", H * h, H * h + 512), ps(WB[h][0], 0, 512))
-            cp(A("NXW", H * h + 512, H * h + H), ps(WB[h][1], 0, 512))
+            for i in range(16):
+                mm(wat(h, i), A("BIh", 128 * i, 128 * i + 128), A("NXH", HJ * h, HJ * h + HJ), True, True)
 
-        calls = {"sg": sgath, "sl": slook, "v": vlook, "a": size, "first": first, "bl": before_last, "succ": succ,
-                 "win": window, "lists": lambda: lists(1), "consts": consts_c if r == 0 else (lambda: None)}
-        lists(0)
+        def wat(h, i):
+            if h == 0:
+                return ps(4 + i // 8, HJ * (i % 8), HJ * (i % 8) + HJ)
+            return ps((6, 7, 0, 3)[i // 4], HJ * (i % 4), HJ * (i % 4) + HJ)
+
+        def wcopy(h):
+            for i in range(16):
+                (cp if (i // (4 if h else 8)) % 2 else act)(A("NXW", H * h + i, H * h + H, 16), wat(h, i))
+
+        def once(k):
+            if r == 0:
+                (consts_1, consts_2)[k - 1]()
+
+        calls = {"sg": sgath, "vg": vgath, "rl": relu, "ab": size, "tp": tpass, "t1": lambda m: tpass(m, False), "far": far, "count": count,
+                 "before": before_last, "d5": dist5, "succ": succ, "win": window, "wc": wcopy, "la": lists, "lb": lists, "c": once}
         for step in PLAN:
             calls[step[0]](*step[1:])
-        if r == 0:
-            consts_b()
+
+        def pick(k):
+            o = 128 * (k % 4)
+            scan(A("CS", 128 * k, 128 * k + 128), K("MS"), A("CM", o, o + 128), Op.add, Op.min)
+
+        now = lambda k: A("CS", 128 * k + 15, 128 * k + 128, 16) if k else K("L0h")
+        lc = lambda k: A("LC", 8 * k, 8 * k + 8) if k else K("L0")
+        cm = lambda k: A("CM", 128 * (k % 4), 128 * (k % 4) + 128)
+
+        def settle(k):
+            ts(lc(k), now(k), K("B", 0, 1), Op.add)
+            mm(ps(7, k - 1, 128, 16), K("NIh"), now(k - 1), True, False)
+            mm(ps(7, k - 1, 128, 16), K("IDh"), now(k), False, True)
+            mm(ps(3, k, 128, 16), K("IDh"), now(k), True, True)
 
         mm(ps(7, 15, 128, 16), K("IDh"), K("ONh"), True, True)
         mm(ps(3, 0, 128, 16), K("IDh"), K("L0h"), True, True)
-        prev, last = K("L0"), K("L0h")
-        sgather(A("Xk", 0, 128), A(X, 0, W), prev)
-        for k in range(1, L):
-            o = 128 * (k % 2)
-            vgather(A("CM", o, o + 128), A("NXW"), prev, K("MK"), Op.mult)
-            scan(A("CS", o, o + 128), K("RSh"), A("CM", o, o + 128), Op.mult, Op.add)
-            prev = A("LC", 8 * k, 8 * k + 8)
-            now = A("CS", o + 15, o + 128, 16)
-            cp(prev, now)
-            mm(ps(3, k, 128, 16), K("IDh"), now, True, True)
-            mm(ps(7, k - 1, 128, 16), K("NIh"), last, True, False)
-            mm(ps(7, k - 1, 128, 16), K("IDh"), now, False, True)
-            last = now
-            if k == L - 1:
-                cp(A("LF"), ps(3, 0, 128))
-                act(A("SW"), ps(7, 0, 128), Fn.Abs, bias=1023.0)
-            sgather(A("Xk", 128 * k, 128 * k + 128), A(X, 0, W), prev)
-        sgather(A("Xst"), A(X, 0, W), A("LF"))
+        cut = 68
+        sgather(cm(1), A("NXW"), lc(0))
+        vgather(A("NX2", 0, 16 * cut), A("NXW"), A("NXU", 0, cut))
+        sgather(A("NX2", 16 * cut, W), A("NXW"), A("NXU", cut, 128))
+        pick(1)
+        settle(1)
+        if r == 0:
+            consts_4()
+        for k in range(2, L, 2):
+            sgather(cm(k + 1), A("NX2"), lc(k - 1))
+            vgather(cm(k), A("NX2"), lc(k - 2))
+            pick(k)
+            settle(k)
+            pick(k + 1)
+            if k + 1 < L - 1:
+                settle(k + 1)
+        k = L - 1
+        mm(ps(7, k - 1, 128, 16), K("NIh"), now(k - 1), True, False)
+        mm(ps(7, k - 1, 128, 16), K("IDh"), now(k), False, True)
+        mm(ps(3, k, 128, 16), K("IDh"), now(k), True, True)
+        if r == 0:
+            consts_3()
 
-        ts(A("J"), A("SW"), 1024.0, Op.not_equal)
+        ts(A("JA"), ps(7, 0, 128), 1.0, Op.not_equal, -1.0, Op.add)
+        ts(A("JB"), ps(7, 0, 128), 1.0 - W, Op.not_equal)
+        scan(A("INC"), A("JA"), A("JB"), Op.add, Op.add)
+        ts(A("LF"), ps(3, 0, 128), K("B", 0, 1), Op.add)
+        sgather(A("Xst"), A(X, 0, W), A("LF"))
         mm(ps(2, 0, 2 * ND), K("IDN"), K("ZR", 0, 2 * ND), True, False)
-        scan(A("INC"), K("ONF"), A("J"), Op.mult, Op.add)
         mm(ps(6, 0, 1), K("LST1"), A("INC", 127, 128), True, True)
-        ts(A("ING"), A("INC"), ps(6, 0, 1), Op.add, 200.0, Op.min)
-        mm(ps(7, 0, 128), K("DSH"), A("ING"), True, True)
-        ts(A("GO"), K("NARR"), ps(6, 0, 1), Op.is_gt)
-        cp(A("DEL"), ps(7, 0, 128))
+        mm(ps(6, 1, 2), K("LSTI"), A("INC", 127, 128), True, True)
+        ts(A("TI"), A("INC"), -1.0, Op.mult, A("INC", 127, 128), Op.add)
         for c in range(2):
-            mm(ps(c, 0, 320), A("DEL"), A("GO", 320 * c, 320 * c + 320), True, True)
+            s, e = 320 * c, 320 * c + 320
+            ts(A("GO", s, e), K("NARR", s, e), ps(6, 0, 1), Op.is_gt)
+            ts(A("GP", s, e), K("NARR", s, e), ps(6, 1, 2), Op.is_gt)
+            mm(ps(c, 0, 320), A("INC"), A("GO", s, e), True, False)
+            mm(ps(c, 0, 320), A("TI"), A("GP", s, e), False, True)
         for c in range(2):
             tt(A("CC", 320 * c, 320 * c + 320), ps(c, 0, 320), K("NP1", 320 * c, 320 * c + 320), Op.is_lt)
         for s, w in (("GO", "GW"), ("CC", "CW")):
             for d in range(ND):
                 mm(ps(2, 2 * d, 2 * d + 2), A(s, 128 * d, 128 * d + 128), K(w, 0, 2), False, s == "CC" and d == ND - 1)
-        ts(A("AL", 0, ND), ps(2, 0, 2 * ND, 2), -1.0, Op.add)
-        ak, qn = "ASK%d" % r, "QIN%d" % r
-        vgather(A(ak), A("Xk"), A("AL", 0, ND))
-        qs = [(Q * d, Q * d + Q) for d in range(ND)]
-        landed["q%d" % r] = send([A(ak, *x) for x in qs], [A(qn, *x) for x in qs], [cores[(rank + 1 + d) % N] for d in range(ND)], "q%d" % r, ND - 1)
-        ts(A("plc", 0, ND), ps(2, 1, 2 * ND, 2), -128.0, Op.add)
-        ts(A("live", 0, ND), A("plc", 0, ND), float(W), Op.is_lt)
-        ts(A("pl8", 0, ND), A("plc", 0, ND), 8193.0, Op.add)
-        mm(ps(6, 0, 128), K("ID16"), K("JJ"), True, False)
-        mm(ps(6, 0, 128), K("IDN"), K("ICOL"), False, False)
+        ts(A("AL", 0, ND), ps(2, 0, 2 * ND, 2), -1.0, Op.add, W - 1.0, Op.min)
+        vgather(A("ASK"), A("Xst"), A("AL", 0, ND))
+        for i in range(16):
+            asel(A("Xnat", 128 * i, 128 * i + 128), A("Xst", i, W, 16), [[0, 128]], Op.is_ge, 0, 0)
 
-        note([], [A(qn)], "q%d" % r, landed["q%d" % r])
-        mm(ps(3, 0, 80), A("WBLK"), A(qn), True, True)
-        act(A("QREP", 0, 80), A(qn))
-        act(A("QREP", 80, 160), A(qn))
+        note([], [A(OTH)], "o%d" % r, NP * 2 * len(topo.engines(core, cores[(rank + 1) % N])))
+        for d in range(ND):
+            mm(ps(3, Q * d, Q * d + Q), A("OTH0", SL * d + W + 16, SL * d + SL), A("ASK", Q * d, Q * d + Q), True, True)
+        act(A("QREP", 0, 80), A("ASK"))
+        act(A("QREP", 80, 160), A("ASK"))
         act(A("QREP", 160, 320), A("QREP", 0, 160))
         act(A("QREP", 320, 640), A("QREP", 0, 320))
         act(A("QREP", 640, 960), A("QREP", 0, 320))
-        tt(A("VM"), ps(3, 0, 80), K("MK", 0, 80), Op.mult)
-        scan(A("VS"), K("RS", 0, 80), A("VM"), Op.mult, Op.add)
+        ts(A("plc", 0, ND), ps(2, 1, 2 * ND, 2), -128.0, Op.add)
+        scan(A("VS"), K("MQ", 0, 80), ps(3, 0, 80), Op.add, Op.min)
         q = lambda n: A("q_" + n, 0, ND)
-        cp(q("vi"), A("VS", 15, 80, 16))
+        ts(q("vi"), A("VS", 15, 80, 16), K("BQ", 0, 1), Op.add)
+        ts(A("live", 0, ND), A("plc", 0, ND), float(W), Op.is_lt)
         ts(q("va"), q("vi"), W - 1, Op.bitwise_and)
         ts(q("vs"), q("vi"), W - 1, Op.bitwise_and, 5, Op.arith_shift_right)
         ts(q("v2"), q("va"), 2, Op.mult)
         tt(q("vb"), q("va"), q("vs"), Op.mult)
+        ts(A("pl8", 0, ND), A("plc", 0, ND), 8193.0, Op.add)
         tt(q("c0"), q("vb"), q("va"), Op.add)
         for d in range(ND):
             ts(A("qraw", d, P * ND, ND), K("MC"), A("q_v2", d, d + 1), Op.mult, A("q_c0", d, d + 1), Op.add)
-        ts(A("qmsk"), A("qraw"), W - 1, Op.bitwise_and)
-        cp(A("qlst"), A("qmsk"))
+        for d in range(ND):
+            ts(A("qmsk", d, P * ND, ND), A("qraw", d, P * ND, ND), W - 1, Op.bitwise_and)
+        for d in range(ND):
+            ts(A("qlst", d, P * ND, ND), A("qmsk", d, P * ND, ND), float(SL * d), Op.add)
+        mm(ps(6, 0, 128), K("IDN"), K("J16", 0, 128), True, False)
         parts = [(0, 60), (60, 120), (120, 160)]
-        gb = gslot(640)
-        sgather(gb, A(X, 0, W), A("qlst", 120, 160))
+        sgather(A("G"), A(OTH), A("qlst", 120, 160))
         for c in range(2):
-            mm(ps(1 - c, 0, 320), K("IDN"), A("G", gb[1] + 320 * c, gb[1] + 320 * c + 320), True, False)
+            mm(ps(1 - c, 0, 320), K("IDN"), A("G", 320 * c, 320 * c + 320), True, False)
             mm(ps(1 - c, 0, 320), K("NEGI"), A("QREP", 0, 320), False, True)
         for t in (0, 2, 1):
             l0, l1 = parts[t]
-            n = 16 * (l1 - l0)
-            d, a, o = slot()
+            n, o = 16 * (l1 - l0), H * t
             if t < 2:
-                vgather(A("D", o, o + n), A(X, 0, W), A("qlst", l0, l1), A("QREP", 0, n), Op.subtract)
-                act(A("AB", o, o + n), A("D", o, o + n), Fn.Abs)
+                vgather(A("D", o, o + n), A(OTH), A("qlst", l0, l1), A("QREP", 0, n), Op.subtract)
+                act(A("RL", o, o + n), A("D", o, o + n), Fn.Abs)
             else:
                 for c in range(2):
-                    act(A("AB", o + 320 * c, o + 320 * c + 320), ps(1 - c, 0, 320), Fn.Abs)
+                    act(A("RL", o + 320 * c, o + 320 * c + 320), ps(1 - c, 0, 320), Fn.Abs)
             mm(ps(4, l0, l1), K("IDN"), K("MROW", l0, l1), True, False)
             for i in range(16):
-                mm(ps(4, l0, l1), A("EI", 128 * i, 128 * i + 128), A("AB", o + i, o + n, 16), False, i == 15)
+                mm(ps(4, l0, l1), K("Z", 15 - i, 143 - i), A("RL", o + i, o + n, 16), False, i == 15)
+        if r == 0:
+            ts(A("T2a", 0, ND), A("OTH0", W + WRAP, None, SL), 64.0, Op.mult)
+            tt(A("T2", 0, ND), A("T2a", 0, ND), A("OTH0", W + WRAP + 1, None, SL), Op.add)
+        tt(A("T2L", 0, ND), A("T2", 0, ND), A("live", 0, ND), Op.mult)
         for d in range(ND):
             a, b = A("q_KM", d, d + 1), ps(4, d, P * ND, ND)
             do("V", lambda: g.vector.tensor_reduce(ap(a), ap(b), AxisListType.X, Op.min), [b], [a])
-        ts(q("ki"), q("KM"), float(P), Op.mult)
-        fl = "FIL%d" % r
-        ts(q("km"), q("ki"), P - 1, Op.bitwise_and)
-        tt(q("kt"), q("km"), q("v2"), Op.mult)
-        tt(q("kc"), q("kt"), q("c0"), Op.add)
-        ts(q("kd"), q("kc"), W - 1, Op.bitwise_and)
-        for f in range(F):
-            ts(A("FL", f, F * ND, F), q("kd"), f + 1, Op.add)
-        ts(A(fl, Q * F, ND * SLOT, SLOT), q("KM"), K("T", 1, 2), Op.is_lt)
-        for d in (0, 3, 1, 4, 2):
-            (sgather if d > 2 else vgather)(A(fl, SLOT * d, SLOT * d + Q * F), A(X, 0, W + 8), A("FL", F * d, F * d + F))
-        z = "ZIN%d" % r
-        zs = [(SLOT * d, SLOT * d + SLOT) for d in range(ND)]
-        landed["z%d" % r] = send([A(fl, *x) for x in zs], [A(z, *x) for x in zs], [cores[(rank - 1 - d) % N] for d in range(ND)], "z%d" % r, 2)
-        for i in range(16):
-            act(A("Xnat", 128 * i, 128 * i + 128), A("Xst", i, W, 16))
 
-        note([], [A(z)], "z%d" % r, landed["z%d" % r])
-        tt(A("an", 0, ND), A(z, Q * F, ND * SLOT, SLOT), A("live", 0, ND), Op.mult)
+        tt(A("an", 0, ND), q("KM"), A("T2L", 0, ND), Op.is_lt)
         mm(ps(5, 0, ND), K("LST6"), A("an", 0, ND), True, False)
         for k in range(1, ND):
             mm(ps(5, k, ND), K("BLK6"), A("an", 0, ND - k), False, False)
         mm(ps(5, 0, ND), K("N8I"), A("an", 0, ND), False, True)
+        ts(q("ki"), q("KM"), float(P), Op.mult)
+        ts(q("km"), q("ki"), P - 1, Op.bitwise_and)
+        tt(q("kt"), q("km"), q("v2"), Op.mult)
         tt(A("a8", 0, ND), ps(5, 0, ND), A("pl8", 0, ND), Op.add)
-        ts(A("ahl", 0, ND), A("a8", 0, ND), 4, Op.arith_shift_right)
-        ts(A("ahl", ND, 2 * ND), A("a8", 0, ND), 15, Op.bitwise_and)
-        cp(A("ahf", 0, 2 * ND), A("ahl", 0, 2 * ND))
+        tt(q("kc"), q("kt"), q("c0"), Op.add)
+        ts(A("alo", 0, ND), A("a8", 0, ND), 15, Op.bitwise_and)
+        tt(A("am", 0, ND), A("a8", 0, ND), K("JK", 0, ND), Op.min)
+        cp(A("alf", 0, ND), A("alo", 0, ND))
+        ts(q("kd"), q("kc"), W - 1, Op.bitwise_and)
         for d in range(ND):
-            o = 128 * d
-            hi, lo = A("ahf", d, d + 1), A("ahf", ND + d, ND + d + 1)
-            ts(A("LT", o, o + 128), K("JJ"), hi, Op.is_gt)
-            ts(A("EQ", o, o + 128), K("JJ"), hi, Op.is_equal)
+            o, lt = 128 * d, 136 * d
+            lo = A("alf", d, d + 1)
+            ts(A("LT", lt, lt + 129), K("J16", 0, 129), A("am", d, d + 1), Op.is_gt)
+            ts(A("HI", o, o + 128), K("IB"), lo, Op.is_le, -6.0, Op.mult)
             ts(A("LO", o, o + 128), K("IARR"), lo, Op.is_gt, -6.0, Op.mult)
-            mm(ps(6, 0, 128), K("NB6"), A("LT", o, o + 128), False, False)
-            mm(ps(6, 0, 128), A("LO", o, o + 128), A("EQ", o, o + 128), False, d == ND - 1)
-        for f in range(F):
-            ts(A("SL", f, F * ND, F), A("a8", 0, ND), f, Op.add)
-        tt(A("SL2", 0, 30), A("SL", 0, 30), K("JK", 0, 30), Op.min)
-        cp(A("SLu", 0, 30), A("SL2", 0, 30))
-        ts(A("PL", HJ, 2 * HJ), ps(6, HJ, 2 * HJ), 0.0, Op.max)
-        ts(A("PL", 0, HJ), ps(6, 0, HJ), 0.0, Op.max)
-        sgather(A(XN, H, W), A("Xnat"), A("PL", HJ, 2 * HJ))
-        vgather(A(XN, 0, H), A("Xnat"), A("PL", 0, HJ))
+            mm(ps(6, 0, 128), A("HI", o, o + 128), A("LT", lt, lt + 128), False, False)
+            mm(ps(6, 0, 128), A("LO", o, o + 128), A("LT", lt + 1, lt + 129), False, d == ND - 1)
+            if d == 0:
+                cp(q("kf"), q("kd"))
         for d in range(ND):
-            scatter(A(XN), A("SLu", F * d, F * d + F), A(z, SLOT * d, SLOT * d + Q * F))
-        if r + 1 < RO:
-            act(A(XN, W, W + 8), A(XN, 0, 8))
+            ts(A("FL", F * d, F * d + F), K("FB", F * d, F * d + F), A("q_kf", d, d + 1), Op.add)
+        sgather(A("FIL"), A(OTH), A("FL", 0, ND * F))
+        ts(A("PL", HJ, 2 * HJ), ps(6, HJ, 2 * HJ), K("I16", 0, 1), Op.add, 0.0, Op.max)
+        ts(A("PL", 0, HJ), ps(6, 0, HJ), K("I16", 0, 1), Op.add, 0.0, Op.max)
+        sgather(A(XN, H, W), A("Xnat"), A("PL", HJ, 2 * HJ))
+        for d in range(ND):
+            ts(A("SLu", F * d, F * d + F), K("FC", 0, F), A("am", d, d + 1), Op.add)
+        vgather(A(XN, 0, H), A("Xnat"), A("PL", 0, HJ))
+        scatter(A(XN), A("SLu", 0, ND * F), A("FIL"))
 
     dma("Y", T.y[:, 0:H], T.XC[:, 0:H], "dy0", [A("XC", 0, H)], [])
     dma("S", T.y[:, H:W], T.XC[:, H:W], "dy1", [A("XC", H, W)], [])
@@ -585,5 +667,3 @@ def rank_program(g, core, T, topo):
     g.wait_ge(T.sem.lsem, tot[0])
     for s in ("dwt", "dx0", "dx1", "dth", "dy0", "dy1"):
         g.wait_ge(T.sem[s], 16)
-    for s in ("q0", "q1", "z0", "z1"):
-        g.wait_ge(T.sem[s], landed[s])

@@ -39,11 +39,12 @@ many("OTH0 OTH1", ND * SL, "bfloat16")
 many("Xst Xnat XI", W, "bfloat16")
 many("BIh CS", W, "float16")
 many("D RL", M * W, "bfloat16")
-many("i_ui i_ua i_us i_u2 i_r1 i_r2 i_fr", 2 * HJ, "int32")
+many("i_ui i_ua i_us i_r1 i_r2 i_fr i_n5 i_n6", 2 * HJ, "int32")
 many("raw msk", 2 * M * HJ, "int32")
 sb("lst", 2 * M * HJ, "uint16")
 many("FAR CNT", M * 128, "bfloat16")
-many("f_a f_d f_e", 2 * HJ, "float32")
+sb("FAR5", 128, "bfloat16")
+many("f_e f_g", 2 * HJ, "float32")
 sb("NXH", 2 * HJ, "float16")
 many("NXW NX2", W, "float32")
 sb("CM", 512, "float16")
@@ -58,44 +59,49 @@ sb("AL", 8, "uint16")
 many("plc live pl8 T2 T2a T2L", 8, "float32")
 sb("ASK", ND * Q, "bfloat16")
 sb("FIL", ND * Q * F, "bfloat16")
-sb("QREP", 12 * ND * Q, "bfloat16")
-sb("G", 640, "bfloat16")
+sb("QREP", 16 * ND * Q, "bfloat16")
+sb("G", 960, "bfloat16")
 sb("VS", 80, "float32")
-many("q_vi q_va q_vs q_vb q_ki q_km q_kc q_kd", 8, "int32")
-many("q_c0 q_v2 q_KM q_kt q_kf", 8, "float32")
+many("q_vi q_v q_ki q_km q_kc q_kd", 16, "int32")
+many("q_f q_v2 q_KM q_kt", 16, "float32")
 many("qraw qmsk", P * ND, "int32")
 sb("qlst", P * ND, "uint16")
-many("FL SLu", 32, "uint16")
+many("SD SC k_RZ", 2 * ND * F, "float32")
+sb("k_ONF", 128, "float32")
+sb("FS", 2 * ND * F, "uint16")
 sb("an", 8, "bfloat16")
 many("a8 alo", 8, "int32")
-many("am alf", 8, "float32")
+sb("alf", 8, "float32")
 sb("ONB", M * 128, "bfloat16")
-many("k_TMP k_BLK k_IDN k_LST1 k_LSTI k_LST6 k_BLK6 k_NEGI k_N8I k_IP1 k_IARRt k_IARR k_IB k_MQ", 128, "bfloat16")
-many("k_Z k_WZ k_J16", 144, "bfloat16")
+many("k_TMP k_BLK k_IDN k_ID2 k_LST1 k_LSTI k_LST6 k_BLK6 k_NEGI k_N8I k_IP1 k_IARRt k_IARR k_IBt k_IB k_MQ k_J16 k_ZR", 128, "bfloat16")
+many("k_Z k_WZ", 144, "bfloat16")
+many("k_J16f k_J16h", 144, "float32")
 many("k_B1 k_B2 k_BN", 8, "bfloat16")
 many("k_NP1 k_NARRt k_NARR", 640, "bfloat16")
 sb("k_MROWf", P * ND, "float32")
 sb("k_MROW", P * ND, "bfloat16")
-sb("k_ZR", 16, "bfloat16")
-many("k_MC k_FB", P, "float32")
-many("k_MKi k_MKa k_PWi k_PW", 128, "int32")
-many("k_MK k_MK1 k_MKb k_ONF k_DG k_T1F", 128, "float32")
-many("k_p k_p2 TH k_th k_tl", 8, "int32")
-many("k_I16 k_I128 k_LB k_T k_B k_BQ k_JKb k_JK k_FC WTf", 8, "float32")
+sb("k_MC", P, "float32")
+many("k_MKi k_MKa", 128, "int32")
+many("k_MK k_MK1 k_MKb k_DG k_T1F k_PWi k_PW", 128, "float32")
+many("k_p k_p2 TH", 8, "int32")
+many("k_I16 k_I6 k_IPL k_I128 k_IB1 k_PWl k_LB k_T k_B k_BQ k_JKb k_JK k_FB", 8, "float32")
 sb("k_L0", 8, "uint16")
-many("k_CW k_CWa k_CWb k_GW WT", 8, "bfloat16")
+many("k_CW k_GW WT", 8, "bfloat16")
 for _k in range(8):
     SB["ps%d" % _k] = ("psum", [128, 512], "float32")
 for _d in ARENA:
     SB[ARENA[_d][0]] = ("sbuf", [128, ARENA[_d][1]], _d)
 SCRATCH = SB
-NA = 10
-SEMAPHORES = ["sV", "sS", "sT", "sG", "lsem", "dx0", "dx1", "dwt", "dth", "dy0", "dy1", "o0", "o1", "h0", "h1"] + ["ga%d" % _k for _k in range(NA * RO)]
+SEMAPHORES = ["sV", "sS", "sT", "sG", "lsem", "dx0", "dx1", "dxi", "dwt", "dth", "dy0", "dy1", "o0", "o1", "h0", "h1"] + ["ga%d" % _k for _k in range(M * RO)]
 
 PLAN = [tuple(int(c) if c.isdigit() else c for c in x.split(".")) for x in (
-    "la.0.0.3 sg.0.0 la.1.0.3 sg.0.1 vg.1.0 sg.2.0 vg.1.1 sg.2.1 c.1 lb.0.3.6 lb.1.3.6 sg.3.0 sg.3.1 sg.4.0 rl.1.0 rl.1.1 tp.1 c.2 "
-    "rl.0.0 rl.0.1 tp.0 vg.4.1 far.1 rl.2.0 rl.2.1 tp.2 vg.5.0 far.0 ab.4.1 ab.3.0 ab.3.1 t1.3 vg.5.1 far.2 ab.4.0 t1.4 far.3 far.4 "
-    "ab.5.0 ab.5.1 count d5.0 before d5.1 succ.0 win.0 succ.1 win.1 wc.0 wc.1").split()]
+    "l0 sg.0.0 sg.0.1 l1 sg.2.0 vg.1.0 sg.2.1 vg.1.1 sg.4.0 vg.3.0 td.1 sg.4.1 once td.0 vg.3.1 ab.3.0 rl.1.0 ab.3.1 vg.5.0 td.2 ab.2.1 "
+    "rl.1.1 tr.3 ab.5.0 rl.0.0 tr.1 rl.2.0 ab.4.0 rl.0.1 tr.2 vg.5.1 ab.4.1 tr.0 far.3 ab.5.1 n5 tr.4 far.1 far.2 n6 far.0 tr.5 far.4 "
+    "count far.5 succ").split()]
+TWO = [s[1] for s in PLAN if s[0] == "td"]
+CUT = 68
+PARTS = (60, 60, 40)
+XCUT = 64
 
 
 def helpers(topo, cores, core):
@@ -256,7 +262,7 @@ def rank_program(g, core, T, topo):
         do("V", lambda: g.vector.tensor_tensor_scan(ap(out), ap(d0), ap(d1), 0.0, op0, op1), [d0, d1], [out])
 
     def act(out, in_, func=Fn.Copy, scale=1.0, bias=0.0):
-        do("S", lambda: g.scalar.activation(ap(out), ap(in_), func, bias=bias, scale=val(scale)), [in_] + ([scale] if is_ap(scale) else []), [out])
+        do("S", lambda: g.scalar.activation(ap(out), ap(in_), func, bias=val(bias), scale=val(scale)), [x for x in (in_, scale, bias) if is_ap(x)], [out])
 
     def mm(out, l, r, start, stop):
         do("T", lambda: g.tensor.matmul(ap(out), ap(l), ap(r), start, stop), [l, r], [out])
@@ -290,99 +296,98 @@ def rank_program(g, core, T, topo):
     K = lambda n, c0=0, c1=None, step=1: A("k_" + n, c0, c1, step)
     ON = A("ONB", 0, 128)
     ps = lambda k, c0, c1, step=1: A("ps%d" % k, c0, c1, step)
+    col = lambda n: K(n, 0, 1)
     ms(ON, 1.0)
     asel(K("TMP"), ON, [[-16, 8], [0, 16]], Op.is_ge, 0, 1)
     asel(K("BLK"), K("TMP"), [[16, 8], [0, 16]], Op.is_ge, 15, -1)
     iota(K("MKi"), [[-1, 128]], 128, 1)
-    iota(K("p", 0, 1), [[0, 1]], 0, 1)
+    iota(col("p"), [[0, 1]], 0, 1)
     asel(K("IDN"), ON, [[-1, 128]], Op.is_equal, 0, 1)
-    iota(K("PWi"), [[16, 128]], 1, 0)
+    iota(K("PWi"), [[16, 128]], 1, 0, True)
     iota(K("LB"), [[16, 8]], 0, 0, True)
-    ms(K("Z"), 0.0)
-    ms(K("WZ"), 0.0)
+    dma("Y", T.XI[:, :], T.x0[:, :], "dxi", [], [A("XI")])
+    span = lambda a, b: (a[0], a[1], b[2], 1)
+    ms(span(K("ZR"), K("WZ")), 0.0)
     ms(A("ONB", 128), 1.0)
+    ms(span(A("SC"), K("ONF")), 1.0)
     ms(A("FAR", 0, None, M), 0.0)
-    ms(K("ONF"), 1.0)
+    ms(K("RZ", 0, None, F), 0.0)
     B8 = K("BLK", 0, 128, 16)
     act(K("Z", 15, 143, 16), B8)
     act(K("B1"), B8)
     act(K("B2"), B8, scale=2.0)
     act(K("BN"), B8, scale=-1.0)
     ts(K("MKa"), K("MKi"), 15, Op.bitwise_and)
+    ts(col("p2"), col("p"), 15, Op.bitwise_and)
     ts(K("MK"), K("MKa"), 0, Op.is_equal)
-    for i in range(16):
-        act(A("BIh", 128 * i, 128 * i + 128), K("BLK"), scale=K("MK", i, i + 1))
+    cp(col("I16"), col("p2"))
     ts(K("WZ", 15, 143, 16), B8, A("WT", 0, 1), Op.mult)
-    ts(A("XA", W + 16, SL), K("BLK"), A("WT", 0, 1), Op.mult)
     cp(K("T", 0, 2), A("TH", 0, 2))
-    ts(K("th", 0, 1), A("TH", 1, 2), 6, Op.arith_shift_right)
-    ts(K("tl", 0, 1), A("TH", 1, 2), 63, Op.bitwise_and)
-    ts(K("p2", 0, 1), K("p", 0, 1), 15, Op.bitwise_and)
-    cp(A("XA", W + WRAP, W + WRAP + 1), K("th", 0, 1))
-    cp(A("XA", W + WRAP + 1, W + WRAP + 2), K("tl", 0, 1))
-    cp(K("I16", 0, 1), K("p2", 0, 1))
-    ts(K("DG"), K("IDN"), K("T", 0, 1), Op.mult)
+    ts(A("XA", W + 16, SL), K("BLK"), A("WT", 0, 1), Op.mult)
+    hi, lo = A("XA", W + WRAP, W + WRAP + 1), A("XA", W + WRAP + 1, W + WRAP + 2)
+    act(col("B"), K("MK", 15, 16), scale=-BIG, bias=BIG)
+    act(col("I128"), col("I16"), scale=128.0)
+    act(hi, K("T", 1, 2))
+    act(col("PWl"), col("I16"), bias=W - 15.0)
+    act(lo, hi, Fn.Identity, scale=-1.0, bias=K("T", 1, 2))
+    act(K("DG"), K("IDN"), scale=col("T"))
+    act(col("IB1"), col("B"), Fn.Identity, scale=-1.0, bias=col("I128"))
+    act(K("PW", 0, 127), K("PWi", 0, 127), Fn.Identity, bias=col("I16"))
+    act(K("PW", 127, 128), K("MK", 15, 16), Fn.Identity, scale=-float(W), bias=col("PWl"))
+    act(K("L0h"), K("LB"), Fn.Identity, bias=col("IB1"))
+    cp(A("XA", W, W + WRAP), A("XA", 0, WRAP))
+    ts(K("MK1"), K("MKa"), 15, Op.is_equal, -BIG, Op.mult)
+    ts(K("MKb"), K("MK"), 2 * BIG, Op.mult)
+    for i in range(16):
+        a = A("BIh", 128 * i, 128 * i + 128)
+        if i < 6:
+            ts(a, K("BLK"), K("MK", i, i + 1), Op.mult)
+        else:
+            act(a, K("BLK"), scale=K("MK", i, i + 1))
+    tt(K("MS"), K("MK1"), K("MKb"), Op.add)
+    ts(K("L0"), K("LB"), col("I128"), Op.add)
 
-    def consts_1():
-        mm(ps(3, 0, 128), K("ONF"), K("DG"), True, True)
-        cp(K("T1F"), ps(3, 0, 128))
+    def diag(out, c):
+        asel(out, K("ZR"), [[-1, 128]], Op.not_equal, 0, 1, c)
 
-    def consts_g(k):
-        if k == 0:
-            iota(K("NP1"), [[16, ND], [0, 8], [1, 16]], 1, 0, True)
-        if k == 1:
-            asel(K("NARRt"), K("NP1"), [[0, ND], [-16, 8], [0, 16]], Op.is_ge, 0, 1)
-        if k == 2:
-            asel(K("NARR"), K("NARRt"), [[0, ND], [16, 8], [0, 16]], Op.is_ge, 15, -1)
-        if k == 3:
-            asel(K("LST1"), K("BLK"), [[1, 128]], Op.is_ge, -1, -1)
-            asel(K("LSTI"), K("BLK"), [[1, 128]], Op.is_ge, 0, -1)
-            iota(K("J16"), [[16, 144]], 0, 0, True)
-        if k == 4:
-            iota(K("IP1"), [[0, 8], [1, 16]], 1, 0, True)
-            asel(K("IARRt"), K("IP1"), [[-16, 8], [0, 16]], Op.is_ge, 0, 1)
-            asel(K("IARR"), K("IARRt"), [[16, 8], [0, 16]], Op.is_ge, 15, -1)
-        if k == 5:
-            asel(K("IARRt"), K("IP1"), [[-16, 8], [0, 16]], Op.is_ge, 0, 1, 99.0)
-            asel(K("IB"), K("IARRt"), [[16, 8], [0, 16]], Op.is_ge, 15, -1, 99.0)
-            iota(K("MC"), [[1, P]], 0, 0, True)
-        if k == 6:
-            iota(K("MROWf"), [[1, P], [0, ND]], 0, 0, True)
-            iota(K("JKb", 0, ND), [[16 * F, ND]], 2560, 0, True)
-            iota(K("FB", 0, ND * F), [[SL, ND], [1, F]], 1, 0, True)
-            iota(K("FC", 0, F), [[1, F]], 0, 0, True)
+    def consts_g():
+        diag(K("ID2"), 2.0)
+        diag(K("IDh"), 1.0)
+        diag(K("NIh"), -1.0)
+        asel(K("ONh"), A("ONB", 0, 8), [[0, 8]], Op.is_ge, 0, 0)
+        iota(K("NP1"), [[16, ND], [0, 8], [1, 16]], 1, 0, True)
+        asel(K("NARRt"), K("NP1"), [[0, ND], [-16, 8], [0, 16]], Op.is_ge, 0, 1)
+        asel(K("NARR"), K("NARRt"), [[0, ND], [16, 8], [0, 16]], Op.is_ge, 15, -1)
+        asel(K("LST1"), K("BLK"), [[1, 128]], Op.is_ge, -1, -1)
+        asel(K("LSTI"), K("BLK"), [[1, 128]], Op.is_ge, 0, -1)
+        iota(K("J16f"), [[16, 144]], 0, 0, True)
+        iota(K("MROWf"), [[1, P], [0, ND]], 0, 0, True)
+        iota(K("JKb", 0, ND), [[16 * F, ND]], 2560, 0, True)
+        iota(K("MC"), [[2, P]], 1, 0, True)
+        iota(K("FB", 0, ND), [[SL, ND]], 1, 0, True)
+        diag(K("NEGI"), -1.0)
+        diag(K("N8I"), -8192.0)
+        iota(K("IP1"), [[0, 8], [1, 16]], 1, 0, True)
+        asel(K("IARRt"), K("IP1"), [[-16, 8], [0, 16]], Op.is_ge, 0, 1)
+        asel(K("IBt"), K("IP1"), [[-16, 8], [0, 16]], Op.is_ge, 0, 1, 99.0)
+        asel(K("IARR"), K("IARRt"), [[16, 8], [0, 16]], Op.is_ge, 15, -1)
+        asel(K("IB"), K("IBt"), [[16, 8], [0, 16]], Op.is_ge, 15, -1, 99.0)
 
-    def consts_2():
-        ts(K("PW"), K("PWi"), K("I16", 0, 1), Op.add)
-        ts(K("PW"), K("PW"), W - 1, Op.bitwise_and)
-        ts(K("MK1"), K("MKa"), 15, Op.is_equal, -BIG, Op.mult)
-        ts(K("MKb"), K("MK"), 2 * BIG, Op.mult)
-        tt(K("MS"), K("MK1"), K("MKb"), Op.add)
-        ts(K("MQ"), K("MS"), 1024.0, Op.mult)
-        ts(K("B", 0, 1), K("I16", 0, 1), 15.0, Op.is_lt, BIG, Op.mult)
-        ts(K("BQ", 0, 1), K("B", 0, 1), 1024.0, Op.mult)
-        ts(K("I128", 0, 1), K("I16", 0, 1), 128.0, Op.mult)
-        ts(K("L0"), K("LB"), K("I128", 0, 1), Op.add)
-        ts(K("L0h"), K("LB"), K("I128", 0, 1), Op.add, K("B", 0, 1), Op.subtract)
-        cp(K("IDh"), K("IDN"))
-        ts(K("NIh"), K("IDN"), -1.0, Op.mult)
-        cp(K("ONh"), A("ONB", 0, 8))
-
-    def consts_3():
-        act(K("MROW"), K("MROWf"), scale=1.0 / P)
-        act(K("LST6"), K("LST1"), scale=6.0)
-        act(K("BLK6"), K("BLK"), scale=6.0)
-        act(K("N8I"), K("IDN"), scale=-8192.0)
-        act(K("NEGI"), K("IDN"), scale=-1.0)
-        act(K("ZR"), A("ONB", 0, 16), scale=0.0)
-        act(K("CW", 0, 1), A("ONB", 0, 1), scale=16.0)
-        act(K("CW", 1, 2), A("ONB", 0, 1))
-        act(K("GW", 0, 1), A("ONB", 0, 1))
-        act(K("GW", 1, 2), A("ONB", 0, 1), scale=128.0)
-
-    def consts_4():
-        ts(K("JKb", ND, ND + 1), K("I16", 0, 1), float(F), Op.mult)
-        ts(K("JK", 0, ND), K("JKb", 0, ND), K("JKb", ND, ND + 1), Op.add)
+    consts_s = [
+        lambda: act(K("MQ"), K("MS"), scale=1024.0),
+        lambda: act(col("BQ"), col("B"), scale=1024.0),
+        lambda: act(col("I6"), col("I16"), scale=float(F)),
+        lambda: act(col("IPL"), col("I16"), bias=-3.0 * ND * Q),
+        lambda: act(K("LST6"), K("LST1"), scale=6.0),
+        lambda: act(K("BLK6"), K("BLK"), scale=6.0),
+        lambda: act(K("J16"), K("J16f", 0, 128)),
+        lambda: act(K("J16h"), K("J16f"), bias=-0.5),
+        lambda: act(K("MROW"), K("MROWf"), scale=1.0 / P),
+        lambda: act(K("JK", 0, ND), K("JKb", 0, ND), Fn.Identity, bias=col("I6")),
+        lambda: act(K("CW", 0, 1), A("ONB", 0, 1), scale=16.0),
+        lambda: act(K("CW", 1, 2), A("ONB", 0, 1)),
+        lambda: act(K("GW", 0, 1), A("ONB", 0, 1)),
+        lambda: act(K("GW", 1, 2), A("ONB", 0, 1), scale=128.0)]
 
     hs = helpers(topo, cores, core)
     tot, na = [0], [0]
@@ -393,166 +398,153 @@ def rank_program(g, core, T, topo):
         for h in range(2):
             for i in range(16):
                 mm(ps(h, 0, HJ), K("WZ", 15 - i, 143 - i), A(X, H * h + i, H * h + H, 16), i == 0, i == 15)
-        n = WRAP if r == 0 else 16
-        act(A(X, W, W + n), A(X, 0, n))
-        for h in range(2):
-            act(A("XI", H * h, H * h + H), A(X, H * h, H * h + H))
+        if r:
+            cp(A(X, W, W + 16), A(X, 0, 16))
+        if r == 0:
+            mm(ps(2, 0, 128), K("ONF"), K("DG"), True, True)
+            act(K("T1F"), ps(2, 0, 128))
+        else:
+            act(A("XI"), A(X, 0, W))
         n = SENT[r] // NP
-        need("G", [A(X, 0, SENT[r])], [])
-        trs = []
-        for k in range(NP):
-            rid, pid = topo.addr(hs[k], core)
-            es = topo.engines(core, hs[k])
-            e = len(es) // NP
-            trs.append(RemoteDMATransfer(dst_ids=[DstId(rid=rid, pnc=pid)], dma_engine_mask=sum(1 << x for x in es[e * k:e * k + e]),
-                                         remote_sem=T.sem["h%d" % r], src=T[X][:, n * k:n * k + n], dst=T[OTH][:, n * k:n * k + n]))
-            tot[0] += e
-        g.remote_dma_fused(trs, local_sem=T.sem.lsem)
+        for ks in ([0], range(1, NP)) if r == 0 else (range(NP),):
+            trs = []
+            for k in ks:
+                need("G", [A(X, n * k, n * k + n)], [])
+                rid, pid = topo.addr(hs[k], core)
+                es = topo.engines(core, hs[k])
+                e = len(es) // NP
+                trs.append(RemoteDMATransfer(dst_ids=[DstId(rid=rid, pnc=pid)], dma_engine_mask=sum(1 << x for x in es[e * k:e * k + e]),
+                                             remote_sem=T.sem["h%d" % r], src=T[X][:, n * k:n * k + n], dst=T[OTH][:, n * k:n * k + n]))
+                tot[0] += e
+            g.remote_dma_fused(trs, local_sem=T.sem.lsem)
 
-        def lists(h, m0, m1):
-            o, e = HJ * h, HJ * h + HJ
-            ui, ua, us = [A("i_" + n, o, e) for n in ("ui", "ua", "us")]
-            u2, bb = ps(6 + h, 128, 128 + HJ), ps(6 + h, 256, 256 + HJ)
-            R = lambda m: A("raw", M * HJ * h + HJ * m, M * HJ * h + HJ * m + HJ)
-            al = lambda n: A(n, M * HJ * h + HJ * m0, M * HJ * h + HJ * m1)
-            if m0 == 0:
-                cp(ui, ps(h, 0, HJ))
-                ts(ua, ui, W - 1, Op.bitwise_and)
-                ts(us, ui, W - 1, Op.bitwise_and, 5, Op.arith_shift_right)
-                tt(bb, ua, us, Op.mult)
-                ts(u2, ua, 2, Op.mult)
-                tt(R(0), bb, ua, Op.add)
-            for m in range(max(m0, 1), m1):
-                tt(R(m), u2, R(m - 1), Op.add)
-            ts(al("msk"), al("raw"), W - 1, Op.bitwise_and)
-            cp(al("lst"), al("msk"))
-            if m1 == M:
-                ts(A("i_r1", o, e), R(0), 1, Op.add)
-                ts(A("i_u2", o, e), ua, 2, Op.mult)
+        I = lambda n, h=None: A("i_" + n) if h is None else A("i_" + n, HJ * h, HJ * h + HJ)
+        u2 = ps(7, 0, 128)
+        bb = lambda h: ps(7, 128 + HJ * h, 128 + HJ * h + HJ)
+        lk = lambda n, m, h: A(n, 128 * m + HJ * h, 128 * m + HJ * h + HJ)
+        lks = lambda n, m0, m1: A(n, 128 * m0, 128 * m1)
+        more = lambda m: tt(lks("raw", m, m + 1), u2, lks("raw", m - 1, m), Op.add)
+        low = lambda a, b: ts(a, b, W - 1, Op.bitwise_and)
 
-        def lk(m, h):
-            return A("lst", M * HJ * h + HJ * m, M * HJ * h + HJ * m + HJ)
+        def first_look(h):
+            return [lambda: cp(I("ui", h), ps(h, 0, HJ)),
+                    lambda: low(I("ua", h), I("ui", h)),
+                    lambda: ts(I("us", h), I("ui", h), W - 1, Op.bitwise_and, 5, Op.arith_shift_right),
+                    lambda: tt(bb(h), I("ua", h), I("us", h), Op.mult),
+                    lambda: tt(lk("raw", 0, h), bb(h), I("ua", h), Op.add),
+                    lambda: low(lk("msk", 0, h), lk("raw", 0, h)),
+                    lambda: cp(lk("lst", 0, h), lk("msk", 0, h))]
+
+        def lists0():
+            a, b = first_look(0), first_look(1)
+            for f in a[:5] + [b[0], a[5], b[1], a[6], b[2], lambda: ts(u2, I("ua"), 2, Op.mult), b[3], b[4], lambda: more(1), b[5],
+                              lambda: more(2), b[6], lambda: low(lks("msk", 1, 3), lks("raw", 1, 3)), lambda: more(3),
+                              lambda: cp(lks("lst", 1, 3), lks("msk", 1, 3))]:
+                f()
+
+        def lists1():
+            more(4)
+            ts(I("r1"), lks("raw", 0, 1), 1, Op.add)
+            more(5)
+            low(lks("msk", 3, M), lks("raw", 3, M))
+            ts(I("n5"), lks("raw", 5, M), 1, Op.add)
+            cp(lks("lst", 3, M), lks("msk", 3, M))
 
         U = lambda n, m, h: A(n, W * m + H * h, W * m + H * h + H)
+        dist = lambda m, i=None: ps(1 + m, 0, 128) if i is None else ps(1 + m, i, 128, 16)
 
         def sgath(m, h):
             a, b = U("D", m, h), A(X, H * h, H * h + H)
-            sgather(a, A(X, 0, W), lk(m, h), scale=-1.0)
+            sgather(a, A(X, 0, W), lk("lst", m, h), scale=-1.0)
             dma("G", ap(a), ap(b), "ga%d" % na[0], [b], [a], accum_op=Op.add)
-            if r == 0:
-                consts_g(na[0])
             na[0] += 1
 
         def vgath(m, h):
-            vgather(U("D", m, h), A(X, 0, W), lk(m, h), A("XI", H * h, H * h + H), Op.subtract)
+            vgather(U("D", m, h), A(X, 0, W), lk("lst", m, h), A("XI", H * h, H * h + H), Op.subtract)
 
         def relu(m, h):
             ts(U("RL", m, h), U("D", m, h), 0.0, Op.max)
 
         def size(m, h):
-            act(U("RL", m, h), U("D", m, h), Fn.Abs)
+            act(U("RL", m, h), U("D", m, h), Fn.Relu if m in TWO else Fn.Abs)
 
-        def tpass(m, both=True):
+        def tdiff(m):
+            mm(dist(m), K("IDN"), K("ZR"), True, False)
             for i in range(16):
-                out = ps(2 + m % 2, 128 * (m // 2) + i, 128 * (m // 2) + 128, 16)
-                if both:
-                    mm(out, A("D", W * m + i, W * m + W, 16), K("BN"), True, False)
-                mm(out, A("RL", W * m + i, W * m + W, 16), K("B2") if both else K("B1"), not both, True)
+                mm(dist(m, i), A("D", W * m + i, W * m + W, 16), K("BN"), False, False)
+
+        def tsize(m):
+            two = m in TWO
+            for i in range(16):
+                mm(dist(m, i), A("RL", W * m + i, W * m + W, 16), K("B2") if two else K("B1"), not two, not two or i == 15)
 
         def far(m):
-            tt(A("FAR", M - 1 - m, None, M), ps(2 + m % 2, 128 * (m // 2), 128 * (m // 2) + 128), K("T1F"), Op.is_ge)
+            tt(A("FAR", M - 1 - m, None, M) if m < M - 1 else A("FAR5"), dist(m), K("T1F"), Op.is_ge)
 
         def count():
             scan(A("CNT"), A("ONB"), A("FAR"), Op.add, Op.mult)
-            mm(ps(3, 256, 384), A("CNT", M - 1, None, M), K("IDN"), True, True)
+            mm(ps(7, 0, 128), A("CNT", M - 1, None, M), K("ID2"), True, True)
 
-        def before_last():
-            c, ft, fd = ps(3, 256, 384), ps(2, 128, 256), ps(2, 256, 384)
-            tt(ft, c, A("i_u2"), Op.mult)
-            ts(A("f_a"), c, float(M - 1), Op.is_ge)
-            tt(A("i_r2"), ft, A("i_r1"), Op.add)
-            ts(A("i_fr"), A("i_r2"), W - 1, Op.bitwise_and)
-            tt(fd, K("PW"), A("i_fr"), Op.subtract)
-            tt(A("f_e"), fd, A("f_a"), Op.mult)
-
-        def dist5(h):
-            o = W * (M - 1) + H * h
+        def succ():
+            c, ft, fa, y = [ps(7, 128 * k, 128 * k + 128) for k in range(4)]
+            mm(ps(0, 0, 128), A("FAR5"), K("IDN"), True, True)
+            tt(ft, c, I("ua"), Op.mult)
+            ts(fa, c, 2.0 * (M - 1), Op.is_ge)
+            tt(I("r2"), ft, I("r1"), Op.add)
+            tt(A("f_g"), fa, A("f_e"), Op.mult)
+            low(I("fr"), I("r2"))
+            tt(y, ps(0, 0, 128), A("f_g"), Op.mult)
+            tt(A("NXH"), y, I("fr"), Op.add)
+            at = lambda i: ps(i // 2, 128 * (i % 2), 128 * (i % 2) + 128)
             for i in range(16):
-                mm(ps(h, 0, HJ), K("Z", 15 - i, 143 - i), A("RL", o + i, o + H, 16), i == 0, i == 15)
-
-        def succ(h):
-            s, e = HJ * h, HJ * h + HJ
-            ft, fd = ps(2, 128, 128 + HJ), ps(2, 256, 256 + HJ)
-            ts(ft, ps(h, 0, HJ), K("T", 0, 1), Op.is_ge)
-            tt(fd, ft, A("f_e", s, e), Op.mult)
-            tt(A("NXH", s, e), fd, A("i_fr", s, e), Op.add)
-            cp(A("NXU", s, e), A("NXH", s, e))
-
-        def window(h):
+                mm(at(i), A("BIh", 128 * i, 128 * i + 128), A("NXH"), True, True)
+            cp(A("NXU"), A("NXH"))
             for i in range(16):
-                mm(wat(h, i), A("BIh", 128 * i, 128 * i + 128), A("NXH", HJ * h, HJ * h + HJ), True, True)
+                (cp if (i // 2) % 2 else act)(A("NXW", i, W, 16), at(i))
 
-        def wat(h, i):
-            if h == 0:
-                return ps(4 + i // 8, HJ * (i % 8), HJ * (i % 8) + HJ)
-            return ps((6, 7, 0, 3)[i // 4], HJ * (i % 4), HJ * (i % 4) + HJ)
-
-        def wcopy(h):
-            for i in range(16):
-                (cp if (i // (4 if h else 8)) % 2 else act)(A("NXW", H * h + i, H * h + H, 16), wat(h, i))
-
-        def once(k):
-            if r == 0:
-                (consts_1, consts_2)[k - 1]()
-
-        calls = {"sg": sgath, "vg": vgath, "rl": relu, "ab": size, "tp": tpass, "t1": lambda m: tpass(m, False), "far": far, "count": count,
-                 "before": before_last, "d5": dist5, "succ": succ, "win": window, "wc": wcopy, "la": lists, "lb": lists, "c": once}
+        calls = {"sg": sgath, "vg": vgath, "rl": relu, "ab": size, "td": tdiff, "tr": tsize, "far": far, "count": count, "succ": succ,
+                 "l0": lists0, "l1": lists1, "n5": lambda: low(I("n6"), I("n5")), "n6": lambda: tt(A("f_e"), K("PW"), I("n6"), Op.subtract),
+                 "once": consts_g if r == 0 else (lambda: None)}
         for step in PLAN:
             calls[step[0]](*step[1:])
-
-        def pick(k):
-            o = 128 * (k % 4)
-            scan(A("CS", 128 * k, 128 * k + 128), K("MS"), A("CM", o, o + 128), Op.add, Op.min)
 
         now = lambda k: A("CS", 128 * k + 15, 128 * k + 128, 16) if k else K("L0h")
         lc = lambda k: A("LC", 8 * k, 8 * k + 8) if k else K("L0")
         cm = lambda k: A("CM", 128 * (k % 4), 128 * (k % 4) + 128)
+        pick = lambda k: scan(A("CS", 128 * k, 128 * k + 128), K("MS"), cm(k), Op.add, Op.min)
+        relist = lambda k: ts(lc(k), now(k), col("B"), Op.add)
 
         def settle(k):
-            ts(lc(k), now(k), K("B", 0, 1), Op.add)
             mm(ps(7, k - 1, 128, 16), K("NIh"), now(k - 1), True, False)
-            mm(ps(7, k - 1, 128, 16), K("IDh"), now(k), False, True)
             mm(ps(3, k, 128, 16), K("IDh"), now(k), True, True)
+            mm(ps(7, k - 1, 128, 16), K("IDh"), now(k), False, True)
 
         mm(ps(7, 15, 128, 16), K("IDh"), K("ONh"), True, True)
         mm(ps(3, 0, 128, 16), K("IDh"), K("L0h"), True, True)
-        cut = 68
         sgather(cm(1), A("NXW"), lc(0))
-        vgather(A("NX2", 0, 16 * cut), A("NXW"), A("NXU", 0, cut))
-        sgather(A("NX2", 16 * cut, W), A("NXW"), A("NXU", cut, 128))
+        vgather(A("NX2", 0, 16 * CUT), A("NXW"), A("NXU", 0, CUT))
+        sgather(A("NX2", 16 * CUT, W), A("NXW"), A("NXU", CUT, 128))
         pick(1)
+        relist(1)
         settle(1)
-        if r == 0:
-            consts_4()
         for k in range(2, L, 2):
             sgather(cm(k + 1), A("NX2"), lc(k - 1))
             vgather(cm(k), A("NX2"), lc(k - 2))
+            if r == 0:
+                for f in consts_s[k - 2:k]:
+                    f()
             pick(k)
-            settle(k)
             pick(k + 1)
-            if k + 1 < L - 1:
-                settle(k + 1)
-        k = L - 1
-        mm(ps(7, k - 1, 128, 16), K("NIh"), now(k - 1), True, False)
-        mm(ps(7, k - 1, 128, 16), K("IDh"), now(k), False, True)
-        mm(ps(3, k, 128, 16), K("IDh"), now(k), True, True)
-        if r == 0:
-            consts_3()
+            if k + 2 < L:
+                relist(k)
+                relist(k + 1)
+            settle(k)
+            settle(k + 1)
 
+        ts(A("LF"), ps(3, 0, 128), col("B"), Op.add)
         ts(A("JA"), ps(7, 0, 128), 1.0, Op.not_equal, -1.0, Op.add)
         ts(A("JB"), ps(7, 0, 128), 1.0 - W, Op.not_equal)
         scan(A("INC"), A("JA"), A("JB"), Op.add, Op.add)
-        ts(A("LF"), ps(3, 0, 128), K("B", 0, 1), Op.add)
         sgather(A("Xst"), A(X, 0, W), A("LF"))
         mm(ps(2, 0, 2 * ND), K("IDN"), K("ZR", 0, 2 * ND), True, False)
         mm(ps(6, 0, 1), K("LST1"), A("INC", 127, 128), True, True)
@@ -570,6 +562,7 @@ def rank_program(g, core, T, topo):
             for d in range(ND):
                 mm(ps(2, 2 * d, 2 * d + 2), A(s, 128 * d, 128 * d + 128), K(w, 0, 2), False, s == "CC" and d == ND - 1)
         ts(A("AL", 0, ND), ps(2, 0, 2 * ND, 2), -1.0, Op.add, W - 1.0, Op.min)
+        ts(A("plc", 0, ND), ps(2, 1, 2 * ND, 2), -128.0, Op.add)
         vgather(A("ASK"), A("Xst"), A("AL", 0, ND))
         for i in range(16):
             asel(A("Xnat", 128 * i, 128 * i + 128), A("Xst", i, W, 16), [[0, 128]], Op.is_ge, 0, 0)
@@ -579,52 +572,52 @@ def rank_program(g, core, T, topo):
             mm(ps(3, Q * d, Q * d + Q), A("OTH0", SL * d + W + 16, SL * d + SL), A("ASK", Q * d, Q * d + Q), True, True)
         act(A("QREP", 0, 80), A("ASK"))
         act(A("QREP", 80, 160), A("ASK"))
-        act(A("QREP", 160, 320), A("QREP", 0, 160))
-        act(A("QREP", 320, 640), A("QREP", 0, 320))
-        act(A("QREP", 640, 960), A("QREP", 0, 320))
-        ts(A("plc", 0, ND), ps(2, 1, 2 * ND, 2), -128.0, Op.add)
-        scan(A("VS"), K("MQ", 0, 80), ps(3, 0, 80), Op.add, Op.min)
+        n, top = 160, 16 * max(PARTS)
+        while n < top:
+            act(A("QREP", n, min(2 * n, top)), A("QREP", 0, min(n, top - n)))
+            n *= 2
         q = lambda n: A("q_" + n, 0, ND)
-        ts(q("vi"), A("VS", 15, 80, 16), K("BQ", 0, 1), Op.add)
         ts(A("live", 0, ND), A("plc", 0, ND), float(W), Op.is_lt)
-        ts(q("va"), q("vi"), W - 1, Op.bitwise_and)
-        ts(q("vs"), q("vi"), W - 1, Op.bitwise_and, 5, Op.arith_shift_right)
-        ts(q("v2"), q("va"), 2, Op.mult)
-        tt(q("vb"), q("va"), q("vs"), Op.mult)
         ts(A("pl8", 0, ND), A("plc", 0, ND), 8193.0, Op.add)
-        tt(q("c0"), q("vb"), q("va"), Op.add)
+        if r == 0:
+            tt(A("T2", 0, ND), A("OTH0", W + WRAP, None, SL), A("OTH0", W + WRAP + 1, None, SL), Op.add)
+        scan(A("VS"), K("MQ", 0, 80), ps(3, 0, 80), Op.add, Op.min)
+        ts(q("vi"), A("VS", 15, 80, 16), col("BQ"), Op.add)
+        tt(A("T2L", 0, ND), A("T2", 0, ND), A("live", 0, ND), Op.mult)
+        va, vs = A("q_v", 0, ND), A("q_v", ND, 2 * ND)
+        low(va, q("vi"))
+        ts(vs, q("vi"), W - 1, Op.bitwise_and, 5, Op.arith_shift_right)
+        cp(A("q_f", 0, 2 * ND), A("q_v", 0, 2 * ND))
         for d in range(ND):
-            ts(A("qraw", d, P * ND, ND), K("MC"), A("q_v2", d, d + 1), Op.mult, A("q_c0", d, d + 1), Op.add)
-        for d in range(ND):
-            ts(A("qmsk", d, P * ND, ND), A("qraw", d, P * ND, ND), W - 1, Op.bitwise_and)
+            ts(A("qraw", d, P * ND, ND), K("MC"), A("q_f", ND + d, ND + d + 1), Op.add, A("q_f", d, d + 1), Op.mult)
+        low(A("qmsk"), A("qraw"))
         for d in range(ND):
             ts(A("qlst", d, P * ND, ND), A("qmsk", d, P * ND, ND), float(SL * d), Op.add)
-        mm(ps(6, 0, 128), K("IDN"), K("J16", 0, 128), True, False)
-        parts = [(0, 60), (60, 120), (120, 160)]
-        sgather(A("G"), A(OTH), A("qlst", 120, 160))
+        mm(ps(6, 0, 128), K("IDN"), K("J16"), True, False)
+        edge = [0, PARTS[0], PARTS[0] + PARTS[1], P * ND]
+        n = 8 * PARTS[2]
+        sgather(A("G", 0, 2 * n), A(OTH), A("qlst", edge[2], edge[3]))
         for c in range(2):
-            mm(ps(1 - c, 0, 320), K("IDN"), A("G", 320 * c, 320 * c + 320), True, False)
-            mm(ps(1 - c, 0, 320), K("NEGI"), A("QREP", 0, 320), False, True)
+            mm(ps(1 - c, 0, n), K("IDN"), A("G", n * c, n * c + n), True, False)
+            mm(ps(1 - c, 0, n), K("NEGI"), A("QREP", 0, n), False, True)
         for t in (0, 2, 1):
-            l0, l1 = parts[t]
-            n, o = 16 * (l1 - l0), H * t
+            l0, l1 = edge[t], edge[t + 1]
+            o, e = 16 * l0, 16 * l1
             if t < 2:
-                vgather(A("D", o, o + n), A(OTH), A("qlst", l0, l1), A("QREP", 0, n), Op.subtract)
-                act(A("RL", o, o + n), A("D", o, o + n), Fn.Abs)
+                vgather(A("D", o, e), A(OTH), A("qlst", l0, l1), A("QREP", 0, e - o), Op.subtract)
+                act(A("RL", o, e), A("D", o, e), Fn.Abs)
             else:
                 for c in range(2):
-                    act(A("RL", o + 320 * c, o + 320 * c + 320), ps(1 - c, 0, 320), Fn.Abs)
+                    act(A("RL", o + n * c, o + n * c + n), ps(1 - c, 0, n), Fn.Abs)
             mm(ps(4, l0, l1), K("IDN"), K("MROW", l0, l1), True, False)
             for i in range(16):
-                mm(ps(4, l0, l1), K("Z", 15 - i, 143 - i), A("RL", o + i, o + n, 16), False, i == 15)
-        if r == 0:
-            ts(A("T2a", 0, ND), A("OTH0", W + WRAP, None, SL), 64.0, Op.mult)
-            tt(A("T2", 0, ND), A("T2a", 0, ND), A("OTH0", W + WRAP + 1, None, SL), Op.add)
-        tt(A("T2L", 0, ND), A("T2", 0, ND), A("live", 0, ND), Op.mult)
+                mm(ps(4, l0, l1), K("Z", 15 - i, 143 - i), A("RL", o + i, e, 16), False, i == 15)
+        ts(q("v2"), va, 2, Op.mult)
         for d in range(ND):
             a, b = A("q_KM", d, d + 1), ps(4, d, P * ND, ND)
             do("V", lambda: g.vector.tensor_reduce(ap(a), ap(b), AxisListType.X, Op.min), [b], [a])
 
+        am = lambda d: A("SC", F * (ND + d), F * (ND + d) + 1)
         tt(A("an", 0, ND), q("KM"), A("T2L", 0, ND), Op.is_lt)
         mm(ps(5, 0, ND), K("LST6"), A("an", 0, ND), True, False)
         for k in range(1, ND):
@@ -634,36 +627,36 @@ def rank_program(g, core, T, topo):
         ts(q("km"), q("ki"), P - 1, Op.bitwise_and)
         tt(q("kt"), q("km"), q("v2"), Op.mult)
         tt(A("a8", 0, ND), ps(5, 0, ND), A("pl8", 0, ND), Op.add)
-        tt(q("kc"), q("kt"), q("c0"), Op.add)
+        tt(q("kc"), q("kt"), A("qraw", 0, ND), Op.add)
         ts(A("alo", 0, ND), A("a8", 0, ND), 15, Op.bitwise_and)
-        tt(A("am", 0, ND), A("a8", 0, ND), K("JK", 0, ND), Op.min)
+        tt(A("SC", F * ND, None, F), A("a8", 0, ND), K("JK", 0, ND), Op.min)
         cp(A("alf", 0, ND), A("alo", 0, ND))
-        ts(q("kd"), q("kc"), W - 1, Op.bitwise_and)
+        low(q("kd"), q("kc"))
         for d in range(ND):
             o, lt = 128 * d, 136 * d
             lo = A("alf", d, d + 1)
-            ts(A("LT", lt, lt + 129), K("J16", 0, 129), A("am", d, d + 1), Op.is_gt)
-            ts(A("HI", o, o + 128), K("IB"), lo, Op.is_le, -6.0, Op.mult)
-            ts(A("LO", o, o + 128), K("IARR"), lo, Op.is_gt, -6.0, Op.mult)
+            act(A("LT", lt, lt + 129), K("J16h", 0, 129), Fn.Sign, scale=-1.0, bias=am(d))
+            ts(A("HI", o, o + 128), K("IB"), lo, Op.is_le, 3.0, Op.mult)
+            ts(A("LO", o, o + 128), K("IARR"), lo, Op.is_gt, 3.0, Op.mult)
             mm(ps(6, 0, 128), A("HI", o, o + 128), A("LT", lt, lt + 128), False, False)
             mm(ps(6, 0, 128), A("LO", o, o + 128), A("LT", lt + 1, lt + 129), False, d == ND - 1)
             if d == 0:
-                cp(q("kf"), q("kd"))
-        for d in range(ND):
-            ts(A("FL", F * d, F * d + F), K("FB", F * d, F * d + F), A("q_kf", d, d + 1), Op.add)
-        sgather(A("FIL"), A(OTH), A("FL", 0, ND * F))
-        ts(A("PL", HJ, 2 * HJ), ps(6, HJ, 2 * HJ), K("I16", 0, 1), Op.add, 0.0, Op.max)
-        ts(A("PL", 0, HJ), ps(6, 0, HJ), K("I16", 0, 1), Op.add, 0.0, Op.max)
-        sgather(A(XN, H, W), A("Xnat"), A("PL", HJ, 2 * HJ))
-        for d in range(ND):
-            ts(A("SLu", F * d, F * d + F), K("FC", 0, F), A("am", d, d + 1), Op.add)
-        vgather(A(XN, 0, H), A("Xnat"), A("PL", 0, HJ))
-        scatter(A(XN), A("SLu", 0, ND * F), A("FIL"))
+                tt(A("SC", 0, F * ND, F), q("kd"), K("FB", 0, ND), Op.add)
+            if d == 1:
+                scan(A("SD"), K("RZ"), A("SC"), Op.mult, Op.add)
+            if d == 2:
+                cp(A("FS"), A("SD"))
+        sgather(A("FIL"), A(OTH), A("FS", 0, ND * F))
+        ts(A("PL", XCUT, 128), ps(6, XCUT, 128), col("IPL"), Op.add, 0.0, Op.max)
+        ts(A("PL", 0, XCUT), ps(6, 0, XCUT), col("IPL"), Op.add, 0.0, Op.max)
+        sgather(A(XN, 16 * XCUT, W), A("Xnat"), A("PL", XCUT, 128))
+        vgather(A(XN, 0, 16 * XCUT), A("Xnat"), A("PL", 0, XCUT))
+        scatter(A(XN), A("FS", ND * F, 2 * ND * F), A("FIL"))
 
     dma("Y", T.y[:, 0:H], T.XC[:, 0:H], "dy0", [A("XC", 0, H)], [])
     dma("S", T.y[:, H:W], T.XC[:, H:W], "dy1", [A("XC", H, W)], [])
     for e in ("V", "S", "T", "G"):
         wait("G", semof[e], cnt[e])
     g.wait_ge(T.sem.lsem, tot[0])
-    for s in ("dwt", "dx0", "dx1", "dth", "dy0", "dy1"):
+    for s in ("dwt", "dx0", "dx1", "dxi", "dth", "dy0", "dy1"):
         g.wait_ge(T.sem[s], 16)

@@ -1,4 +1,4 @@
-import numpy as np
+import math
 from concourse.bass import DstId, RemoteDMATransfer
 from concourse.mybir import dt, AluOpType as Op, AxisListType, ActivationFunctionType as Fn
 
@@ -6,7 +6,6 @@ N, W, L, M, P, Q, F, RO = 6, 2048, 16, 6, 32, 16, 6, 2
 H = W // 2
 HJ = H // 16
 ND = N - 1
-XW = 3072
 WRAP = 14
 SL = W + 16 + 128
 SENT = (SL, W + 16)
@@ -34,9 +33,10 @@ def many(names, cols, dtype):
 
 
 sb("XA", SL, "bfloat16")
-many("XB XC", XW, "bfloat16")
+many("XB XC", W + 16, "bfloat16")
 many("OTH0 OTH1", ND * SL, "bfloat16")
-many("Xst Xnat XI", W, "bfloat16")
+many("Xst XI", W, "bfloat16")
+sb("Xnat", W + 8 * ND * Q, "bfloat16")
 many("BIh CS", W, "float16")
 many("D RL", M * W, "bfloat16")
 many("i_ui i_ua i_us i_r1 i_r2 i_fr i_n5 i_n6", 2 * HJ, "int32")
@@ -46,45 +46,45 @@ many("FAR CNT", M * 128, "bfloat16")
 sb("FAR5", 128, "bfloat16")
 many("f_e f_g", 2 * HJ, "float32")
 sb("NXH", 2 * HJ, "float16")
-many("NXW NX2", W, "float32")
-sb("CM", 512, "float16")
-many("k_MS k_IDh k_NIh", 128, "float16")
-many("k_L0h k_ONh", 8, "float16")
+many("NXW NX2 NX3", W, "float32")
+sb("CM", 768, "float16")
+many("k_MS k_IDh k_NIh k_BLK8", 128, "float16")
+many("k_L0h k_ONh k_M8", 8, "float16")
 many("LC LF PL NXU", 128, "uint16")
 many("JA JB INC TI", 128, "bfloat16")
-many("GO GP CC", 640, "bfloat16")
-sb("LT", ND * 136, "bfloat16")
-many("LO HI", 640, "bfloat16")
+many("GO GP CC LT", 640, "bfloat16")
+sb("EQ", ND * 136, "float16")
+many("P1 P2 P3", 640, "float16")
 sb("AL", 8, "uint16")
-many("plc live pl8 T2 T2a T2L", 8, "float32")
+many("pl8 T2", 8, "float32")
 sb("ASK", ND * Q, "bfloat16")
-sb("FIL", ND * Q * F, "bfloat16")
-sb("QREP", 16 * ND * Q, "bfloat16")
-sb("G", 960, "bfloat16")
+sb("QREP", 1024, "bfloat16")
+sb("G", 512, "bfloat16")
 sb("VS", 80, "float32")
-many("q_vi q_v q_ki q_km q_kc q_kd", 16, "int32")
-many("q_f q_v2 q_KM q_kt", 16, "float32")
+many("q_vi q_v q_ki q_km q_kc q_kd q_pi q_pe q_e ai", 16, "int32")
+many("q_f q_h1 q_KM q_kt q_kf q_w q_w6 q_wn af", 16, "float32")
 many("qraw qmsk", P * ND, "int32")
 sb("qlst", P * ND, "uint16")
-many("SD SC k_RZ", 2 * ND * F, "float32")
 sb("k_ONF", 128, "float32")
-sb("FS", 2 * ND * F, "uint16")
+sb("FS", 8 * ND, "uint16")
+many("FR k_FB", 8 * ND, "float16")
+sb("k_FBf", 8 * ND, "float32")
 sb("an", 8, "bfloat16")
-many("a8 alo", 8, "int32")
-sb("alf", 8, "float32")
 sb("ONB", M * 128, "bfloat16")
-many("k_TMP k_BLK k_IDN k_ID2 k_LST1 k_LSTI k_LST6 k_BLK6 k_NEGI k_N8I k_IP1 k_IARRt k_IARR k_IBt k_IB k_MQ k_J16 k_ZR", 128, "bfloat16")
+many("k_TMP k_TMP8 k_BLK k_IDN k_ID2 k_ID32 k_LST1 k_LSTI k_LST6 k_LSTN k_BLK6 k_BLK3 k_NEGI k_IP1 k_IARRt k_IARR k_IARR6 k_IBt k_IB k_IB10 k_MQ k_J16",
+     128, "bfloat16")
+sb("k_JJ", 144, "bfloat16")
+sb("k_ZR", 128, "bfloat16")
 many("k_Z k_WZ", 144, "bfloat16")
-many("k_J16f k_J16h", 144, "float32")
+sb("k_J32", 128, "float32")
 many("k_B1 k_B2 k_BN", 8, "bfloat16")
 many("k_NP1 k_NARRt k_NARR", 640, "bfloat16")
-sb("k_MROWf", P * ND, "float32")
 sb("k_MROW", P * ND, "bfloat16")
 sb("k_MC", P, "float32")
 many("k_MKi k_MKa", 128, "int32")
 many("k_MK k_MK1 k_MKb k_DG k_T1F k_PWi k_PW", 128, "float32")
 many("k_p k_p2 TH", 8, "int32")
-many("k_I16 k_I6 k_IPL k_I128 k_IB1 k_PWl k_LB k_T k_B k_BQ k_JKb k_JK k_FB", 8, "float32")
+many("k_I16 k_IPL k_I128 k_IB1 k_PWl k_LB k_T k_B k_BQ k_SLb k_SLOT k_GE8 k_C16 k_T8 k_F1a k_F1", 8, "float32")
 sb("k_L0", 8, "uint16")
 many("k_CW k_GW WT", 8, "bfloat16")
 for _k in range(8):
@@ -92,16 +92,29 @@ for _k in range(8):
 for _d in ARENA:
     SB[ARENA[_d][0]] = ("sbuf", [128, ARENA[_d][1]], _d)
 SCRATCH = SB
-SEMAPHORES = ["sV", "sS", "sT", "sG", "lsem", "dx0", "dx1", "dxi", "dwt", "dth", "dy0", "dy1", "o0", "o1", "h0", "h1"] + ["ga%d" % _k for _k in range(M * RO)]
+SEMAPHORES = (["sV", "sS", "sT", "sG", "lsem", "dx0", "dx1", "dwt", "dth", "di0", "di1", "dy0", "dy1", "dy2", "dy3", "o0", "o1", "h0", "h1"]
+              + ["ga%d" % _k for _k in range(M * RO)])
 
-PLAN = [tuple(int(c) if c.isdigit() else c for c in x.split(".")) for x in (
-    "l0 sg.0.0 sg.0.1 l1 sg.2.0 vg.1.0 sg.2.1 vg.1.1 sg.4.0 vg.3.0 td.1 sg.4.1 once td.0 vg.3.1 ab.3.0 rl.1.0 ab.3.1 vg.5.0 td.2 ab.2.1 "
-    "rl.1.1 tr.3 ab.5.0 rl.0.0 tr.1 rl.2.0 ab.4.0 rl.0.1 tr.2 vg.5.1 ab.4.1 tr.0 far.3 ab.5.1 n5 tr.4 far.1 far.2 n6 far.0 tr.5 far.4 "
-    "count far.5 succ").split()]
+
+def order(text):
+    return [tuple(int(c) if c.isdigit() else c for c in x.split(".")) for x in text.split()]
+
+
+PLAN = order(
+    "send l0 sg.0.0 t1 sg.0.1 l1 sg.2.0 vg.1.0 sg.2.1 vg.1.1 sg.4.0 vg.3.0 td.1 sg.4.1 once td.0 vg.3.1 ab.3.0 rl.1.0 ab.3.1 vg.5.0 td.2 ab.2.1.5 "
+    "rl.1.1 tr.3 ab.5.0 rl.0.0 tr.1 rl.2.0 rl.2.1.5 ab.4.0 rl.0.1 tr.2 vg.5.1 ab.4.1 tr.0 t2 far.3 ab.5.1 cs n5 tr.4 far.1 far.2 n6 far.0 tr.5 far.4 "
+    "count far.5 ft fa r2 fg fr succ")
+BIV = 9
 TWO = [s[1] for s in PLAN if s[0] == "td"]
-CUT = 68
-PARTS = (60, 60, 40)
-XCUT = 64
+CUT = (64, 72)
+XCUT = 112
+WIN = ((0, 4), (1, 8), (5, 8), (2, 4), (3, 8), (7, 8))
+BATCH = ((0, 2), (2, 3), (3, ND))
+CHAIN = ((0, 2), (2, ND))
+NEXT = order(
+    "sum.0 km.0 an.0 k1.0 sum.1 k2.0 n.0 sum.2 km.1 k3.0 a1.0 b1.1 k4.0 a2.0 km.2 a3.0 k5.0 b2.1 an.1 n.1 ls.0 ls.1 sa.0 k1.1 eq.0 sb.0 k2.1 "
+    "k6.0 ma.0 a1.1 mb.0 fr.0 lm.0 lm.1 k3.1 eq.1 fm.0 a2.1 sb.1 k4.1 sa.1 a3.1 ls.2 ls.3 ls.4 ma.1 mb.1 fs.0 k5.1 eq.2 sa.2 k6.1 sb.2 fg.0 "
+    "fr.1 eq.3 ma.2 mb.2 lm.2 fm.1 sb.3 sa.3 lm.3 eq.4 sa.4 lm.4 fs.1 ma.3 mb.3 fg.1 sb.4 ma.4 mb.4")
 
 
 def helpers(topo, cores, core):
@@ -172,9 +185,7 @@ def rank_program(g, core, T, topo):
     def overlap(a, b):
         if a[1] >= b[2] or b[1] >= a[2]:
             return False
-        if a[3] == b[3] and a[3] > 1 and (a[1] - b[1]) % a[3]:
-            return False
-        return True
+        return (a[1] - b[1]) % math.gcd(a[3], b[3]) == 0
 
     def wait(e, sem, val):
         k = known[e]
@@ -261,6 +272,9 @@ def rank_program(g, core, T, topo):
     def scan(out, d0, d1, op0, op1):
         do("V", lambda: g.vector.tensor_tensor_scan(ap(out), ap(d0), ap(d1), 0.0, op0, op1), [d0, d1], [out])
 
+    def least(out, in_):
+        do("V", lambda: g.vector.tensor_reduce(ap(out), ap(in_), AxisListType.X, Op.min), [in_], [out])
+
     def act(out, in_, func=Fn.Copy, scale=1.0, bias=0.0):
         do("S", lambda: g.scalar.activation(ap(out), ap(in_), func, bias=val(bias), scale=val(scale)), [x for x in (in_, scale, bias) if is_ap(x)], [out])
 
@@ -275,9 +289,6 @@ def rank_program(g, core, T, topo):
 
     def sgather(out, win, off, scale=1.0):
         do("S", lambda: g.scalar.activation(ap(out), ap(win).indirect(ap(off)), Fn.Copy, scale=scale), [win, off], [out])
-
-    def scatter(win, off, in_):
-        do("V", lambda: g.vector.tensor_copy(ap(win).indirect(ap(off)), ap(in_)), [off, in_], [win])
 
     def iota(out, pattern, base, chan, flag=False):
         if flag:
@@ -302,50 +313,52 @@ def rank_program(g, core, T, topo):
     asel(K("BLK"), K("TMP"), [[16, 8], [0, 16]], Op.is_ge, 15, -1)
     iota(K("MKi"), [[-1, 128]], 128, 1)
     iota(col("p"), [[0, 1]], 0, 1)
-    asel(K("IDN"), ON, [[-1, 128]], Op.is_equal, 0, 1)
     iota(K("PWi"), [[16, 128]], 1, 0, True)
     iota(K("LB"), [[16, 8]], 0, 0, True)
-    dma("Y", T.XI[:, :], T.x0[:, :], "dxi", [], [A("XI")])
+    asel(K("IDN"), ON, [[-1, 128]], Op.is_equal, 0, 1)
+    dma("Y", T.XI[:, :], T.x0[:, :], "di0", [], [A("XI")])
     span = lambda a, b: (a[0], a[1], b[2], 1)
     ms(span(K("ZR"), K("WZ")), 0.0)
     ms(A("ONB", 128), 1.0)
-    ms(span(A("SC"), K("ONF")), 1.0)
+    ms(K("ONF"), 1.0)
     ms(A("FAR", 0, None, M), 0.0)
-    ms(K("RZ", 0, None, F), 0.0)
     B8 = K("BLK", 0, 128, 16)
     act(K("Z", 15, 143, 16), B8)
+    act(K("BN"), B8, scale=-1.0)
     act(K("B1"), B8)
     act(K("B2"), B8, scale=2.0)
-    act(K("BN"), B8, scale=-1.0)
+    act(K("BLK6"), K("BLK"), scale=6.0)
     ts(K("MKa"), K("MKi"), 15, Op.bitwise_and)
     ts(col("p2"), col("p"), 15, Op.bitwise_and)
     ts(K("MK"), K("MKa"), 0, Op.is_equal)
     cp(col("I16"), col("p2"))
-    ts(K("WZ", 15, 143, 16), B8, A("WT", 0, 1), Op.mult)
-    cp(K("T", 0, 2), A("TH", 0, 2))
-    ts(A("XA", W + 16, SL), K("BLK"), A("WT", 0, 1), Op.mult)
-    hi, lo = A("XA", W + WRAP, W + WRAP + 1), A("XA", W + WRAP + 1, W + WRAP + 2)
+    ts(K("MK1"), K("MKa"), 15, Op.is_equal, -BIG, Op.mult)
+    ts(K("MKb"), K("MK"), 2 * BIG, Op.mult)
+    ts(col("GE8"), col("p2"), 8, Op.is_ge)
+    tt(K("M8"), K("MK", 0, 8), K("MK", 8, 16), Op.add)
+    tt(K("MS"), K("MK1"), K("MKb"), Op.add)
     act(col("B"), K("MK", 15, 16), scale=-BIG, bias=BIG)
     act(col("I128"), col("I16"), scale=128.0)
-    act(hi, K("T", 1, 2))
     act(col("PWl"), col("I16"), bias=W - 15.0)
-    act(lo, hi, Fn.Identity, scale=-1.0, bias=K("T", 1, 2))
-    act(K("DG"), K("IDN"), scale=col("T"))
     act(col("IB1"), col("B"), Fn.Identity, scale=-1.0, bias=col("I128"))
     act(K("PW", 0, 127), K("PWi", 0, 127), Fn.Identity, bias=col("I16"))
     act(K("PW", 127, 128), K("MK", 15, 16), Fn.Identity, scale=-float(W), bias=col("PWl"))
     act(K("L0h"), K("LB"), Fn.Identity, bias=col("IB1"))
+    ts(K("WZ", 15, 143, 16), B8, A("WT", 0, 1), Op.mult)
+    cp(K("T", 0, 2), A("TH", 0, 2))
+    ts(A("XA", W + 16, SL), K("BLK"), A("WT", 0, 1), Op.mult)
+    hi, lo = A("XA", W + WRAP, W + WRAP + 1), A("XA", W + WRAP + 1, W + WRAP + 2)
+    act(hi, K("T", 1, 2))
+    act(K("DG"), K("IDN"), scale=col("T"))
+    act(lo, hi, Fn.Identity, scale=-1.0, bias=K("T", 1, 2))
     cp(A("XA", W, W + WRAP), A("XA", 0, WRAP))
-    ts(K("MK1"), K("MKa"), 15, Op.is_equal, -BIG, Op.mult)
-    ts(K("MKb"), K("MK"), 2 * BIG, Op.mult)
+    ts(K("L0"), K("LB"), col("I128"), Op.add)
     for i in range(16):
         a = A("BIh", 128 * i, 128 * i + 128)
-        if i < 6:
+        if i < BIV:
             ts(a, K("BLK"), K("MK", i, i + 1), Op.mult)
         else:
             act(a, K("BLK"), scale=K("MK", i, i + 1))
-    tt(K("MS"), K("MK1"), K("MKb"), Op.add)
-    ts(K("L0"), K("LB"), col("I128"), Op.add)
 
     def diag(out, c):
         asel(out, K("ZR"), [[-1, 128]], Op.not_equal, 0, 1, c)
@@ -360,34 +373,41 @@ def rank_program(g, core, T, topo):
         asel(K("NARR"), K("NARRt"), [[0, ND], [16, 8], [0, 16]], Op.is_ge, 15, -1)
         asel(K("LST1"), K("BLK"), [[1, 128]], Op.is_ge, -1, -1)
         asel(K("LSTI"), K("BLK"), [[1, 128]], Op.is_ge, 0, -1)
-        iota(K("J16f"), [[16, 144]], 0, 0, True)
-        iota(K("MROWf"), [[1, P], [0, ND]], 0, 0, True)
-        iota(K("JKb", 0, ND), [[16 * F, ND]], 2560, 0, True)
+        iota(K("CW", 0, 2), [[-15, 2]], 16, 0, True)
+        iota(K("GW", 0, 2), [[127, 2]], 1, 0, True)
+        iota(K("SLb", 0, ND), [[128, ND]], W, 0, True)
         iota(K("MC"), [[2, P]], 1, 0, True)
-        iota(K("FB", 0, ND), [[SL, ND]], 1, 0, True)
         diag(K("NEGI"), -1.0)
-        diag(K("N8I"), -8192.0)
+        for d0, d1 in BATCH:
+            iota(K("MROW", P * d0, P * d1), [[1, P], [0, d1 - d0]], 0, 0, True)
+        diag(K("ID32"), 1.0 / P)
+        iota(K("J16"), [[16, 128]], 0, 0, True)
+        iota(K("J32"), [[32, 128]], -1, 0, True)
+        asel(K("LST6"), K("BLK6"), [[1, 128]], Op.is_ge, -1, -1)
+        asel(K("LSTN"), K("LST6"), [[-1, 128]], Op.not_equal, 0, 1, -8192.0)
+        iota(K("FBf"), [[SL, ND], [0, 8]], 0, 0, True)
+        asel(K("FB"), K("FBf"), [[0, 8 * ND]], Op.is_ge, 0, 0)
         iota(K("IP1"), [[0, 8], [1, 16]], 1, 0, True)
         asel(K("IARRt"), K("IP1"), [[-16, 8], [0, 16]], Op.is_ge, 0, 1)
         asel(K("IBt"), K("IP1"), [[-16, 8], [0, 16]], Op.is_ge, 0, 1, 99.0)
         asel(K("IARR"), K("IARRt"), [[16, 8], [0, 16]], Op.is_ge, 15, -1)
         asel(K("IB"), K("IBt"), [[16, 8], [0, 16]], Op.is_ge, 15, -1, 99.0)
+        iota(K("JJ", 0, 129), [[1, 129]], -1, 0, True)
+        asel(K("TMP8"), ON, [[-8, 16], [0, 8]], Op.is_ge, 0, 1)
+        asel(K("BLK8"), K("TMP8"), [[8, 16], [0, 8]], Op.is_ge, 7, -1)
 
-    consts_s = [
-        lambda: act(K("MQ"), K("MS"), scale=1024.0),
-        lambda: act(col("BQ"), col("B"), scale=1024.0),
-        lambda: act(col("I6"), col("I16"), scale=float(F)),
-        lambda: act(col("IPL"), col("I16"), bias=-3.0 * ND * Q),
-        lambda: act(K("LST6"), K("LST1"), scale=6.0),
-        lambda: act(K("BLK6"), K("BLK"), scale=6.0),
-        lambda: act(K("J16"), K("J16f", 0, 128)),
-        lambda: act(K("J16h"), K("J16f"), bias=-0.5),
-        lambda: act(K("MROW"), K("MROWf"), scale=1.0 / P),
-        lambda: act(K("JK", 0, ND), K("JKb", 0, ND), Fn.Identity, bias=col("I6")),
-        lambda: act(K("CW", 0, 1), A("ONB", 0, 1), scale=16.0),
-        lambda: act(K("CW", 1, 2), A("ONB", 0, 1)),
-        lambda: act(K("GW", 0, 1), A("ONB", 0, 1)),
-        lambda: act(K("GW", 1, 2), A("ONB", 0, 1), scale=128.0)]
+    def consts_1():
+        mm(ps(0, 128, 256), K("ONF"), K("DG"), True, True)
+
+    def consts_t():
+        act(col("BQ"), col("B"), scale=1024.0)
+        act(K("MQ"), K("MS"), scale=1024.0)
+        act(K("BLK3"), K("BLK"), scale=3.0)
+        act(col("IPL"), col("I16"), bias=-3.0 * ND * Q)
+        act(col("C16"), col("I16"), scale=16.0)
+        act(col("F1a"), col("I16"), bias=1.0)
+        act(col("T8"), col("GE8"), Fn.Identity, scale=-120.0, bias=col("C16"))
+        act(col("F1"), col("GE8"), Fn.Identity, scale=-8.0, bias=col("F1a"))
 
     hs = helpers(topo, cores, core)
     tot, na = [0], [0]
@@ -399,31 +419,31 @@ def rank_program(g, core, T, topo):
             for i in range(16):
                 mm(ps(h, 0, HJ), K("WZ", 15 - i, 143 - i), A(X, H * h + i, H * h + H, 16), i == 0, i == 15)
         if r:
-            cp(A(X, W, W + 16), A(X, 0, 16))
-        if r == 0:
-            mm(ps(2, 0, 128), K("ONF"), K("DG"), True, True)
-            act(K("T1F"), ps(2, 0, 128))
-        else:
-            act(A("XI"), A(X, 0, W))
-        n = SENT[r] // NP
-        for ks in ([0], range(1, NP)) if r == 0 else (range(NP),):
-            trs = []
-            for k in ks:
-                need("G", [A(X, n * k, n * k + n)], [])
-                rid, pid = topo.addr(hs[k], core)
-                es = topo.engines(core, hs[k])
-                e = len(es) // NP
-                trs.append(RemoteDMATransfer(dst_ids=[DstId(rid=rid, pnc=pid)], dma_engine_mask=sum(1 << x for x in es[e * k:e * k + e]),
-                                             remote_sem=T.sem["h%d" % r], src=T[X][:, n * k:n * k + n], dst=T[OTH][:, n * k:n * k + n]))
-                tot[0] += e
-            g.remote_dma_fused(trs, local_sem=T.sem.lsem)
+            act(A(X, W, W + 16), A(X, 0, 16))
+            act(A("XI", 0, H), A(X, 0, H))
+            dma("Y", T.XI[:, H:W], T[X][:, H:W], "di1", [A(X, H, W)], [A("XI", H, W)])
+
+        def send():
+            n = SENT[r] // NP
+            for ks in ([0], range(1, NP)) if r == 0 else (range(NP),):
+                trs = []
+                for k in ks:
+                    need("G", [A(X, n * k, n * k + n)], [])
+                    rid, pid = topo.addr(hs[k], core)
+                    es = topo.engines(core, hs[k])
+                    e = len(es) // NP
+                    trs.append(RemoteDMATransfer(dst_ids=[DstId(rid=rid, pnc=pid)], dma_engine_mask=sum(1 << x for x in es[e * k:e * k + e]),
+                                                 remote_sem=T.sem["h%d" % r], src=T[X][:, n * k:n * k + n], dst=T[OTH][:, n * k:n * k + n]))
+                    tot[0] += e
+                g.remote_dma_fused(trs, local_sem=T.sem.lsem)
 
         I = lambda n, h=None: A("i_" + n) if h is None else A("i_" + n, HJ * h, HJ * h + HJ)
-        u2 = ps(7, 0, 128)
+        u2 = ps(7, 256, 384)
         bb = lambda h: ps(7, 128 + HJ * h, 128 + HJ * h + HJ)
         lk = lambda n, m, h: A(n, 128 * m + HJ * h, 128 * m + HJ * h + HJ)
         lks = lambda n, m0, m1: A(n, 128 * m0, 128 * m1)
-        more = lambda m: tt(lks("raw", m, m + 1), u2, lks("raw", m - 1, m), Op.add)
+        u4 = ps(7, 384, 512)
+        more = lambda m, k: tt(lks("raw", m, m + 1), (u2, u4)[k - 1], lks("raw", m - k, m - k + 1), Op.add)
         low = lambda a, b: ts(a, b, W - 1, Op.bitwise_and)
 
         def first_look(h):
@@ -437,16 +457,20 @@ def rank_program(g, core, T, topo):
 
         def lists0():
             a, b = first_look(0), first_look(1)
-            for f in a[:5] + [b[0], a[5], b[1], a[6], b[2], lambda: ts(u2, I("ua"), 2, Op.mult), b[3], b[4], lambda: more(1), b[5],
-                              lambda: more(2), b[6], lambda: low(lks("msk", 1, 3), lks("raw", 1, 3)), lambda: more(3),
-                              lambda: cp(lks("lst", 1, 3), lks("msk", 1, 3))]:
+            for f in a[:5] + [b[0], a[5], b[1], b[2], a[6], lambda: ts(u2, I("ua"), 2, Op.mult), b[3], lambda: ts(u4, I("ua"), 4, Op.mult), b[4], b[5]]:
                 f()
+            more(1, 1)
+            more(2, 2)
+            b[6]()
+            more(3, 2)
+            low(lks("msk", 1, 3), lks("raw", 1, 3))
+            more(4, 2)
+            more(5, 2)
+            cp(lks("lst", 1, 3), lks("msk", 1, 3))
 
         def lists1():
-            more(4)
-            ts(I("r1"), lks("raw", 0, 1), 1, Op.add)
-            more(5)
             low(lks("msk", 3, M), lks("raw", 3, M))
+            ts(I("r1"), lks("raw", 0, 1), 1, Op.add)
             ts(I("n5"), lks("raw", 5, M), 1, Op.add)
             cp(lks("lst", 3, M), lks("msk", 3, M))
 
@@ -462,16 +486,17 @@ def rank_program(g, core, T, topo):
         def vgath(m, h):
             vgather(U("D", m, h), A(X, 0, W), lk("lst", m, h), A("XI", H * h, H * h + H), Op.subtract)
 
-        def relu(m, h):
-            ts(U("RL", m, h), U("D", m, h), 0.0, Op.max)
+        def relu(m, h, c=0):
+            o, e = U("D", m, h)[1:3]
+            ts(A("RL", o + 128 * c, e), A("D", o + 128 * c, e), 0.0, Op.max)
 
-        def size(m, h):
-            act(U("RL", m, h), U("D", m, h), Fn.Relu if m in TWO else Fn.Abs)
+        def size(m, h, c=8):
+            o = U("D", m, h)[1]
+            act(A("RL", o, o + 128 * c), A("D", o, o + 128 * c), Fn.Relu if m in TWO else Fn.Abs)
 
         def tdiff(m):
-            mm(dist(m), K("IDN"), K("ZR"), True, False)
             for i in range(16):
-                mm(dist(m, i), A("D", W * m + i, W * m + W, 16), K("BN"), False, False)
+                mm(dist(m, i), A("D", W * m + i, W * m + W, 16), K("BN"), i == 0, False)
 
         def tsize(m):
             two = m in TWO
@@ -480,73 +505,85 @@ def rank_program(g, core, T, topo):
 
         def far(m):
             tt(A("FAR", M - 1 - m, None, M) if m < M - 1 else A("FAR5"), dist(m), K("T1F"), Op.is_ge)
+            if m == M - 1:
+                mm(ps(0, 0, 128), A("FAR5"), K("IDN"), True, True)
+
+        c, ft, fa, y = [ps(7, 128 * k, 128 * k + 128) for k in range(4)]
 
         def count():
             scan(A("CNT"), A("ONB"), A("FAR"), Op.add, Op.mult)
-            mm(ps(7, 0, 128), A("CNT", M - 1, None, M), K("ID2"), True, True)
+            mm(c, A("CNT", M - 1, None, M), K("ID2"), True, True)
 
         def succ():
-            c, ft, fa, y = [ps(7, 128 * k, 128 * k + 128) for k in range(4)]
-            mm(ps(0, 0, 128), A("FAR5"), K("IDN"), True, True)
-            tt(ft, c, I("ua"), Op.mult)
-            ts(fa, c, 2.0 * (M - 1), Op.is_ge)
-            tt(I("r2"), ft, I("r1"), Op.add)
-            tt(A("f_g"), fa, A("f_e"), Op.mult)
-            low(I("fr"), I("r2"))
             tt(y, ps(0, 0, 128), A("f_g"), Op.mult)
             tt(A("NXH"), y, I("fr"), Op.add)
-            at = lambda i: ps(i // 2, 128 * (i % 2), 128 * (i % 2) + 128)
-            for i in range(16):
-                mm(at(i), A("BIh", 128 * i, 128 * i + 128), A("NXH"), True, True)
             cp(A("NXU"), A("NXH"))
-            for i in range(16):
-                (cp if (i // 2) % 2 else act)(A("NXW", i, W, 16), at(i))
+            for bank, (i0, step) in enumerate(WIN):
+                n = 16 // step
+                for k in range(n):
+                    i = i0 + step * k
+                    mm(ps(bank, k, 128 * n, n), A("BIh", 128 * i, 128 * i + 128), A("NXH"), True, True)
+                (act if n == 4 else cp)(A("NXW", i0, W, step), ps(bank, 0, 128 * n))
 
-        calls = {"sg": sgath, "vg": vgath, "rl": relu, "ab": size, "td": tdiff, "tr": tsize, "far": far, "count": count, "succ": succ,
+        first = lambda f: f if r == 0 else (lambda: None)
+        calls = {"send": send, "sg": sgath, "vg": vgath, "rl": relu, "ab": size, "td": tdiff, "tr": tsize, "far": far, "count": count, "succ": succ,
                  "l0": lists0, "l1": lists1, "n5": lambda: low(I("n6"), I("n5")), "n6": lambda: tt(A("f_e"), K("PW"), I("n6"), Op.subtract),
-                 "once": consts_g if r == 0 else (lambda: None)}
+                 "ft": lambda: tt(ft, c, I("ua"), Op.mult), "fa": lambda: ts(fa, c, 2.0 * (M - 1), Op.is_ge),
+                 "r2": lambda: tt(I("r2"), ft, I("r1"), Op.add), "fg": lambda: tt(A("f_g"), fa, A("f_e"), Op.mult), "fr": lambda: low(I("fr"), I("r2")),
+                 "once": first(consts_g), "cs": first(consts_t), "t1": first(consts_1), "t2": first(lambda: cp(K("T1F"), ps(0, 128, 256)))}
         for step in PLAN:
             calls[step[0]](*step[1:])
 
         now = lambda k: A("CS", 128 * k + 15, 128 * k + 128, 16) if k else K("L0h")
         lc = lambda k: A("LC", 8 * k, 8 * k + 8) if k else K("L0")
-        cm = lambda k: A("CM", 128 * (k % 4), 128 * (k % 4) + 128)
+        cm = lambda k: A("CM", 128 * (k % 6), 128 * (k % 6) + 128)
         pick = lambda k: scan(A("CS", 128 * k, 128 * k + 128), K("MS"), cm(k), Op.add, Op.min)
         relist = lambda k: ts(lc(k), now(k), col("B"), Op.add)
 
-        def settle(k):
-            mm(ps(7, k - 1, 128, 16), K("NIh"), now(k - 1), True, False)
-            mm(ps(3, k, 128, 16), K("IDh"), now(k), True, True)
-            mm(ps(7, k - 1, 128, 16), K("IDh"), now(k), False, True)
+        def settle(*ks):
+            for k in ks:
+                mm(ps(7, k - 1, 128, 16), K("IDh"), now(k), False, True)
+                if k < L - 1 and k != ks[-1]:
+                    mm(ps(7, k, 128, 16), K("NIh"), now(k), True, False)
+            for k in ks:
+                mm(ps(3, k, 128, 16), K("IDh"), now(k), True, True)
+            if ks[-1] < L - 1:
+                mm(ps(7, ks[-1], 128, 16), K("NIh"), now(ks[-1]), True, False)
 
         mm(ps(7, 15, 128, 16), K("IDh"), K("ONh"), True, True)
         mm(ps(3, 0, 128, 16), K("IDh"), K("L0h"), True, True)
+        mm(ps(7, 0, 128, 16), K("NIh"), K("L0h"), True, False)
         sgather(cm(1), A("NXW"), lc(0))
-        vgather(A("NX2", 0, 16 * CUT), A("NXW"), A("NXU", 0, CUT))
-        sgather(A("NX2", 16 * CUT, W), A("NXW"), A("NXU", CUT, 128))
+        window = lambda f, a, b, c0, c1: f(A(a, 16 * c0, 16 * c1), A(b), A("NXU", c0, c1))
+        window(vgather, "NX2", "NXW", 0, CUT[0])
+        window(sgather, "NX2", "NXW", CUT[0], 128)
         pick(1)
         relist(1)
-        settle(1)
-        for k in range(2, L, 2):
-            sgather(cm(k + 1), A("NX2"), lc(k - 1))
-            vgather(cm(k), A("NX2"), lc(k - 2))
-            if r == 0:
-                for f in consts_s[k - 2:k]:
-                    f()
-            pick(k)
+        window(vgather, "NX3", "NX2", 0, CUT[1] // 2)
+        sgather(cm(3), A("NX2"), lc(1))
+        sgather(cm(2), A("NX2"), lc(0))
+        window(sgather, "NX3", "NX2", CUT[1], 128)
+        pick(3)
+        window(vgather, "NX3", "NX2", CUT[1] // 2, CUT[1])
+        relist(3)
+        pick(2)
+        settle(1, 2, 3)
+        for k in range(3, L - 1, 3):
+            vgather(cm(k + 3), A("NX3"), lc(k))
+            sgather(cm(k + 1), A("NXW"), lc(k))
+            sgather(cm(k + 2), A("NX2"), lc(k))
+            pick(k + 3)
             pick(k + 1)
-            if k + 2 < L:
-                relist(k)
-                relist(k + 1)
-            settle(k)
-            settle(k + 1)
+            if k + 3 < L - 1:
+                relist(k + 3)
+            pick(k + 2)
+            settle(k + 1, k + 2, k + 3)
 
-        ts(A("LF"), ps(3, 0, 128), col("B"), Op.add)
         ts(A("JA"), ps(7, 0, 128), 1.0, Op.not_equal, -1.0, Op.add)
         ts(A("JB"), ps(7, 0, 128), 1.0 - W, Op.not_equal)
+        ts(A("LF"), ps(3, 0, 128), col("B"), Op.add)
         scan(A("INC"), A("JA"), A("JB"), Op.add, Op.add)
-        sgather(A("Xst"), A(X, 0, W), A("LF"))
-        mm(ps(2, 0, 2 * ND), K("IDN"), K("ZR", 0, 2 * ND), True, False)
+        sgather(A("Xst", 0, 16 * XCUT), A(X, 0, W), A("LF", 0, XCUT))
         mm(ps(6, 0, 1), K("LST1"), A("INC", 127, 128), True, True)
         mm(ps(6, 1, 2), K("LSTI"), A("INC", 127, 128), True, True)
         ts(A("TI"), A("INC"), -1.0, Op.mult, A("INC", 127, 128), Op.add)
@@ -560,103 +597,127 @@ def rank_program(g, core, T, topo):
             tt(A("CC", 320 * c, 320 * c + 320), ps(c, 0, 320), K("NP1", 320 * c, 320 * c + 320), Op.is_lt)
         for s, w in (("GO", "GW"), ("CC", "CW")):
             for d in range(ND):
-                mm(ps(2, 2 * d, 2 * d + 2), A(s, 128 * d, 128 * d + 128), K(w, 0, 2), False, s == "CC" and d == ND - 1)
+                mm(ps(2, 2 * d, 2 * d + 2), A(s, 128 * d, 128 * d + 128), K(w, 0, 2), s == "GO" and d == 0, s == "CC" and d == ND - 1)
+        vgather(A("Xst", 16 * XCUT, W), A(X, 0, W), A("LF", XCUT, 128))
         ts(A("AL", 0, ND), ps(2, 0, 2 * ND, 2), -1.0, Op.add, W - 1.0, Op.min)
-        ts(A("plc", 0, ND), ps(2, 1, 2 * ND, 2), -128.0, Op.add)
         vgather(A("ASK"), A("Xst"), A("AL", 0, ND))
+        ts(A("q_pi", 0, ND), ps(2, 1, 2 * ND, 2), -127.0, Op.add)
         for i in range(16):
             asel(A("Xnat", 128 * i, 128 * i + 128), A("Xst", i, W, 16), [[0, 128]], Op.is_ge, 0, 0)
 
         note([], [A(OTH)], "o%d" % r, NP * 2 * len(topo.engines(core, cores[(rank + 1) % N])))
         for d in range(ND):
             mm(ps(3, Q * d, Q * d + Q), A("OTH0", SL * d + W + 16, SL * d + SL), A("ASK", Q * d, Q * d + Q), True, True)
-        act(A("QREP", 0, 80), A("ASK"))
-        act(A("QREP", 80, 160), A("ASK"))
-        n, top = 160, 16 * max(PARTS)
-        while n < top:
-            act(A("QREP", n, min(2 * n, top)), A("QREP", 0, min(n, top - n)))
-            n *= 2
-        q = lambda n: A("q_" + n, 0, ND)
-        ts(A("live", 0, ND), A("plc", 0, ND), float(W), Op.is_lt)
-        ts(A("pl8", 0, ND), A("plc", 0, ND), 8193.0, Op.add)
-        if r == 0:
-            tt(A("T2", 0, ND), A("OTH0", W + WRAP, None, SL), A("OTH0", W + WRAP + 1, None, SL), Op.add)
+        edge = [Q * P * d0 for d0, d1 in BATCH] + [Q * P * ND]
+        qa, qb, qc = edge[1:]
+        dd = lambda t: range(*BATCH[t])
+        of = lambda d: [t for t in range(3) if d in dd(t)][0]
+        ask = lambda t: A("ASK", Q * BATCH[t][0], Q * BATCH[t][1])
+        q = lambda n, d0=0, d1=ND: A("q_" + n, d0, d1)
+        ql = lambda n, d: A(n, P * BATCH[of(d)][0] + d - BATCH[of(d)][0], P * BATCH[of(d)][1], len(dd(of(d))))
+        keys = lambda t, c=0, step=1: ps((4, 2, 3)[t], 128 + c, 128 + P * len(dd(t)), step)
+        for t, bank in ((0, 1), (2, 5)):
+            for k in range(8):
+                mm(ps(bank, 32 * k, 32 * k + 32), K("IDN"), ask(t), True, True)
+            act(A("QREP", 256 * t, 256 * t + 256), ps(bank, 0, 256))
+            if t == 0:
+                act(A("QREP", 256, 512), A("QREP", 0, 256))
+        for k in range(P):
+            mm(ps(0, Q * k, Q * k + Q), K("NEGI"), ask(1), k == 0, False)
+        ts(q("pe"), q("pi"), 2 * W - 2, Op.bitwise_and)
         scan(A("VS"), K("MQ", 0, 80), ps(3, 0, 80), Op.add, Op.min)
         ts(q("vi"), A("VS", 15, 80, 16), col("BQ"), Op.add)
-        tt(A("T2L", 0, ND), A("T2", 0, ND), A("live", 0, ND), Op.mult)
         va, vs = A("q_v", 0, ND), A("q_v", ND, 2 * ND)
+        ts(A("pl8", 0, ND), q("pi"), 8192.0, Op.add)
         low(va, q("vi"))
         ts(vs, q("vi"), W - 1, Op.bitwise_and, 5, Op.arith_shift_right)
         cp(A("q_f", 0, 2 * ND), A("q_v", 0, 2 * ND))
         for d in range(ND):
-            ts(A("qraw", d, P * ND, ND), K("MC"), A("q_f", ND + d, ND + d + 1), Op.add, A("q_f", d, d + 1), Op.mult)
+            ts(ql("qraw", d), K("MC"), A("q_f", ND + d, ND + d + 1), Op.add, A("q_f", d, d + 1), Op.mult)
         low(A("qmsk"), A("qraw"))
-        for d in range(ND):
-            ts(A("qlst", d, P * ND, ND), A("qmsk", d, P * ND, ND), float(SL * d), Op.add)
-        mm(ps(6, 0, 128), K("IDN"), K("J16"), True, False)
-        edge = [0, PARTS[0], PARTS[0] + PARTS[1], P * ND]
-        n = 8 * PARTS[2]
-        sgather(A("G", 0, 2 * n), A(OTH), A("qlst", edge[2], edge[3]))
-        for c in range(2):
-            mm(ps(1 - c, 0, n), K("IDN"), A("G", n * c, n * c + n), True, False)
-            mm(ps(1 - c, 0, n), K("NEGI"), A("QREP", 0, n), False, True)
-        for t in (0, 2, 1):
-            l0, l1 = edge[t], edge[t + 1]
-            o, e = 16 * l0, 16 * l1
-            if t < 2:
-                vgather(A("D", o, e), A(OTH), A("qlst", l0, l1), A("QREP", 0, e - o), Op.subtract)
-                act(A("RL", o, e), A("D", o, e), Fn.Abs)
+        for d in (2, 0, 1, 3, 4):
+            ts(ql("qlst", d), ql("qmsk", d), float(SL * d), Op.add)
+        for t in (1, 0, 2):
+            if t == 1:
+                sgather(A("G"), A(OTH), A("qlst", qa // 16, qb // 16))
+                act(A("QREP", 768, 1024), A("QREP", 512, 768))
+                if r == 0:
+                    act(K("SLOT", 0, ND), K("SLb", 0, ND), Fn.Identity, bias=col("T8"))
             else:
-                for c in range(2):
-                    act(A("RL", o + n * c, o + n * c + n), ps(1 - c, 0, n), Fn.Abs)
-            mm(ps(4, l0, l1), K("IDN"), K("MROW", l0, l1), True, False)
-            for i in range(16):
-                mm(ps(4, l0, l1), K("Z", 15 - i, 143 - i), A("RL", o + i, e, 16), False, i == 15)
-        ts(q("v2"), va, 2, Op.mult)
-        for d in range(ND):
-            a, b = A("q_KM", d, d + 1), ps(4, d, P * ND, ND)
-            do("V", lambda: g.vector.tensor_reduce(ap(a), ap(b), AxisListType.X, Op.min), [b], [a])
+                for o in range(edge[t], edge[t + 1], 512):
+                    vgather(A("D", o, o + 512), A(OTH), A("qlst", o // 16, o // 16 + 32), A("QREP", 256 * t, 256 * t + 512), Op.subtract)
+        mm(ps(0, 0, 512), K("IDN"), A("G"), False, True)
+        mm(ps(6, 0, 128), K("IDN"), K("J16"), True, False)
+        for t in range(3):
+            mm(keys(t), K("ID32"), K("MROW", edge[t] // 16, edge[t + 1] // 16), True, False)
+        for o in range(0, qc, 512):
+            act(A("RL", o, o + 512), ps(0, 0, 512) if o == qa else A("D", o, o + 512), Fn.Abs)
+        if r == 0:
+            ts(K("IARR6"), K("IARR"), -float(F), Op.add)
+            ts(K("IB10"), K("IB"), 16.0 - F, Op.add)
+            tt(A("T2", 0, ND), A("OTH0", W + WRAP, None, SL), A("OTH0", W + WRAP + 1, None, SL), Op.add)
 
-        am = lambda d: A("SC", F * (ND + d), F * (ND + d) + 1)
-        tt(A("an", 0, ND), q("KM"), A("T2L", 0, ND), Op.is_lt)
-        mm(ps(5, 0, ND), K("LST6"), A("an", 0, ND), True, False)
-        for k in range(1, ND):
-            mm(ps(5, k, ND), K("BLK6"), A("an", 0, ND - k), False, False)
-        mm(ps(5, 0, ND), K("N8I"), A("an", 0, ND), False, True)
-        ts(q("ki"), q("KM"), float(P), Op.mult)
-        ts(q("km"), q("ki"), P - 1, Op.bitwise_and)
-        tt(q("kt"), q("km"), q("v2"), Op.mult)
-        tt(A("a8", 0, ND), ps(5, 0, ND), A("pl8", 0, ND), Op.add)
-        tt(q("kc"), q("kt"), A("qraw", 0, ND), Op.add)
-        ts(A("alo", 0, ND), A("a8", 0, ND), 15, Op.bitwise_and)
-        tt(A("SC", F * ND, None, F), A("a8", 0, ND), K("JK", 0, ND), Op.min)
-        cp(A("alf", 0, ND), A("alo", 0, ND))
-        low(q("kd"), q("kc"))
-        for d in range(ND):
-            o, lt = 128 * d, 136 * d
-            lo = A("alf", d, d + 1)
-            act(A("LT", lt, lt + 129), K("J16h", 0, 129), Fn.Sign, scale=-1.0, bias=am(d))
-            ts(A("HI", o, o + 128), K("IB"), lo, Op.is_le, 3.0, Op.mult)
-            ts(A("LO", o, o + 128), K("IARR"), lo, Op.is_gt, 3.0, Op.mult)
-            mm(ps(6, 0, 128), A("HI", o, o + 128), A("LT", lt, lt + 128), False, False)
-            mm(ps(6, 0, 128), A("LO", o, o + 128), A("LT", lt + 1, lt + 129), False, d == ND - 1)
-            if d == 0:
-                tt(A("SC", 0, F * ND, F), q("kd"), K("FB", 0, ND), Op.add)
-            if d == 1:
-                scan(A("SD"), K("RZ"), A("SC"), Op.mult, Op.add)
-            if d == 2:
-                cp(A("FS"), A("SD"))
-        sgather(A("FIL"), A(OTH), A("FS", 0, ND * F))
-        ts(A("PL", XCUT, 128), ps(6, XCUT, 128), col("IPL"), Op.add, 0.0, Op.max)
-        ts(A("PL", 0, XCUT), ps(6, 0, XCUT), col("IPL"), Op.add, 0.0, Op.max)
-        sgather(A(XN, 16 * XCUT, W), A("Xnat"), A("PL", XCUT, 128))
-        vgather(A(XN, 0, 16 * XCUT), A("Xnat"), A("PL", 0, XCUT))
-        scatter(A(XN), A("FS", ND * F, 2 * ND * F), A("FIL"))
+        tt(q("w"), K("SLOT", 0, ND), q("pe"), Op.subtract)
+        ts(q("e"), q("pi"), 1, Op.bitwise_and)
+        ts(q("h1"), vs, 1, Op.add)
+        ts(q("w6"), q("w"), float(F), Op.add)
+        ts(q("wn"), q("w"), -1.0, Op.mult, -float(F), Op.add)
+        ai = lambda d0, d1, k: A("ai", 3 * d0 + k * (d1 - d0), 3 * d0 + (k + 1) * (d1 - d0))
+        af = lambda d, k: [A("af", 2 * d0 + k * (d1 - d0) + d, 2 * d0 + k * (d1 - d0) + d + 1) for d0, d1 in CHAIN if d0 <= d < d1][0]
+        blk = lambda n, d: A(n, 128 * d, 128 * d + 128)
+        eq = lambda d, c: A("EQ", 136 * d + c, 136 * d + c + 128)
+        last = [x for x in NEXT if x[0] in ("lm", "ma", "mb")][-1]
 
-    dma("Y", T.y[:, 0:H], T.XC[:, 0:H], "dy0", [A("XC", 0, H)], [])
-    dma("S", T.y[:, H:W], T.XC[:, H:W], "dy1", [A("XC", H, W)], [])
+        def chain(t):
+            d0, d1 = CHAIN[t]
+            p = lambda n: q(n, d0, d1)
+            return {
+                "an": lambda: tt(A("an", d0, d1), p("KM"), A("T2", d0, d1), Op.is_lt),
+                "n": lambda: [mm(ps(5, d0 + k, d1), K("BLK6" if k else "LSTN"), A("an", d0, d1 - k), k == 0, k == d1 - d0 - 1) for k in range(d1 - d0)],
+                "b1": lambda: [mm(ps(1, 0, 1), K("BLK6"), A("an", d, d + 1), d == 0, d == d0 - 1) for d in range(d0)],
+                "b2": lambda: ts(A("pl8", d0, d1), A("pl8", d0, d1), ps(1, 0, 1), Op.add),
+                "a1": lambda: tt(ai(d0, d1, 0), ps(5, d0, d1), A("pl8", d0, d1), Op.add),
+                "a2": lambda: [ts(ai(d0, d1, 1), ai(d0, d1, 0), 15, Op.bitwise_and), ts(ai(d0, d1, 2), ai(d0, d1, 0), 4, Op.arith_shift_right)],
+                "a3": lambda: cp(A("af", 3 * d0, 3 * d1), A("ai", 3 * d0, 3 * d1)),
+                "k1": lambda: ts(p("ki"), p("KM"), 2.0 * P, Op.mult),
+                "k2": lambda: ts(p("km"), p("ki"), 2 * P - 2, Op.bitwise_and),
+                "k3": lambda: tt(p("kt"), p("km"), p("h1"), Op.add),
+                "k4": lambda: tt(p("kc"), p("kt"), p("f"), Op.mult),
+                "k5": lambda: low(p("kd"), p("kc")),
+                "k6": lambda: tt(p("kf"), p("kd"), p("e"), Op.subtract),
+                "fr": lambda: [ts(A("FR", 8 * d, 8 * d + 8), K("M8"), q("kf", d, d + 1), Op.mult) for d in range(d0, d1)],
+                "fm": lambda: [mm(ps(7, 8 * d0, 8 * d1), K("IDh"), K("FB", 8 * d0, 8 * d1), True, False),
+                               mm(ps(7, 8 * d0, 8 * d1), K("BLK8"), A("FR", 8 * d0, 8 * d1), False, True)],
+                "fs": lambda: ts(A("FS", 8 * d0, 8 * d1), ps(7, 8 * d0, 8 * d1), col("F1"), Op.add),
+                "fg": lambda: sgather(A("Xnat", W + 128 * d0, W + 128 * d1), A(OTH), A("FS", 8 * d0, 8 * d1))}
+
+        calls = {
+            "eq": lambda d: ts(A("EQ", 136 * d, 136 * d + 129), K("JJ", 0, 129), af(d, 2), Op.is_equal),
+            "sum": lambda t: [mm(keys(t), K("Z", 15 - i, 143 - i), A("RL", edge[t] + i, edge[t + 1], 16), False, i == 15) for i in range(16)],
+            "km": lambda t: [least(q("KM", d, d + 1), keys(t, d - BATCH[t][0], len(dd(t)))) for d in dd(t)],
+            "ls": lambda d: act(blk("LT", d), K("J32"), Fn.Sign, scale=-0.5, bias=af(d, 0)),
+            "lm": lambda d: mm(ps(6, 0, 128), K("BLK3"), blk("LT", d), False, last == ("lm", d)),
+            "sa": lambda d: ts(blk("P1", d), K("IARR"), af(d, 1), Op.is_gt, q("w", d, d + 1), Op.mult),
+            "sb": lambda d: [ts(blk("P2", d), K("IARR6"), af(d, 1), Op.is_gt, q("wn", d, d + 1), Op.mult),
+                             ts(blk("P3", d), K("IB10"), af(d, 1), Op.is_le, q("w6", d, d + 1), Op.mult)],
+            "ma": lambda d: mm(ps(6, 0, 128), blk("P1", d), eq(d, 1), False, last == ("ma", d)),
+            "mb": lambda d: [mm(ps(6, 0, 128), blk("P2", d), eq(d, 1), False, False),
+                             mm(ps(6, 0, 128), blk("P3", d), eq(d, 0), False, last == ("mb", d))]}
+        chains = [chain(t) for t in range(len(CHAIN))]
+        for name, t in NEXT:
+            if name in calls:
+                calls[name](t)
+            else:
+                chains[t][name]()
+        for h in range(2):
+            ts(A("PL", HJ * h, HJ * h + HJ), ps(6, HJ * h, HJ * h + HJ), col("IPL"), Op.add)
+        for k in range(4):
+            (vgather if k % 2 else sgather)(A(XN, 512 * k, 512 * k + 512), A("Xnat"), A("PL", 32 * k, 32 * k + 32))
+
+    for k in (0, 1, 3, 2):
+        dma("S" if k == 2 else "Y", T.y[:, 512 * k:512 * k + 512], T.XC[:, 512 * k:512 * k + 512], "dy%d" % k, [A("XC", 512 * k, 512 * k + 512)], [])
     for e in ("V", "S", "T", "G"):
         wait("G", semof[e], cnt[e])
     g.wait_ge(T.sem.lsem, tot[0])
-    for s in ("dwt", "dx0", "dx1", "dxi", "dth", "dy0", "dy1"):
+    for s in ("dwt", "dx0", "dx1", "dth", "di0", "di1", "dy0", "dy1", "dy2", "dy3"):
         g.wait_ge(T.sem[s], 16)

import math
from concourse.bass import DstId, RemoteDMATransfer
from concourse.mybir import dt, AluOpType as Op, AxisListType, ActivationFunctionType as Fn

N, W, L, M, P, Q, F, RO = 6, 2048, 16, 6, 32, 16, 6, 2
H = W // 2
HJ = H // 16
ND = N - 1
WRAP = 14
SL = W + 16 + 128
SENT = (SL, W + 16)
NP = 4
BIG = 2048.0

SB = {}
PART = {}
ARENA = {"int32": ["ar_i", 0], "float32": ["ar_f", 0], "bfloat16": ["ar_b", 0], "uint16": ["ar_u", 0], "float16": ["ar_h", 0]}
OWN = ("WT", "TH")


def sb(name, cols, dtype):
    if cols <= 160 and name not in OWN:
        a = ARENA[dtype]
        PART[name] = (a[0], a[1], cols)
        a[1] += -(-cols // 16) * 16
    else:
        SB[name] = ("sbuf", [128, cols], dtype)


def many(names, cols, dtype):
    for n in names.split():
        sb(n, cols, dtype)


sb("XA", SL, "bfloat16")
many("XB XC", W + 16, "bfloat16")
many("OTH0 OTH1", ND * SL, "bfloat16")
many("Xst XI", W, "bfloat16")
sb("Xnat", W + 8 * ND * Q, "bfloat16")
many("BIh CS", W, "float16")
many("D RL", M * W, "bfloat16")
many("i_ui i_ua i_us i_r1 i_r2 i_fr i_n5 i_n6", 2 * HJ, "int32")
many("raw msk", 2 * M * HJ, "int32")
sb("lst", 2 * M * HJ, "uint16")
many("FAR CNT", M * 128, "bfloat16")
sb("FAR5", 128, "bfloat16")
many("f_e f_g", 2 * HJ, "float32")
sb("NXH", 2 * HJ, "float16")
many("NXW NX2 NX3", W, "float32")
sb("CM", 768, "float16")
many("k_MS k_IDh k_NIh k_BLK8", 128, "float16")
many("k_L0h k_ONh k_M8", 8, "float16")
many("LC LF PL NXU", 128, "uint16")
many("JA JB INC TI", 128, "bfloat16")
many("GO GP CC LT", 640, "bfloat16")
sb("EQ", ND * 136, "float16")
many("P1 P2 P3", 640, "float16")
sb("AL", 8, "uint16")
many("pl8 T2", 8, "float32")
sb("ASK", ND * Q, "bfloat16")
sb("QREP", 1024, "bfloat16")
sb("G", 512, "bfloat16")
sb("VS", 80, "float32")
many("q_vi q_v q_ki q_km q_kc q_kd q_pi q_pe q_e ai", 16, "int32")
many("q_f q_h1 q_KM q_kt q_kf q_w q_w6 q_wn af", 16, "float32")
many("qraw qmsk", P * ND, "int32")
sb("qlst", P * ND, "uint16")
sb("k_ONF", 128, "float32")
sb("FS", 8 * ND, "uint16")
many("FR k_FB", 8 * ND, "float16")
sb("k_FBf", 8 * ND, "float32")
sb("an", 8, "bfloat16")
sb("ONB", M * 128, "bfloat16")
many("k_TMP k_TMP8 k_BLK k_IDN k_ID2 k_ID32 k_LST1 k_LSTI k_LST6 k_LSTN k_BLK6 k_BLK3 k_NEGI k_IP1 k_IARRt k_IARR k_IARR6 k_IBt k_IB k_IB10 k_MQ k_J16",
     128, "bfloat16")
sb("k_JJ", 144, "bfloat16")
sb("k_ZR", 128, "bfloat16")
many("k_Z k_WZ", 144, "bfloat16")
sb("k_J32", 128, "float32")
many("k_B1 k_B2 k_BN", 8, "bfloat16")
many("k_NP1 k_NARRt k_NARR", 640, "bfloat16")
sb("k_MROW", P * ND, "bfloat16")
sb("k_MC", P, "float32")
many("k_MKi k_MKa", 128, "int32")
many("k_MK k_MK1 k_MKb k_DG k_T1F k_PWi k_PW", 128, "float32")
many("k_p k_p2 TH", 8, "int32")
many("k_I16 k_IPL k_I128 k_IB1 k_PWl k_LB k_T k_B k_BQ k_SLb k_SLOT k_GE8 k_C16 k_T8 k_F1a k_F1", 8, "float32")
sb("k_L0", 8, "uint16")
many("k_CW k_GW WT", 8, "bfloat16")
for _k in range(8):
    SB["ps%d" % _k] = ("psum", [128, 512], "float32")
for _d in ARENA:
    SB[ARENA[_d][0]] = ("sbuf", [128, ARENA[_d][1]], _d)
SCRATCH = SB
SEMAPHORES = (["sV", "sS", "sT", "sG", "lsem", "dx0", "dx1", "dwt", "dth", "di0", "di1", "dy0", "dy1", "dy2", "dy3", "o0", "o1", "h0", "h1"]
              + ["ga%d" % _k for _k in range(M * RO)])


def order(text):
    return [tuple(int(c) if c.isdigit() else c for c in x.split(".")) for x in text.split()]


PLAN = order(
    "send l0 sg.0.0 t1 sg.0.1 l1 sg.2.0 vg.1.0 sg.2.1 vg.1.1 sg.4.0 vg.3.0 td.1 sg.4.1 once td.0 vg.3.1 ab.3.0 rl.1.0 ab.3.1 vg.5.0 td.2 ab.2.1.5 "
    "rl.1.1 tr.3 ab.5.0 rl.0.0 tr.1 rl.2.0 rl.2.1.5 ab.4.0 rl.0.1 tr.2 vg.5.1 ab.4.1 tr.0 t2 far.3 ab.5.1 cs n5 tr.4 far.1 far.2 n6 far.0 tr.5 far.4 "
    "count far.5 ft fa r2 fg fr succ")
BIV = 9
TWO = [s[1] for s in PLAN if s[0] == "td"]
CUT = (64, 72)
XCUT = 112
WIN = ((0, 4), (1, 8), (5, 8), (2, 4), (3, 8), (7, 8))
BATCH = ((0, 2), (2, 3), (3, ND))
CHAIN = ((0, 2), (2, ND))
NEXT = order(
    "sum.0 km.0 an.0 k1.0 sum.1 k2.0 n.0 sum.2 km.1 k3.0 a1.0 b1.1 k4.0 a2.0 km.2 a3.0 k5.0 b2.1 an.1 n.1 ls.0 ls.1 sa.0 k1.1 eq.0 sb.0 k2.1 "
    "k6.0 ma.0 a1.1 mb.0 fr.0 lm.0 lm.1 k3.1 eq.1 fm.0 a2.1 sb.1 k4.1 sa.1 a3.1 ls.2 ls.3 ls.4 ma.1 mb.1 fs.0 k5.1 eq.2 sa.2 k6.1 sb.2 fg.0 "
    "fr.1 eq.3 ma.2 mb.2 lm.2 fm.1 sb.3 sa.3 lm.3 eq.4 sa.4 lm.4 fs.1 ma.3 mb.3 fg.1 sb.4 ma.4 mb.4")


def helpers(topo, cores, core):
    able = [c for c in topo.cores_of(core) if c != core and all(topo.may_write(c, o) for o in cores if o != core)]
    dies = sorted(set(topo.die(c) for c in able))
    out = []
    for k in range(NP):
        on = [c for c in able if topo.die(c) == dies[k % len(dies)]]
        out.append(on[(k // len(dies)) % len(on)])
    return out


def helper_program(g, core, T, topo):
    cores = T.cores
    owner = [c for c in cores if core in topo.cores_of(c)]
    if not owner:
        return
    rank = T.rank_of(owner[0])
    mine = [k for k, c in enumerate(helpers(topo, cores, owner[0])) if c == core]
    if not mine:
        return
    left = 0
    for r in range(RO):
        n = SENT[r] // NP
        g.wait_ge(T.sem["h%d" % r], len(mine) * len(topo.engines(owner[0], core)) // NP)
        for k in mine:
            trs = []
            for d in range(ND):
                dest = cores[(rank - 1 - d) % N]
                rid, pid = topo.addr(dest, core)
                es = topo.engines(core, dest)
                src, dst = T["OTH%d" % r][:, n * k:n * k + n], T["OTH%d" % r][:, SL * d + n * k:SL * d + n * k + n]
                if d < ND - 1:
                    e = len(es) // (ND - 1)
                    trs.append(RemoteDMATransfer(dst_ids=[DstId(rid=rid, pnc=pid)], dma_engine_mask=sum(1 << x for x in es[e * d:e * d + e]),
                                                 remote_sem=T.sem["o%d" % r], src=src, dst=dst))
                    left += e
                else:
                    g.remote_dma_fused(trs, local_sem=T.sem.lsem)
                    g.remote_dma(dst, src, T.sem["o%d" % r], T.sem.lsem, pid, rid, topo.mask(core, dest))
                    left += len(es)
    g.wait_ge(T.sem.lsem, left)


def rank_program(g, core, T, topo):
    rank = T.rank_of(core)
    if rank is None:
        helper_program(g, core, T, topo)
        return
    cores = T.cores
    queue = {"V": g.vector, "S": g.scalar, "T": g.tensor, "G": g, "Y": g.sync}
    semof = {"V": "sV", "S": "sS", "T": "sT", "G": "sG"}
    cnt = {"V": 0, "S": 0, "T": 0, "G": 0}
    known = {"V": {}, "S": {}, "T": {}, "G": {}, "Y": {}}
    snap = {}
    log = {}

    def A(name, c0=0, c1=None, step=1):
        if name in PART:
            a, o, n = PART[name]
            return (a, o + c0, o + (n if c1 is None else c1), step)
        n = SB[name][1][1]
        return (name, c0, n if c1 is None else c1, step)

    def ap(a):
        return T[a[0]][:, a[1]:a[2]:a[3]] if a[3] != 1 else T[a[0]][:, a[1]:a[2]]

    def overlap(a, b):
        if a[1] >= b[2] or b[1] >= a[2]:
            return False
        return (a[1] - b[1]) % math.gcd(a[3], b[3]) == 0

    def wait(e, sem, val):
        k = known[e]
        if k.get(sem, 0) >= val:
            return
        queue[e].wait_ge(T.sem[sem], val)
        s = snap.get((sem, val))
        if s:
            for q in s:
                if s[q] > k.get(q, 0):
                    k[q] = s[q]
        k[sem] = val

    def need(e, reads, writes):
        own = semof.get(e)
        req = {}
        for lst, isw in ((reads, False), (writes, True)):
            for a in lst:
                ps = SB[a[0]][0] == "psum"
                for (w, b, sem, val) in log.get(a[0], ()):
                    if sem == own:
                        if not (w or isw) or (ps and e == "T" and isw) or not overlap(a, b):
                            continue
                    elif not ps:
                        if not (w or isw) or not overlap(a, b):
                            continue
                    if val > req.get(sem, 0):
                        req[sem] = val
        for s in sorted(req, key=lambda s: -req[s]):
            wait(e, s, req[s])

    def covers(a, b):
        return a[1] <= b[1] and a[2] >= b[2] and (a[3] == 1 or (a[3] == b[3] and (a[1] - b[1]) % a[3] == 0))

    def note(reads, writes, sem, val):
        for a in writes:
            l = log.get(a[0], [])
            if SB[a[0]][0] != "psum":
                l = [x for x in l if not covers(a, x[1])]
            else:
                l = [x for x in l if not (x[0] and x[2] == sem and covers(a, x[1]))]
            l.append((True, a, sem, val))
            log[a[0]] = l
        for a in reads:
            l = log.setdefault(a[0], [])
            l[:] = [x for x in l if x[0] or x[2] != sem or not covers(a, x[1])]
            l.append((False, a, sem, val))

    def do(e, fn, reads, writes):
        need(e, reads, writes)
        cnt[e] += 1
        fn().then_inc(T.sem[semof[e]], 1)
        snap[(semof[e], cnt[e])] = dict(known[e])
        note(reads, writes, semof[e], cnt[e])

    def dma(e, out, in_, sem, reads, writes, **kw):
        need(e, reads, writes)
        queue[e].dma_start(out=out, in_=in_, **kw).then_inc(T.sem[sem], 16)
        snap[(sem, 16)] = dict(known[e])
        note(reads, writes, sem, 16)

    def is_ap(x):
        return isinstance(x, tuple)

    def val(x):
        return ap(x) if is_ap(x) else x

    def cp(out, in_):
        do("V", lambda: g.vector.tensor_copy(ap(out), ap(in_)), [in_], [out])

    def tt(out, a, b, op):
        do("V", lambda: g.vector.tensor_tensor(ap(out), ap(a), ap(b), op), [a, b], [out])

    def ts(out, a, s1, op0, s2=None, op1=None):
        rd = [a] + [s for s in (s1, s2) if is_ap(s)]
        if op1 is None:
            do("V", lambda: g.vector.tensor_scalar(ap(out), ap(a), val(s1), None, op0), rd, [out])
        else:
            do("V", lambda: g.vector.tensor_scalar(ap(out), ap(a), val(s1), val(s2), op0, op1), rd, [out])

    def ms(out, c):
        do("V", lambda: g.vector.memset(ap(out), c), [], [out])

    def scan(out, d0, d1, op0, op1):
        do("V", lambda: g.vector.tensor_tensor_scan(ap(out), ap(d0), ap(d1), 0.0, op0, op1), [d0, d1], [out])

    def least(out, in_):
        do("V", lambda: g.vector.tensor_reduce(ap(out), ap(in_), AxisListType.X, Op.min), [in_], [out])

    def act(out, in_, func=Fn.Copy, scale=1.0, bias=0.0):
        do("S", lambda: g.scalar.activation(ap(out), ap(in_), func, bias=val(bias), scale=val(scale)), [x for x in (in_, scale, bias) if is_ap(x)], [out])

    def mm(out, l, r, start, stop):
        do("T", lambda: g.tensor.matmul(ap(out), ap(l), ap(r), start, stop), [l, r], [out])

    def vgather(out, win, off, b=None, op=None):
        if b is None:
            do("V", lambda: g.vector.tensor_copy(ap(out), ap(win).indirect(ap(off))), [win, off], [out])
        else:
            do("V", lambda: g.vector.tensor_tensor(ap(out), ap(win).indirect(ap(off)), ap(b), op), [win, off, b], [out])

    def sgather(out, win, off, scale=1.0):
        do("S", lambda: g.scalar.activation(ap(out), ap(win).indirect(ap(off)), Fn.Copy, scale=scale), [win, off], [out])

    def iota(out, pattern, base, chan, flag=False):
        if flag:
            do("G", lambda: g.iota(ap(out), pattern, base, chan, allow_small_or_imprecise_dtypes=True), [], [out])
        else:
            do("G", lambda: g.iota(ap(out), pattern, base, chan), [], [out])

    def asel(out, in_, pattern, op, base, chan, fill=0.0):
        do("G", lambda: g.affine_select(ap(out), ap(in_), pattern, op, fill, base, chan), [in_], [out])

    dma("Y", T.WT[:, 0:1], T.wt[:, :], "dwt", [], [A("WT", 0, 1)])
    dma("S", T.XA[:, 0:H], T.x0[:, 0:H], "dx0", [], [A("XA", 0, H)])
    dma("Y", T.TH[:, 0:2], T.th[:, :], "dth", [], [A("TH", 0, 2)])
    dma("Y", T.XA[:, H:W], T.x0[:, H:W], "dx1", [], [A("XA", H, W)])

    K = lambda n, c0=0, c1=None, step=1: A("k_" + n, c0, c1, step)
    ON = A("ONB", 0, 128)
    ps = lambda k, c0, c1, step=1: A("ps%d" % k, c0, c1, step)
    col = lambda n: K(n, 0, 1)
    ms(ON, 1.0)
    asel(K("TMP"), ON, [[-16, 8], [0, 16]], Op.is_ge, 0, 1)
    asel(K("BLK"), K("TMP"), [[16, 8], [0, 16]], Op.is_ge, 15, -1)
    iota(K("MKi"), [[-1, 128]], 128, 1)
    iota(col("p"), [[0, 1]], 0, 1)
    iota(K("PWi"), [[16, 128]], 1, 0, True)
    iota(K("LB"), [[16, 8]], 0, 0, True)
    asel(K("IDN"), ON, [[-1, 128]], Op.is_equal, 0, 1)
    dma("Y", T.XI[:, :], T.x0[:, :], "di0", [], [A("XI")])
    span = lambda a, b: (a[0], a[1], b[2], 1)
    ms(span(K("ZR"), K("WZ")), 0.0)
    ms(A("ONB", 128), 1.0)
    ms(K("ONF"), 1.0)
    ms(A("FAR", 0, None, M), 0.0)
    B8 = K("BLK", 0, 128, 16)
    act(K("Z", 15, 143, 16), B8)
    act(K("BN"), B8, scale=-1.0)
    act(K("B1"), B8)
    act(K("B2"), B8, scale=2.0)
    act(K("BLK6"), K("BLK"), scale=6.0)
    ts(K("MKa"), K("MKi"), 15, Op.bitwise_and)
    ts(col("p2"), col("p"), 15, Op.bitwise_and)
    ts(K("MK"), K("MKa"), 0, Op.is_equal)
    cp(col("I16"), col("p2"))
    ts(K("MK1"), K("MKa"), 15, Op.is_equal, -BIG, Op.mult)
    ts(K("MKb"), K("MK"), 2 * BIG, Op.mult)
    ts(col("GE8"), col("p2"), 8, Op.is_ge)
    tt(K("M8"), K("MK", 0, 8), K("MK", 8, 16), Op.add)
    tt(K("MS"), K("MK1"), K("MKb"), Op.add)
    act(col("B"), K("MK", 15, 16), scale=-BIG, bias=BIG)
    act(col("I128"), col("I16"), scale=128.0)
    act(col("PWl"), col("I16"), bias=W - 15.0)
    act(col("IB1"), col("B"), Fn.Identity, scale=-1.0, bias=col("I128"))
    act(K("PW", 0, 127), K("PWi", 0, 127), Fn.Identity, bias=col("I16"))
    act(K("PW", 127, 128), K("MK", 15, 16), Fn.Identity, scale=-float(W), bias=col("PWl"))
    act(K("L0h"), K("LB"), Fn.Identity, bias=col("IB1"))
    ts(K("WZ", 15, 143, 16), B8, A("WT", 0, 1), Op.mult)
    cp(K("T", 0, 2), A("TH", 0, 2))
    ts(A("XA", W + 16, SL), K("BLK"), A("WT", 0, 1), Op.mult)
    hi, lo = A("XA", W + WRAP, W + WRAP + 1), A("XA", W + WRAP + 1, W + WRAP + 2)
    act(hi, K("T", 1, 2))
    act(K("DG"), K("IDN"), scale=col("T"))
    act(lo, hi, Fn.Identity, scale=-1.0, bias=K("T", 1, 2))
    cp(A("XA", W, W + WRAP), A("XA", 0, WRAP))
    ts(K("L0"), K("LB"), col("I128"), Op.add)
    for i in range(16):
        a = A("BIh", 128 * i, 128 * i + 128)
        if i < BIV:
            ts(a, K("BLK"), K("MK", i, i + 1), Op.mult)
        else:
            act(a, K("BLK"), scale=K("MK", i, i + 1))

    def diag(out, c):
        asel(out, K("ZR"), [[-1, 128]], Op.not_equal, 0, 1, c)

    def consts_g():
        diag(K("ID2"), 2.0)
        diag(K("IDh"), 1.0)
        diag(K("NIh"), -1.0)
        asel(K("ONh"), A("ONB", 0, 8), [[0, 8]], Op.is_ge, 0, 0)
        iota(K("NP1"), [[16, ND], [0, 8], [1, 16]], 1, 0, True)
        asel(K("NARRt"), K("NP1"), [[0, ND], [-16, 8], [0, 16]], Op.is_ge, 0, 1)
        asel(K("NARR"), K("NARRt"), [[0, ND], [16, 8], [0, 16]], Op.is_ge, 15, -1)
        asel(K("LST1"), K("BLK"), [[1, 128]], Op.is_ge, -1, -1)
        asel(K("LSTI"), K("BLK"), [[1, 128]], Op.is_ge, 0, -1)
        iota(K("CW", 0, 2), [[-15, 2]], 16, 0, True)
        iota(K("GW", 0, 2), [[127, 2]], 1, 0, True)
        iota(K("SLb", 0, ND), [[128, ND]], W, 0, True)
        iota(K("MC"), [[2, P]], 1, 0, True)
        diag(K("NEGI"), -1.0)
        for d0, d1 in BATCH:
            iota(K("MROW", P * d0, P * d1), [[1, P], [0, d1 - d0]], 0, 0, True)
        diag(K("ID32"), 1.0 / P)
        iota(K("J16"), [[16, 128]], 0, 0, True)
        iota(K("J32"), [[32, 128]], -1, 0, True)
        asel(K("LST6"), K("BLK6"), [[1, 128]], Op.is_ge, -1, -1)
        asel(K("LSTN"), K("LST6"), [[-1, 128]], Op.not_equal, 0, 1, -8192.0)
        iota(K("FBf"), [[SL, ND], [0, 8]], 0, 0, True)
        asel(K("FB"), K("FBf"), [[0, 8 * ND]], Op.is_ge, 0, 0)
        iota(K("IP1"), [[0, 8], [1, 16]], 1, 0, True)
        asel(K("IARRt"), K("IP1"), [[-16, 8], [0, 16]], Op.is_ge, 0, 1)
        asel(K("IBt"), K("IP1"), [[-16, 8], [0, 16]], Op.is_ge, 0, 1, 99.0)
        asel(K("IARR"), K("IARRt"), [[16, 8], [0, 16]], Op.is_ge, 15, -1)
        asel(K("IB"), K("IBt"), [[16, 8], [0, 16]], Op.is_ge, 15, -1, 99.0)
        iota(K("JJ", 0, 129), [[1, 129]], -1, 0, True)
        asel(K("TMP8"), ON, [[-8, 16], [0, 8]], Op.is_ge, 0, 1)
        asel(K("BLK8"), K("TMP8"), [[8, 16], [0, 8]], Op.is_ge, 7, -1)

    def consts_1():
        mm(ps(0, 128, 256), K("ONF"), K("DG"), True, True)

    def consts_t():
        act(col("BQ"), col("B"), scale=1024.0)
        act(K("MQ"), K("MS"), scale=1024.0)
        act(K("BLK3"), K("BLK"), scale=3.0)
        act(col("IPL"), col("I16"), bias=-3.0 * ND * Q)
        act(col("C16"), col("I16"), scale=16.0)
        act(col("F1a"), col("I16"), bias=1.0)
        act(col("T8"), col("GE8"), Fn.Identity, scale=-120.0, bias=col("C16"))
        act(col("F1"), col("GE8"), Fn.Identity, scale=-8.0, bias=col("F1a"))

    hs = helpers(topo, cores, core)
    tot, na = [0], [0]
    xs = ("XA", "XB", "XC")
    for r in range(RO):
        X, XN, OTH = xs[r], xs[r + 1], "OTH%d" % r

        for h in range(2):
            for i in range(16):
                mm(ps(h, 0, HJ), K("WZ", 15 - i, 143 - i), A(X, H * h + i, H * h + H, 16), i == 0, i == 15)
        if r:
            act(A(X, W, W + 16), A(X, 0, 16))
            act(A("XI", 0, H), A(X, 0, H))
            dma("Y", T.XI[:, H:W], T[X][:, H:W], "di1", [A(X, H, W)], [A("XI", H, W)])

        def send():
            n = SENT[r] // NP
            for ks in ([0], range(1, NP)) if r == 0 else (range(NP),):
                trs = []
                for k in ks:
                    need("G", [A(X, n * k, n * k + n)], [])
                    rid, pid = topo.addr(hs[k], core)
                    es = topo.engines(core, hs[k])
                    e = len(es) // NP
                    trs.append(RemoteDMATransfer(dst_ids=[DstId(rid=rid, pnc=pid)], dma_engine_mask=sum(1 << x for x in es[e * k:e * k + e]),
                                                 remote_sem=T.sem["h%d" % r], src=T[X][:, n * k:n * k + n], dst=T[OTH][:, n * k:n * k + n]))
                    tot[0] += e
                g.remote_dma_fused(trs, local_sem=T.sem.lsem)

        I = lambda n, h=None: A("i_" + n) if h is None else A("i_" + n, HJ * h, HJ * h + HJ)
        u2 = ps(7, 256, 384)
        bb = lambda h: ps(7, 128 + HJ * h, 128 + HJ * h + HJ)
        lk = lambda n, m, h: A(n, 128 * m + HJ * h, 128 * m + HJ * h + HJ)
        lks = lambda n, m0, m1: A(n, 128 * m0, 128 * m1)
        u4 = ps(7, 384, 512)
        more = lambda m, k: tt(lks("raw", m, m + 1), (u2, u4)[k - 1], lks("raw", m - k, m - k + 1), Op.add)
        low = lambda a, b: ts(a, b, W - 1, Op.bitwise_and)

        def first_look(h):
            return [lambda: cp(I("ui", h), ps(h, 0, HJ)),
                    lambda: low(I("ua", h), I("ui", h)),
                    lambda: ts(I("us", h), I("ui", h), W - 1, Op.bitwise_and, 5, Op.arith_shift_right),
                    lambda: tt(bb(h), I("ua", h), I("us", h), Op.mult),
                    lambda: tt(lk("raw", 0, h), bb(h), I("ua", h), Op.add),
                    lambda: low(lk("msk", 0, h), lk("raw", 0, h)),
                    lambda: cp(lk("lst", 0, h), lk("msk", 0, h))]

        def lists0():
            a, b = first_look(0), first_look(1)
            for f in a[:5] + [b[0], a[5], b[1], b[2], a[6], lambda: ts(u2, I("ua"), 2, Op.mult), b[3], lambda: ts(u4, I("ua"), 4, Op.mult), b[4], b[5]]:
                f()
            more(1, 1)
            more(2, 2)
            b[6]()
            more(3, 2)
            low(lks("msk", 1, 3), lks("raw", 1, 3))
            more(4, 2)
            more(5, 2)
            cp(lks("lst", 1, 3), lks("msk", 1, 3))

        def lists1():
            low(lks("msk", 3, M), lks("raw", 3, M))
            ts(I("r1"), lks("raw", 0, 1), 1, Op.add)
            ts(I("n5"), lks("raw", 5, M), 1, Op.add)
            cp(lks("lst", 3, M), lks("msk", 3, M))

        U = lambda n, m, h: A(n, W * m + H * h, W * m + H * h + H)
        dist = lambda m, i=None: ps(1 + m, 0, 128) if i is None else ps(1 + m, i, 128, 16)

        def sgath(m, h):
            a, b = U("D", m, h), A(X, H * h, H * h + H)
            sgather(a, A(X, 0, W), lk("lst", m, h), scale=-1.0)
            dma("G", ap(a), ap(b), "ga%d" % na[0], [b], [a], accum_op=Op.add)
            na[0] += 1

        def vgath(m, h):
            vgather(U("D", m, h), A(X, 0, W), lk("lst", m, h), A("XI", H * h, H * h + H), Op.subtract)

        def relu(m, h, c=0):
            o, e = U("D", m, h)[1:3]
            ts(A("RL", o + 128 * c, e), A("D", o + 128 * c, e), 0.0, Op.max)

        def size(m, h, c=8):
            o = U("D", m, h)[1]
            act(A("RL", o, o + 128 * c), A("D", o, o + 128 * c), Fn.Relu if m in TWO else Fn.Abs)

        def tdiff(m):
            for i in range(16):
                mm(dist(m, i), A("D", W * m + i, W * m + W, 16), K("BN"), i == 0, False)

        def tsize(m):
            two = m in TWO
            for i in range(16):
                mm(dist(m, i), A("RL", W * m + i, W * m + W, 16), K("B2") if two else K("B1"), not two, not two or i == 15)

        def far(m):
            tt(A("FAR", M - 1 - m, None, M) if m < M - 1 else A("FAR5"), dist(m), K("T1F"), Op.is_ge)
            if m == M - 1:
                mm(ps(0, 0, 128), A("FAR5"), K("IDN"), True, True)

        c, ft, fa, y = [ps(7, 128 * k, 128 * k + 128) for k in range(4)]

        def count():
            scan(A("CNT"), A("ONB"), A("FAR"), Op.add, Op.mult)
            mm(c, A("CNT", M - 1, None, M), K("ID2"), True, True)

        def succ():
            tt(y, ps(0, 0, 128), A("f_g"), Op.mult)
            tt(A("NXH"), y, I("fr"), Op.add)
            cp(A("NXU"), A("NXH"))
            for bank, (i0, step) in enumerate(WIN):
                n = 16 // step
                for k in range(n):
                    i = i0 + step * k
                    mm(ps(bank, k, 128 * n, n), A("BIh", 128 * i, 128 * i + 128), A("NXH"), True, True)
                (act if n == 4 else cp)(A("NXW", i0, W, step), ps(bank, 0, 128 * n))

        first = lambda f: f if r == 0 else (lambda: None)
        calls = {"send": send, "sg": sgath, "vg": vgath, "rl": relu, "ab": size, "td": tdiff, "tr": tsize, "far": far, "count": count, "succ": succ,
                 "l0": lists0, "l1": lists1, "n5": lambda: low(I("n6"), I("n5")), "n6": lambda: tt(A("f_e"), K("PW"), I("n6"), Op.subtract),
                 "ft": lambda: tt(ft, c, I("ua"), Op.mult), "fa": lambda: ts(fa, c, 2.0 * (M - 1), Op.is_ge),
                 "r2": lambda: tt(I("r2"), ft, I("r1"), Op.add), "fg": lambda: tt(A("f_g"), fa, A("f_e"), Op.mult), "fr": lambda: low(I("fr"), I("r2")),
                 "once": first(consts_g), "cs": first(consts_t), "t1": first(consts_1), "t2": first(lambda: cp(K("T1F"), ps(0, 128, 256)))}
        for step in PLAN:
            calls[step[0]](*step[1:])

        now = lambda k: A("CS", 128 * k + 15, 128 * k + 128, 16) if k else K("L0h")
        lc = lambda k: A("LC", 8 * k, 8 * k + 8) if k else K("L0")
        cm = lambda k: A("CM", 128 * (k % 6), 128 * (k % 6) + 128)
        pick = lambda k: scan(A("CS", 128 * k, 128 * k + 128), K("MS"), cm(k), Op.add, Op.min)
        relist = lambda k: ts(lc(k), now(k), col("B"), Op.add)

        def settle(*ks):
            for k in ks:
                mm(ps(7, k - 1, 128, 16), K("IDh"), now(k), False, True)
                if k < L - 1 and k != ks[-1]:
                    mm(ps(7, k, 128, 16), K("NIh"), now(k), True, False)
            for k in ks:
                mm(ps(3, k, 128, 16), K("IDh"), now(k), True, True)
            if ks[-1] < L - 1:
                mm(ps(7, ks[-1], 128, 16), K("NIh"), now(ks[-1]), True, False)

        mm(ps(7, 15, 128, 16), K("IDh"), K("ONh"), True, True)
        mm(ps(3, 0, 128, 16), K("IDh"), K("L0h"), True, True)
        mm(ps(7, 0, 128, 16), K("NIh"), K("L0h"), True, False)
        sgather(cm(1), A("NXW"), lc(0))
        window = lambda f, a, b, c0, c1: f(A(a, 16 * c0, 16 * c1), A(b), A("NXU", c0, c1))
        window(vgather, "NX2", "NXW", 0, CUT[0])
        window(sgather, "NX2", "NXW", CUT[0], 128)
        pick(1)
        relist(1)
        window(vgather, "NX3", "NX2", 0, CUT[1] // 2)
        sgather(cm(3), A("NX2"), lc(1))
        sgather(cm(2), A("NX2"), lc(0))
        window(sgather, "NX3", "NX2", CUT[1], 128)
        pick(3)
        window(vgather, "NX3", "NX2", CUT[1] // 2, CUT[1])
        relist(3)
        pick(2)
        settle(1, 2, 3)
        for k in range(3, L - 1, 3):
            vgather(cm(k + 3), A("NX3"), lc(k))
            sgather(cm(k + 1), A("NXW"), lc(k))
            sgather(cm(k + 2), A("NX2"), lc(k))
            pick(k + 3)
            pick(k + 1)
            if k + 3 < L - 1:
                relist(k + 3)
            pick(k + 2)
            settle(k + 1, k + 2, k + 3)

        ts(A("JA"), ps(7, 0, 128), 1.0, Op.not_equal, -1.0, Op.add)
        ts(A("JB"), ps(7, 0, 128), 1.0 - W, Op.not_equal)
        ts(A("LF"), ps(3, 0, 128), col("B"), Op.add)
        scan(A("INC"), A("JA"), A("JB"), Op.add, Op.add)
        sgather(A("Xst", 0, 16 * XCUT), A(X, 0, W), A("LF", 0, XCUT))
        mm(ps(6, 0, 1), K("LST1"), A("INC", 127, 128), True, True)
        mm(ps(6, 1, 2), K("LSTI"), A("INC", 127, 128), True, True)
        ts(A("TI"), A("INC"), -1.0, Op.mult, A("INC", 127, 128), Op.add)
        for c in range(2):
            s, e = 320 * c, 320 * c + 320
            ts(A("GO", s, e), K("NARR", s, e), ps(6, 0, 1), Op.is_gt)
            ts(A("GP", s, e), K("NARR", s, e), ps(6, 1, 2), Op.is_gt)
            mm(ps(c, 0, 320), A("INC"), A("GO", s, e), True, False)
            mm(ps(c, 0, 320), A("TI"), A("GP", s, e), False, True)
        for c in range(2):
            tt(A("CC", 320 * c, 320 * c + 320), ps(c, 0, 320), K("NP1", 320 * c, 320 * c + 320), Op.is_lt)
        for s, w in (("GO", "GW"), ("CC", "CW")):
            for d in range(ND):
                mm(ps(2, 2 * d, 2 * d + 2), A(s, 128 * d, 128 * d + 128), K(w, 0, 2), s == "GO" and d == 0, s == "CC" and d == ND - 1)
        vgather(A("Xst", 16 * XCUT, W), A(X, 0, W), A("LF", XCUT, 128))
        ts(A("AL", 0, ND), ps(2, 0, 2 * ND, 2), -1.0, Op.add, W - 1.0, Op.min)
        vgather(A("ASK"), A("Xst"), A("AL", 0, ND))
        ts(A("q_pi", 0, ND), ps(2, 1, 2 * ND, 2), -127.0, Op.add)
        for i in range(16):
            asel(A("Xnat", 128 * i, 128 * i + 128), A("Xst", i, W, 16), [[0, 128]], Op.is_ge, 0, 0)

        note([], [A(OTH)], "o%d" % r, NP * 2 * len(topo.engines(core, cores[(rank + 1) % N])))
        for d in range(ND):
            mm(ps(3, Q * d, Q * d + Q), A("OTH0", SL * d + W + 16, SL * d + SL), A("ASK", Q * d, Q * d + Q), True, True)
        edge = [Q * P * d0 for d0, d1 in BATCH] + [Q * P * ND]
        qa, qb, qc = edge[1:]
        dd = lambda t: range(*BATCH[t])
        of = lambda d: [t for t in range(3) if d in dd(t)][0]
        ask = lambda t: A("ASK", Q * BATCH[t][0], Q * BATCH[t][1])
        q = lambda n, d0=0, d1=ND: A("q_" + n, d0, d1)
        ql = lambda n, d: A(n, P * BATCH[of(d)][0] + d - BATCH[of(d)][0], P * BATCH[of(d)][1], len(dd(of(d))))
        keys = lambda t, c=0, step=1: ps((4, 2, 3)[t], 128 + c, 128 + P * len(dd(t)), step)
        for t, bank in ((0, 1), (2, 5)):
            for k in range(8):
                mm(ps(bank, 32 * k, 32 * k + 32), K("IDN"), ask(t), True, True)
            act(A("QREP", 256 * t, 256 * t + 256), ps(bank, 0, 256))
            if t == 0:
                act(A("QREP", 256, 512), A("QREP", 0, 256))
        for k in range(P):
            mm(ps(0, Q * k, Q * k + Q), K("NEGI"), ask(1), k == 0, False)
        ts(q("pe"), q("pi"), 2 * W - 2, Op.bitwise_and)
        scan(A("VS"), K("MQ", 0, 80), ps(3, 0, 80), Op.add, Op.min)
        ts(q("vi"), A("VS", 15, 80, 16), col("BQ"), Op.add)
        va, vs = A("q_v", 0, ND), A("q_v", ND, 2 * ND)
        ts(A("pl8", 0, ND), q("pi"), 8192.0, Op.add)
        low(va, q("vi"))
        ts(vs, q("vi"), W - 1, Op.bitwise_and, 5, Op.arith_shift_right)
        cp(A("q_f", 0, 2 * ND), A("q_v", 0, 2 * ND))
        for d in range(ND):
            ts(ql("qraw", d), K("MC"), A("q_f", ND + d, ND + d + 1), Op.add, A("q_f", d, d + 1), Op.mult)
        low(A("qmsk"), A("qraw"))
        for d in (2, 0, 1, 3, 4):
            ts(ql("qlst", d), ql("qmsk", d), float(SL * d), Op.add)
        for t in (1, 0, 2):
            if t == 1:
                sgather(A("G"), A(OTH), A("qlst", qa // 16, qb // 16))
                act(A("QREP", 768, 1024), A("QREP", 512, 768))
                if r == 0:
                    act(K("SLOT", 0, ND), K("SLb", 0, ND), Fn.Identity, bias=col("T8"))
            else:
                for o in range(edge[t], edge[t + 1], 512):
                    vgather(A("D", o, o + 512), A(OTH), A("qlst", o // 16, o // 16 + 32), A("QREP", 256 * t, 256 * t + 512), Op.subtract)
        mm(ps(0, 0, 512), K("IDN"), A("G"), False, True)
        mm(ps(6, 0, 128), K("IDN"), K("J16"), True, False)
        for t in range(3):
            mm(keys(t), K("ID32"), K("MROW", edge[t] // 16, edge[t + 1] // 16), True, False)
        for o in range(0, qc, 512):
            act(A("RL", o, o + 512), ps(0, 0, 512) if o == qa else A("D", o, o + 512), Fn.Abs)
        if r == 0:
            ts(K("IARR6"), K("IARR"), -float(F), Op.add)
            ts(K("IB10"), K("IB"), 16.0 - F, Op.add)
            tt(A("T2", 0, ND), A("OTH0", W + WRAP, None, SL), A("OTH0", W + WRAP + 1, None, SL), Op.add)

        tt(q("w"), K("SLOT", 0, ND), q("pe"), Op.subtract)
        ts(q("e"), q("pi"), 1, Op.bitwise_and)
        ts(q("h1"), vs, 1, Op.add)
        ts(q("w6"), q("w"), float(F), Op.add)
        ts(q("wn"), q("w"), -1.0, Op.mult, -float(F), Op.add)
        ai = lambda d0, d1, k: A("ai", 3 * d0 + k * (d1 - d0), 3 * d0 + (k + 1) * (d1 - d0))
        af = lambda d, k: [A("af", 2 * d0 + k * (d1 - d0) + d, 2 * d0 + k * (d1 - d0) + d + 1) for d0, d1 in CHAIN if d0 <= d < d1][0]
        blk = lambda n, d: A(n, 128 * d, 128 * d + 128)
        eq = lambda d, c: A("EQ", 136 * d + c, 136 * d + c + 128)
        last = [x for x in NEXT if x[0] in ("lm", "ma", "mb")][-1]

        def chain(t):
            d0, d1 = CHAIN[t]
            p = lambda n: q(n, d0, d1)
            return {
                "an": lambda: tt(A("an", d0, d1), p("KM"), A("T2", d0, d1), Op.is_lt),
                "n": lambda: [mm(ps(5, d0 + k, d1), K("BLK6" if k else "LSTN"), A("an", d0, d1 - k), k == 0, k == d1 - d0 - 1) for k in range(d1 - d0)],
                "b1": lambda: [mm(ps(1, 0, 1), K("BLK6"), A("an", d, d + 1), d == 0, d == d0 - 1) for d in range(d0)],
                "b2": lambda: ts(A("pl8", d0, d1), A("pl8", d0, d1), ps(1, 0, 1), Op.add),
                "a1": lambda: tt(ai(d0, d1, 0), ps(5, d0, d1), A("pl8", d0, d1), Op.add),
                "a2": lambda: [ts(ai(d0, d1, 1), ai(d0, d1, 0), 15, Op.bitwise_and), ts(ai(d0, d1, 2), ai(d0, d1, 0), 4, Op.arith_shift_right)],
                "a3": lambda: cp(A("af", 3 * d0, 3 * d1), A("ai", 3 * d0, 3 * d1)),
                "k1": lambda: ts(p("ki"), p("KM"), 2.0 * P, Op.mult),
                "k2": lambda: ts(p("km"), p("ki"), 2 * P - 2, Op.bitwise_and),
                "k3": lambda: tt(p("kt"), p("km"), p("h1"), Op.add),
                "k4": lambda: tt(p("kc"), p("kt"), p("f"), Op.mult),
                "k5": lambda: low(p("kd"), p("kc")),
                "k6": lambda: tt(p("kf"), p("kd"), p("e"), Op.subtract),
                "fr": lambda: [ts(A("FR", 8 * d, 8 * d + 8), K("M8"), q("kf", d, d + 1), Op.mult) for d in range(d0, d1)],
                "fm": lambda: [mm(ps(7, 8 * d0, 8 * d1), K("IDh"), K("FB", 8 * d0, 8 * d1), True, False),
                               mm(ps(7, 8 * d0, 8 * d1), K("BLK8"), A("FR", 8 * d0, 8 * d1), False, True)],
                "fs": lambda: ts(A("FS", 8 * d0, 8 * d1), ps(7, 8 * d0, 8 * d1), col("F1"), Op.add),
                "fg": lambda: sgather(A("Xnat", W + 128 * d0, W + 128 * d1), A(OTH), A("FS", 8 * d0, 8 * d1))}

        calls = {
            "eq": lambda d: ts(A("EQ", 136 * d, 136 * d + 129), K("JJ", 0, 129), af(d, 2), Op.is_equal),
            "sum": lambda t: [mm(keys(t), K("Z", 15 - i, 143 - i), A("RL", edge[t] + i, edge[t + 1], 16), False, i == 15) for i in range(16)],
            "km": lambda t: [least(q("KM", d, d + 1), keys(t, d - BATCH[t][0], len(dd(t)))) for d in dd(t)],
            "ls": lambda d: act(blk("LT", d), K("J32"), Fn.Sign, scale=-0.5, bias=af(d, 0)),
            "lm": lambda d: mm(ps(6, 0, 128), K("BLK3"), blk("LT", d), False, last == ("lm", d)),
            "sa": lambda d: ts(blk("P1", d), K("IARR"), af(d, 1), Op.is_gt, q("w", d, d + 1), Op.mult),
            "sb": lambda d: [ts(blk("P2", d), K("IARR6"), af(d, 1), Op.is_gt, q("wn", d, d + 1), Op.mult),
                             ts(blk("P3", d), K("IB10"), af(d, 1), Op.is_le, q("w6", d, d + 1), Op.mult)],
            "ma": lambda d: mm(ps(6, 0, 128), blk("P1", d), eq(d, 1), False, last == ("ma", d)),
            "mb": lambda d: [mm(ps(6, 0, 128), blk("P2", d), eq(d, 1), False, False),
                             mm(ps(6, 0, 128), blk("P3", d), eq(d, 0), False, last == ("mb", d))]}
        chains = [chain(t) for t in range(len(CHAIN))]
        for name, t in NEXT:
            if name in calls:
                calls[name](t)
            else:
                chains[t][name]()
        for h in range(2):
            ts(A("PL", HJ * h, HJ * h + HJ), ps(6, HJ * h, HJ * h + HJ), col("IPL"), Op.add)
        for k in range(4):
            (vgather if k % 2 else sgather)(A(XN, 512 * k, 512 * k + 512), A("Xnat"), A("PL", 32 * k, 32 * k + 32))

    for k in (0, 1, 3, 2):
        dma("S" if k == 2 else "Y", T.y[:, 512 * k:512 * k + 512], T.XC[:, 512 * k:512 * k + 512], "dy%d" % k, [A("XC", 512 * k, 512 * k + 512)], [])
    for e in ("V", "S", "T", "G"):
        wait("G", semof[e], cnt[e])
    g.wait_ge(T.sem.lsem, tot[0])
    for s in ("dwt", "dx0", "dx1", "dth", "di0", "di1", "dy0", "dy1", "dy2", "dy3"):
        g.wait_ge(T.sem[s], 16)
